import numpy as np
import ml_dtypes


def mxq(x, axis, fmt="e4m3"):
    dtype, down = {"e4m3": (ml_dtypes.float8_e4m3fn, 7), "e5m2": (ml_dtypes.float8_e5m2, 14)}[fmt]
    v = np.moveaxis(np.asarray(x, np.float32).astype(ml_dtypes.bfloat16).astype(np.float64), axis, -1)
    blocks = v.reshape(v.shape[:-1] + (-1, 32))
    amax = np.abs(blocks).max(-1, keepdims=True)
    byte = np.maximum(np.where(amax > 0, np.frexp(amax)[1] - 1 + 127, 0) - down, 1)
    scale = np.exp2(byte - 127.0)
    codes = (blocks / scale).astype(np.float32).astype(dtype).astype(np.float64)
    return np.moveaxis((codes * scale).reshape(v.shape), -1, axis)


WIDE = False


def mx_kscale(k):
    if not WIDE:
        return np.ones(k)
    levels = np.array([18, -18])
    if k % 512:
        return np.exp2(np.random.permutation(np.resize(levels, k // 32))).repeat(32)
    a = np.empty((k // 512, 16))
    for p in range(k // 512):
        a[p, :8] = np.random.permutation(np.resize(levels, 8))
        for g in range(8):
            far = levels[np.abs(levels - a[p, g]) >= 10]
            a[p, g + 8] = far[np.random.randint(len(far))]
    return np.exp2(a.ravel()).repeat(32)


def f64(x):
    return np.asarray(x).astype(np.float64)


def striped(idx):
    return np.tile(np.asarray(idx).reshape(-1, 16).T, (8, 1)).astype(np.uint16)


def unstriped(offs):
    return offs[:16].T.reshape(-1).astype(np.int64)

def planes(y):
    n, m = y.shape
    v = y.astype(np.float32).astype(ml_dtypes.bfloat16).astype(np.float64).reshape(n // 32, 32, m)
    top = np.abs(v).max(1)
    byte = np.clip(np.where(top > 0, np.frexp(top)[1] - 1 + 127 - 7, 1), 1, 254)
    codes = (v * np.exp2(127.0 - byte)[:, None, :]).reshape(n, m).astype(np.float32).astype(ml_dtypes.float8_e4m3fn).view(np.uint8)
    words = codes.reshape(n // 512, 128, 4, m).transpose(0, 1, 3, 2)
    return np.ascontiguousarray(words), np.ascontiguousarray(byte.astype(np.uint8).reshape(n // 512, 16, m))


B, N, T, D, R = 1, 512, 2048, 512, 512
LR = 0.1
BETA = 0.9


def setup_inputs():
    n = np.random.standard_normal
    idx = np.random.permutation(T)[:B * N]
    s = mx_kscale(D)[:, None]
    z = mx_kscale(R)[:, None]
    x = n((B, D, R))
    return {
        "xT": (x * s).astype(np.float32),
        "wT": (n((D, T)) * (1.00 / np.sqrt(D)) / s).astype(np.float32),
        "y": (2 * np.random.randint(0, 2, (B, R, N)) - 1).astype(np.float32),
        "wt": (np.random.uniform(0.5, 1.5, (B, R, 1)) * 1.0 / np.sqrt(R) * z).astype(np.float32),
        "xm": (x.transpose(0, 2, 1) / z / s[:, 0]).astype(np.float32),
        "mT": (0.3 * n((D, T)) / s).astype(np.float32),
        "offs": striped(idx),
    }


def reference(xT, wT, y, wt, xm, mT, offs):
    idx = unstriped(offs)
    pick = lambda x: x[:, idx].reshape(x.shape[0], B, N).transpose(1, 0, 2)
    w = pick(f64(wT))
    a = mxq(f64(xT), 1, "e4m3").transpose(0, 2, 1) @ mxq(w, 1, "e4m3")
    g = -f64(wt) * f64(y) / (1.0 + np.exp(f64(y) * a))
    dw = mxq(f64(xm), 1, "e4m3").transpose(0, 2, 1) @ mxq(g, 1, "e5m2")
    nm = BETA * pick(f64(mT)) + dw
    nw = w - LR * nm
    tables = []
    for old, new in ((wT, nw), (mT, nm),):
        table = f64(old)
        table[:, idx] = new.transpose(1, 0, 2).reshape(D, B * N)
        tables.append(table)
    return tuple(tables) + planes(tables[0])

@@ -1,0 +1,224 @@
+from contextlib import ExitStack
+
+import concourse.mybir as mybir
+from concourse.masks import make_identity
+
+F32 = mybir.dt.float32
+BF16 = mybir.dt.bfloat16
+I32 = mybir.dt.int32
+U32 = mybir.dt.uint32
+U16 = mybir.dt.uint16
+U8 = mybir.dt.uint8
+E4M3 = mybir.dt.float8_e4m3fn_x4
+E5M2 = mybir.dt.float8_e5m2_x4
+MULT = mybir.AluOpType.mult
+ADD = mybir.AluOpType.add
+COPY = mybir.ActivationFunctionType.Copy
+SIGMOID = mybir.ActivationFunctionType.Sigmoid
+
+P = 128
+LANES = 4
+N, T, D, R = 512, 2048, 512, 512
+LR = 0.1
+BETA = 0.9
+FLOPS = 2 * 2 * D * R * N
+
+BLOCKS = T // P
+CHUNKS = 4
+CHUNK = T // CHUNKS
+
+
+def tile_attend_gsig_pl_mom_kernel(tc, xT, wT, y, wt, xm, mT, offs, out_0, out_1, out_2, out_3):
+    nc = tc.nc
+    with ExitStack() as ctx:
+        sb = ctx.enter_context(tc.tile_pool(name="sb", bufs=1))
+        ps = ctx.enter_context(tc.psum_pool(name="ps", bufs=8))
+
+        def tile(shape, dtype, name, tag=None):
+            return sb.tile(shape, dtype, name=name, tag=tag or name, align_bytes=64)
+
+        def bank(name):
+            return ps.tile([P, 512], F32, name=name, tag="bank")
+
+        def planes(table):
+            return table.rearrange("(p t) c -> p t c", t=LANES)
+
+        w_hbm, m_hbm, o0_hbm, o1_hbm = planes(wT), planes(mT), planes(out_0), planes(out_1)
+
+        offsets = sb.tile([P, N // 16], U16, name="offsets")
+        w_src = [tile([P, T], F32, "w_src%d" % t) for t in range(LANES)]
+        for t in range(LANES):
+            nc.sync.dma_start(w_src[t][:], w_hbm[:, t, :])
+            if t == 0:
+                nc.sync.dma_start(offsets[:], offs)
+        x_hbm = planes(xT[0])
+        x_raw = [tile([P, LANES, R // 2], F32, "x_raw%d" % h) for h in range(2)]
+        for h in range(2):
+            nc.sync.dma_start(x_raw[h][:], x_hbm[:, :, h * (R // 2):(h + 1) * (R // 2)])
+        y_sb = tile([P, LANES, N], F32, "y_sb")
+        wt_sb = tile([P, LANES], F32, "wt_sb")
+        xm_raw = tile([P, LANES, D], F32, "xm_raw")
+        nc.sync.dma_start(wt_sb[:], wt[0].rearrange("(p t) o -> p (t o)", t=LANES))
+        for h in range(2):
+            nc.sync.dma_start(y_sb[:, 2 * h:2 * h + 2, :], planes(y[0])[:, 2 * h:2 * h + 2, :])
+        nc.sync.dma_start(xm_raw[:], planes(xm[0]))
+        m_src = [tile([P, T], F32, "m_src%d" % t) for t in range(LANES)]
+        for t in range(LANES):
+            nc.sync.dma_start(m_src[t][:], m_hbm[:, t, :])
+        w_new = [tile([P, T], F32, "w_new%d" % t) for t in range(LANES)]
+        m_new = [tile([P, T], F32, "m_new%d" % t) for t in range(LANES)]
+        for t in (2, 3):
+            nc.sync.dma_start(w_new[t][:], w_hbm[:, t, :])
+        nc.sync.dma_start(m_new[0][:], m_hbm[:, 0, :])
+
+        warm = tile([P, 1], F32, "warm")
+        nc.gpsimd.memset(warm[:], 0.0)
+        nc.scalar.activation(warm[:], warm[:], SIGMOID)
+        ident = tile([P, P], F32, "ident")
+        make_identity(nc, ident[:])
+
+        w_g = tile([P, LANES, N], F32, "w_g")
+        w_bf = tile([P, N * LANES], BF16, "w_bf")
+        for t in range(LANES):
+            nc.vector.tensor_copy(w_g[:, t, :], w_src[t][:].indirect(offsets[:]))
+            if t % 2 == 1:
+                nc.vector.tensor_copy(
+                    w_bf[:].rearrange("p (c t) -> p c t", t=LANES)[:, :, t - 1:t + 1],
+                    w_g[:, t - 1:t + 1, :].rearrange("p t c -> p c t"),
+                )
+        for t in (0, 1):
+            nc.scalar.activation(w_new[t][:], w_src[t][:], COPY)
+        w_q = tile([P, N], U32, "w_q")
+        w_s = tile([P, N], U8, "w_s")
+        nc.vector.quantize_mx(w_q[:].bitcast(E4M3), w_s[:], w_bf[:])
+
+        x_bf = tile([P, R * LANES], BF16, "x_bf")
+        x_view = x_bf[:].rearrange("p (t m j) -> p m t j", t=LANES, j=LANES)
+        for h in range(2):
+            for k in range(2):
+                nc.scalar.copy(
+                    x_view[:, h * (P // 2):(h + 1) * (P // 2), 2 * k:2 * k + 2, :],
+                    x_raw[h][:].rearrange("p j (m t) -> p m t j", t=LANES)[:, :, 2 * k:2 * k + 2, :],
+                )
+        x_q = tile([P, R], U32, "x_q")
+        x_s = tile([P, R], U8, "x_s")
+        for k in range(2):
+            cols = slice(k * 2 * P, (k + 1) * 2 * P)
+            nc.vector.quantize_mx(x_q[:, cols].bitcast(E4M3), x_s[:, cols], x_bf[:, k * 2 * P * LANES:(k + 1) * 2 * P * LANES])
+
+        sig = tile([P, LANES, N], F32, "sig")
+        yw = tile([P, LANES, N], F32, "yw")
+        for t in range(LANES):
+            cols = slice(t * P, (t + 1) * P)
+            a = bank("a")
+            nc.tensor.matmul_mx(a[:], x_q[:, cols].bitcast(E4M3), x_s[:, cols], w_q[:].bitcast(E4M3), w_s[:], start=True, stop=True)
+            z = tile([P, N], F32, "z%d" % t, tag=["step0", "step1", "step2", "xm_bf"][t])
+            nc.vector.tensor_tensor(z[:], a[:], y_sb[:, t, :], MULT)
+            nc.scalar.activation(sig[:, t, :], z[:], SIGMOID, scale=-1.0)
+        for t in range(LANES):
+            nc.vector.tensor_scalar(yw[:, t, :], y_sb[:, t, :], wt_sb[:, t:t + 1], -1.0, MULT, MULT)
+
+        xm_bf = tile([P, D * LANES], BF16, "xm_bf")
+        xm_view = xm_bf[:].rearrange("p (t m j) -> p m t j", t=LANES, j=LANES)
+        for k in range(2):
+            nc.scalar.copy(
+                xm_view[:, :, 2 * k:2 * k + 2, :],
+                xm_raw[:].rearrange("p j (m t) -> p m t j", t=LANES)[:, :, 2 * k:2 * k + 2, :],
+            )
+        g_bf = tile([P, N * LANES], BF16, "g_bf")
+        nc.vector.tensor_tensor(
+            g_bf[:].rearrange("p (c i t) -> p c t i", i=2, t=LANES),
+            sig[:].rearrange("p t (c i) -> p c t i", i=2),
+            yw[:].rearrange("p t (c i) -> p c t i", i=2),
+            MULT,
+        )
+        xm_q = tile([P, D], U32, "xm_q")
+        xm_s = tile([P, D], U8, "xm_s")
+        g_q = tile([P, N], U32, "g_q")
+        g_s = tile([P, N], U8, "g_s")
+        for k in range(2):
+            cols = slice(k * 2 * P, (k + 1) * 2 * P)
+            nc.vector.quantize_mx(xm_q[:, cols].bitcast(E4M3), xm_s[:, cols], xm_bf[:, k * 2 * P * LANES:(k + 1) * 2 * P * LANES])
+            if k == 0:
+                nc.vector.quantize_mx(g_q[:].bitcast(E5M2), g_s[:], g_bf[:])
+
+        dw_sb = tile([P, LANES - 1, N], F32, "dw_sb", tag="xm_raw")
+        u = tile([P, LANES - 1, N], F32, "u", tag="y_sb")
+        m_first = tile([P, N], F32, "m_first", tag="g_bf")
+        nm_first = tile([P, N], F32, "nm_first")
+        nc.vector.tensor_scalar(m_first[:], m_src[0][:].indirect(offsets[:]), BETA, 0.0, MULT, ADD)
+        step = []
+        for t in range(LANES):
+            cols = slice(t * P, (t + 1) * P)
+            dw = bank("dw")
+            nc.tensor.matmul_mx(dw[:], xm_q[:, cols].bitcast(E4M3), xm_s[:, cols], g_q[:].bitcast(E5M2), g_s[:], start=True, stop=True)
+            if t == 0:
+                nc.vector.tensor_tensor(nm_first[:], dw[:], m_first[:], ADD)
+            else:
+                nc.scalar.activation(dw_sb[:, t - 1, :], dw[:], COPY, scale=1.0 / BETA)
+        for t in range(LANES):
+            step.append(tile([P, N], F32, "step%d" % t))
+            if t == 0:
+                nc.scalar.activation(step[t][:], nm_first[:], COPY, scale=-LR)
+            else:
+                nc.vector.tensor_tensor(u[:, t - 1, :], m_src[t][:].indirect(offsets[:]), dw_sb[:, t - 1, :], ADD)
+                nc.scalar.activation(step[t][:], u[:, t - 1, :], COPY, scale=-LR * BETA)
+        for t in range(1, LANES):
+            nc.scalar.activation(m_new[t][:], m_src[t][:], COPY)
+
+        turned = {}
+
+        def turn_pair(e2, half_tags):
+            for k, tag in enumerate(half_tags):
+                per = BLOCKS // len(half_tags)
+                dst = tile([P, per, 2 * P], BF16, "turned%d_%d" % (e2, k), tag=tag)
+                for b0 in range(0, per, 2):
+                    acc = bank("t1")
+                    view = acc[:].rearrange("p (b e q) -> p b e q", b=2, e=2)
+                    for b in range(2):
+                        blk = k * per + b0 + b
+                        turned[(e2, blk)] = dst[:, b0 + b, :]
+                        for e in range(2):
+                            nc.tensor.transpose(view[:, b, e, :], w_new[2 * e2 + e][:, blk * P:(blk + 1) * P], ident[:])
+                    nc.scalar.copy(
+                        dst[:, b0:b0 + 2, :].rearrange("p b (q e) -> p b q e", e=2),
+                        acc[:].rearrange("p (b e q) -> p b q e", b=2, e=2),
+                    )
+
+        for t in range(LANES):
+            nc.vector.tensor_tensor(w_new[t][:].indirect(offsets[:]), w_g[:, t, :], step[t][:], ADD)
+            nc.sync.dma_start(o0_hbm[:, t, :], w_new[t][:])
+            if t == 1:
+                turn_pair(0, ["w_src0"])
+
+        nm_rest = tile([P, LANES - 1, N], F32, "nm_rest", tag="step3")
+        for t in range(1, LANES):
+            nc.scalar.activation(nm_rest[:, t - 1, :], u[:, t - 1, :], COPY, scale=BETA)
+        turn_pair(1, ["w_src1", "w_src2"])
+        for t in range(LANES):
+            src = nm_first[:] if t == 0 else nm_rest[:, t - 1, :]
+            nc.vector.tensor_copy(m_new[t][:].indirect(offsets[:]), src)
+            nc.sync.dma_start(o1_hbm[:, t, :], m_new[t][:])
+
+        o_s = tile([P, T], U8, "o_s")
+        words_hbm = out_2[0].rearrange("p c l -> p (c l)").bitcast(I32)
+        for c, (tag_in, tag_out) in enumerate(zip(["x_raw0", "x_raw1", "yw", "sig"], ["w_bf", "x_bf", "xm_bf", "g_bf"])):
+            o_bf = tile([P, CHUNK * LANES], BF16, "o_bf%d" % c, tag=tag_in)
+            for b0 in range(0, CHUNK // P, 2):
+                acc = bank("t2")
+                view = acc[:].rearrange("p (b u n) -> p b u n", b=2, u=2)
+                for b in range(2):
+                    blk = c * (CHUNK // P) + b0 + b
+                    for e2 in range(2):
+                        nc.tensor.transpose(view[:, b, e2, :], turned[(e2, blk)].bitcast(F32), ident[:])
+                nc.scalar.copy(
+                    o_bf[:, b0 * P * LANES:(b0 + 2) * P * LANES].bitcast(F32).rearrange("p (b n u) -> p b n u", b=2, u=2),
+                    acc[:].rearrange("p (b u n) -> p b n u", b=2, u=2),
+                )
+            o_q = tile([P, CHUNK], U32, "o_q%d" % c, tag=tag_out)
+            cols = slice(c * CHUNK, (c + 1) * CHUNK)
+            nc.vector.quantize_mx(o_q[:].bitcast(E4M3), o_s[:, cols], o_bf[:])
+            nc.sync.dma_start(words_hbm[:, cols], o_q[:].bitcast(I32))
+        scales_hbm = out_3[0].bitcast(I32)
+        for q in range(4):
+            nc.scalar.dma_start(scales_hbm[4 * q:4 * q + 4, :], o_s[32 * q:32 * q + 4, :].bitcast(I32))

@@ -76,6 +76,8 @@ def tile_attend_gsig_pl_mom_kernel(tc, xT, wT, y, wt, xm, mT, offs, out_0, out_1
         nc.scalar.activation(warm[:], warm[:], SIGMOID)
         ident = tile([P, P], F32, "ident")
         make_identity(nc, ident[:])
+        ones = tile([P, N], F32, "ones")
+        nc.gpsimd.memset(ones[:], 1.0)
 
         w_g = tile([P, LANES, N], F32, "w_g")
         w_bf = tile([P, N * LANES], BF16, "w_bf")
@@ -93,12 +95,12 @@ def tile_attend_gsig_pl_mom_kernel(tc, xT, wT, y, wt, xm, mT, offs, out_0, out_1
         nc.vector.quantize_mx(w_q[:].bitcast(E4M3), w_s[:], w_bf[:])
 
         x_bf = tile([P, R * LANES], BF16, "x_bf")
-        x_view = x_bf[:].rearrange("p (t m j) -> p m t j", t=LANES, j=LANES)
+        x_view = x_bf[:].rearrange("p (t m j) -> p m j t", t=LANES, j=LANES)
         for h in range(2):
             for k in range(2):
                 nc.scalar.copy(
-                    x_view[:, h * (P // 2):(h + 1) * (P // 2), 2 * k:2 * k + 2, :],
-                    x_raw[h][:].rearrange("p j (m t) -> p m t j", t=LANES)[:, :, 2 * k:2 * k + 2, :],
+                    x_view[:, h * (P // 2):(h + 1) * (P // 2), :, 2 * k:2 * k + 2],
+                    x_raw[h][:].rearrange("p j (m t) -> p m j t", t=LANES)[:, :, :, 2 * k:2 * k + 2],
                 )
         x_q = tile([P, R], U32, "x_q")
         x_s = tile([P, R], U8, "x_s")
@@ -107,7 +109,9 @@ def tile_attend_gsig_pl_mom_kernel(tc, xT, wT, y, wt, xm, mT, offs, out_0, out_1
             nc.vector.quantize_mx(x_q[:, cols].bitcast(E4M3), x_s[:, cols], x_bf[:, k * 2 * P * LANES:(k + 1) * 2 * P * LANES])
 
         sig = tile([P, LANES, N], F32, "sig")
-        yw = tile([P, LANES, N], F32, "yw")
+        g_planes = tile([P, LANES, N], BF16, "g_planes")
+        wt_neg = tile([P, LANES], F32, "wt_neg")
+        nc.vector.tensor_scalar(wt_neg[:], wt_sb[:], -1.0, None, MULT)
         for t in range(LANES):
             cols = slice(t * P, (t + 1) * P)
             a = bank("a")
@@ -116,22 +120,18 @@ def tile_attend_gsig_pl_mom_kernel(tc, xT, wT, y, wt, xm, mT, offs, out_0, out_1
             nc.vector.tensor_tensor(z[:], a[:], y_sb[:, t, :], MULT)
             nc.scalar.activation(sig[:, t, :], z[:], SIGMOID, scale=-1.0)
         for t in range(LANES):
-            nc.vector.tensor_scalar(yw[:, t, :], y_sb[:, t, :], wt_sb[:, t:t + 1], -1.0, MULT, MULT)
+            nc.vector.scalar_tensor_tensor(g_planes[:, t, :], sig[:, t, :], wt_neg[:, t:t + 1], y_sb[:, t, :], MULT, MULT)
 
         xm_bf = tile([P, D * LANES], BF16, "xm_bf")
-        xm_view = xm_bf[:].rearrange("p (t m j) -> p m t j", t=LANES, j=LANES)
-        for k in range(2):
-            nc.scalar.copy(
-                xm_view[:, :, 2 * k:2 * k + 2, :],
-                xm_raw[:].rearrange("p j (m t) -> p m t j", t=LANES)[:, :, 2 * k:2 * k + 2, :],
-            )
+        xm_view = xm_bf[:].rearrange("p (t m j) -> p m j t", t=LANES, j=LANES)
+        xm_cols = xm_raw[:].rearrange("p j (m t) -> p m j t", t=LANES)
+        nc.scalar.copy(xm_view[:, :, :, 0:2], xm_cols[:, :, :, 0:2])
         g_bf = tile([P, N * LANES], BF16, "g_bf")
-        nc.vector.tensor_tensor(
-            g_bf[:].rearrange("p (c i t) -> p c t i", i=2, t=LANES),
-            sig[:].rearrange("p t (c i) -> p c t i", i=2),
-            yw[:].rearrange("p t (c i) -> p c t i", i=2),
-            MULT,
-        )
+        woven = g_bf[:].rearrange("p (c i t) -> p c t i", i=4, t=LANES)
+        plain = g_planes[:].rearrange("p t (c i) -> p c t i", i=4)
+        nc.vector.tensor_copy(woven[:, :80], plain[:, :80])
+        nc.scalar.copy(woven[:, 80:], plain[:, 80:])
+        nc.scalar.copy(xm_view[:, :, :, 2:4], xm_cols[:, :, :, 2:4])
         xm_q = tile([P, D], U32, "xm_q")
         xm_s = tile([P, D], U8, "xm_s")
         g_q = tile([P, N], U32, "g_q")
@@ -191,18 +191,19 @@ def tile_attend_gsig_pl_mom_kernel(tc, xT, wT, y, wt, xm, mT, offs, out_0, out_1
             if t == 1:
                 turn_pair(0, ["w_src0"])
 
-        nm_rest = tile([P, LANES - 1, N], F32, "nm_rest", tag="step3")
-        for t in range(1, LANES):
-            nc.scalar.activation(nm_rest[:, t - 1, :], u[:, t - 1, :], COPY, scale=BETA)
+        beta = tile([P, N], F32, "beta", tag="step3")
+        nc.scalar.activation(beta[:], ones[:], COPY, scale=BETA)
         turn_pair(1, ["w_src1", "w_src2"])
         for t in range(LANES):
-            src = nm_first[:] if t == 0 else nm_rest[:, t - 1, :]
-            nc.vector.tensor_copy(m_new[t][:].indirect(offsets[:]), src)
+            if t == 0:
+                nc.vector.tensor_copy(m_new[t][:].indirect(offsets[:]), nm_first[:])
+            else:
+                nc.vector.tensor_tensor(m_new[t][:].indirect(offsets[:]), u[:, t - 1, :], beta[:], MULT)
             nc.sync.dma_start(o1_hbm[:, t, :], m_new[t][:])
 
-        o_s = tile([P, T], U8, "o_s")
+        o_s = tile([P, CHUNK], U8, "o_s")
         words_hbm = out_2[0].rearrange("p c l -> p (c l)").bitcast(I32)
-        for c, (tag_in, tag_out) in enumerate(zip(["x_raw0", "x_raw1", "yw", "sig"], ["w_bf", "x_bf", "xm_bf", "g_bf"])):
+        for c, (tag_in, tag_out) in enumerate(zip(["x_raw0", "x_raw1", "g_planes", "sig"], ["w_bf", "x_bf", "xm_bf", "g_bf"])):
             o_bf = tile([P, CHUNK * LANES], BF16, "o_bf%d" % c, tag=tag_in)
             for b0 in range(0, CHUNK // P, 2):
                 acc = bank("t2")
@@ -217,8 +218,8 @@ def tile_attend_gsig_pl_mom_kernel(tc, xT, wT, y, wt, xm, mT, offs, out_0, out_1
                 )
             o_q = tile([P, CHUNK], U32, "o_q%d" % c, tag=tag_out)
             cols = slice(c * CHUNK, (c + 1) * CHUNK)
-            nc.vector.quantize_mx(o_q[:].bitcast(E4M3), o_s[:, cols], o_bf[:])
+            nc.vector.quantize_mx(o_q[:].bitcast(E4M3), o_s[4 * c:P, :], o_bf[:])
             nc.sync.dma_start(words_hbm[:, cols], o_q[:].bitcast(I32))
-        scales_hbm = out_3[0].bitcast(I32)
+        scales_hbm = out_3[0].bitcast(I32).rearrange("f (c n) -> c f n", c=CHUNKS)
         for q in range(4):
-            nc.scalar.dma_start(scales_hbm[4 * q:4 * q + 4, :], o_s[32 * q:32 * q + 4, :].bitcast(I32))
+            nc.scalar.dma_start(scales_hbm[:, 4 * q:4 * q + 4, :], o_s[32 * q:32 * q + 16, :].bitcast(I32))

@@ -23,6 +23,7 @@ LR = 0.1
 BETA = 0.9
 FLOPS = 2 * 2 * D * R * N
 
+HALF = N // 2
 BLOCKS = T // P
 CHUNKS = 4
 CHUNK = T // CHUNKS
@@ -66,9 +67,10 @@ def tile_attend_gsig_pl_mom_kernel(tc, xT, wT, y, wt, xm, mT, offs, out_0, out_1
         for t in range(LANES):
             nc.sync.dma_start(m_src[t][:], m_hbm[:, t, :])
         w_new = [tile([P, T], F32, "w_new%d" % t) for t in range(LANES)]
-        m_new = [tile([P, T], F32, "m_new%d" % t) for t in range(LANES)]
+        m_new = [tile([P, T], F32, "m_new0")]
+        copied = [T, T, 3 * T // 4, T // 4]
         for t in (2, 3):
-            nc.sync.dma_start(w_new[t][:], w_hbm[:, t, :])
+            nc.sync.dma_start(w_new[t][:, copied[t]:], w_hbm[:, t, copied[t]:])
         nc.sync.dma_start(m_new[0][:], m_hbm[:, 0, :])
 
         warm = tile([P, 1], F32, "warm")
@@ -88,8 +90,8 @@ def tile_attend_gsig_pl_mom_kernel(tc, xT, wT, y, wt, xm, mT, offs, out_0, out_1
                     w_bf[:].rearrange("p (c t) -> p c t", t=LANES)[:, :, t - 1:t + 1],
                     w_g[:, t - 1:t + 1, :].rearrange("p t c -> p c t"),
                 )
-        for t in (0, 1):
-            nc.scalar.activation(w_new[t][:], w_src[t][:], COPY)
+        for t in range(LANES):
+            nc.scalar.activation(w_new[t][:, :copied[t]], w_src[t][:, :copied[t]], COPY)
         w_q = tile([P, N], U32, "w_q")
         w_s = tile([P, N], U8, "w_s")
         nc.vector.quantize_mx(w_q[:].bitcast(E4M3), w_s[:], w_bf[:])
@@ -109,28 +111,37 @@ def tile_attend_gsig_pl_mom_kernel(tc, xT, wT, y, wt, xm, mT, offs, out_0, out_1
             nc.vector.quantize_mx(x_q[:, cols].bitcast(E4M3), x_s[:, cols], x_bf[:, k * 2 * P * LANES:(k + 1) * 2 * P * LANES])
 
         sig = tile([P, LANES, N], F32, "sig")
-        g_planes = tile([P, LANES, N], BF16, "g_planes")
+        yw = tile([P, LANES, N], F32, "yw")
         wt_neg = tile([P, LANES], F32, "wt_neg")
-        nc.vector.tensor_scalar(wt_neg[:], wt_sb[:], -1.0, None, MULT)
-        for t in range(LANES):
-            cols = slice(t * P, (t + 1) * P)
-            a = bank("a")
-            nc.tensor.matmul_mx(a[:], x_q[:, cols].bitcast(E4M3), x_s[:, cols], w_q[:].bitcast(E4M3), w_s[:], start=True, stop=True)
-            z = tile([P, N], F32, "z%d" % t, tag=["step0", "step1", "step2", "xm_bf"][t])
-            nc.vector.tensor_tensor(z[:], a[:], y_sb[:, t, :], MULT)
-            nc.scalar.activation(sig[:, t, :], z[:], SIGMOID, scale=-1.0)
-        for t in range(LANES):
-            nc.vector.scalar_tensor_tensor(g_planes[:, t, :], sig[:, t, :], wt_neg[:, t:t + 1], y_sb[:, t, :], MULT, MULT)
+        nc.gpsimd.tensor_scalar(wt_neg[:], wt_sb[:], -1.0, 0.0, MULT, ADD)
+        for t in range(2):
+            nc.scalar.activation(yw[:, t, :], y_sb[:, t, :], COPY, scale=wt_neg[:, t:t + 1])
+        for t in range(2, LANES):
+            nc.gpsimd.tensor_scalar(yw[:, t, :], y_sb[:, t, :], wt_neg[:, t:t + 1], 0.0, MULT, ADD)
+        for h in range(2):
+            slots = slice(h * HALF, (h + 1) * HALF)
+            for k in range(2):
+                a = bank("a")
+                for e in range(2):
+                    cols = slice((2 * k + e) * P, (2 * k + e + 1) * P)
+                    nc.tensor.matmul_mx(a[:, e * HALF:(e + 1) * HALF], x_q[:, cols].bitcast(E4M3), x_s[:, cols], w_q[:, slots].bitcast(E4M3), w_s[:, slots], start=True, stop=True)
+                z = tile([P, 2, HALF], F32, "z%d%d" % (h, k), tag=["step0", "step1", "step2", "xm_bf"][2 * h + k])
+                nc.vector.tensor_tensor(z[:], a[:].rearrange("p (e n) -> p e n", e=2), y_sb[:, 2 * k:2 * k + 2, slots], MULT)
+                nc.scalar.activation(sig[:, 2 * k:2 * k + 2, slots], z[:], SIGMOID, scale=-1.0)
 
         xm_bf = tile([P, D * LANES], BF16, "xm_bf")
         xm_view = xm_bf[:].rearrange("p (t m j) -> p m j t", t=LANES, j=LANES)
         xm_cols = xm_raw[:].rearrange("p j (m t) -> p m j t", t=LANES)
         nc.scalar.copy(xm_view[:, :, :, 0:2], xm_cols[:, :, :, 0:2])
         g_bf = tile([P, N * LANES], BF16, "g_bf")
-        woven = g_bf[:].rearrange("p (c i t) -> p c t i", i=4, t=LANES)
-        plain = g_planes[:].rearrange("p t (c i) -> p c t i", i=4)
-        nc.vector.tensor_copy(woven[:, :80], plain[:, :80])
-        nc.scalar.copy(woven[:, 80:], plain[:, 80:])
+        for h in range(2):
+            slots = slice(h * HALF, (h + 1) * HALF)
+            nc.vector.tensor_tensor(
+                g_bf[:, h * HALF * LANES:(h + 1) * HALF * LANES].rearrange("p (c i t) -> p c t i", i=2, t=LANES),
+                sig[:, :, slots].rearrange("p t (c i) -> p c t i", i=2),
+                yw[:, :, slots].rearrange("p t (c i) -> p c t i", i=2),
+                MULT,
+            )
         nc.scalar.copy(xm_view[:, :, :, 2:4], xm_cols[:, :, :, 2:4])
         xm_q = tile([P, D], U32, "xm_q")
         xm_s = tile([P, D], U8, "xm_s")
@@ -146,24 +157,22 @@ def tile_attend_gsig_pl_mom_kernel(tc, xT, wT, y, wt, xm, mT, offs, out_0, out_1
         u = tile([P, LANES - 1, N], F32, "u", tag="y_sb")
         m_first = tile([P, N], F32, "m_first", tag="g_bf")
         nm_first = tile([P, N], F32, "nm_first")
-        nc.vector.tensor_scalar(m_first[:], m_src[0][:].indirect(offsets[:]), BETA, 0.0, MULT, ADD)
+        nc.vector.tensor_copy(m_first[:], m_src[0][:].indirect(offsets[:]))
         step = []
         for t in range(LANES):
             cols = slice(t * P, (t + 1) * P)
             dw = bank("dw")
             nc.tensor.matmul_mx(dw[:], xm_q[:, cols].bitcast(E4M3), xm_s[:, cols], g_q[:].bitcast(E5M2), g_s[:], start=True, stop=True)
-            if t == 0:
-                nc.vector.tensor_tensor(nm_first[:], dw[:], m_first[:], ADD)
-            else:
-                nc.scalar.activation(dw_sb[:, t - 1, :], dw[:], COPY, scale=1.0 / BETA)
-        for t in range(LANES):
             step.append(tile([P, N], F32, "step%d" % t))
             if t == 0:
+                nc.vector.scalar_tensor_tensor(nm_first[:], m_first[:], BETA, dw[:], MULT, ADD)
                 nc.scalar.activation(step[t][:], nm_first[:], COPY, scale=-LR)
             else:
+                nc.scalar.activation(dw_sb[:, t - 1, :], dw[:], COPY, scale=1.0 / BETA)
                 nc.vector.tensor_tensor(u[:, t - 1, :], m_src[t][:].indirect(offsets[:]), dw_sb[:, t - 1, :], ADD)
                 nc.scalar.activation(step[t][:], u[:, t - 1, :], COPY, scale=-LR * BETA)
         for t in range(1, LANES):
+            m_new.append(tile([P, T], F32, "m_new%d" % t, tag="g_bf" if t == 1 else None))
             nc.scalar.activation(m_new[t][:], m_src[t][:], COPY)
 
         turned = {}
@@ -203,7 +212,7 @@ def tile_attend_gsig_pl_mom_kernel(tc, xT, wT, y, wt, xm, mT, offs, out_0, out_1
 
         o_s = tile([P, CHUNK], U8, "o_s")
         words_hbm = out_2[0].rearrange("p c l -> p (c l)").bitcast(I32)
-        for c, (tag_in, tag_out) in enumerate(zip(["x_raw0", "x_raw1", "g_planes", "sig"], ["w_bf", "x_bf", "xm_bf", "g_bf"])):
+        for c, (tag_in, tag_out) in enumerate(zip(["x_raw0", "x_raw1", "yw", "sig"], ["w_bf", "x_bf", "xm_bf", "g_bf"])):
             o_bf = tile([P, CHUNK * LANES], BF16, "o_bf%d" % c, tag=tag_in)
             for b0 in range(0, CHUNK // P, 2):
                 acc = bank("t2")

@@ -27,6 +27,7 @@ HALF = N // 2
 BLOCKS = T // P
 CHUNKS = 4
 CHUNK = T // CHUNKS
+COPIED = 7 * T // 8
 
 
 def tile_attend_gsig_pl_mom_kernel(tc, xT, wT, y, wt, xm, mT, offs, out_0, out_1, out_2, out_3):
@@ -47,115 +48,120 @@ def tile_attend_gsig_pl_mom_kernel(tc, xT, wT, y, wt, xm, mT, offs, out_0, out_1
         w_hbm, m_hbm, o0_hbm, o1_hbm = planes(wT), planes(mT), planes(out_0), planes(out_1)
 
         offsets = sb.tile([P, N // 16], U16, name="offsets")
+        wt_sb = tile([P, LANES], F32, "wt_sb")
         w_src = [tile([P, T], F32, "w_src%d" % t) for t in range(LANES)]
         for t in range(LANES):
             nc.sync.dma_start(w_src[t][:], w_hbm[:, t, :])
             if t == 0:
                 nc.sync.dma_start(offsets[:], offs)
+                nc.sync.dma_start(wt_sb[:], wt[0].rearrange("(p t) o -> p (t o)", t=LANES))
         x_hbm = planes(xT[0])
         x_raw = [tile([P, LANES, R // 2], F32, "x_raw%d" % h) for h in range(2)]
         for h in range(2):
             nc.sync.dma_start(x_raw[h][:], x_hbm[:, :, h * (R // 2):(h + 1) * (R // 2)])
-        y_sb = tile([P, LANES, N], F32, "y_sb")
-        wt_sb = tile([P, LANES], F32, "wt_sb")
+        y_sb = [tile([P, 2, N], F32, "y_sb%d" % k) for k in range(2)]
         xm_raw = tile([P, LANES, D], F32, "xm_raw")
-        nc.sync.dma_start(wt_sb[:], wt[0].rearrange("(p t) o -> p (t o)", t=LANES))
         for h in range(2):
-            nc.sync.dma_start(y_sb[:, 2 * h:2 * h + 2, :], planes(y[0])[:, 2 * h:2 * h + 2, :])
+            nc.sync.dma_start(y_sb[h][:], planes(y[0])[:, 2 * h:2 * h + 2, :])
         nc.sync.dma_start(xm_raw[:], planes(xm[0]))
         m_src = [tile([P, T], F32, "m_src%d" % t) for t in range(LANES)]
+        w_new = [tile([P, T], F32, "w_new%d" % t) for t in range(LANES)]
         for t in range(LANES):
             nc.sync.dma_start(m_src[t][:], m_hbm[:, t, :])
-        w_new = [tile([P, T], F32, "w_new%d" % t) for t in range(LANES)]
-        m_new = [tile([P, T], F32, "m_new0")]
-        copied = [T, T, 3 * T // 4, T // 4]
-        for t in (2, 3):
-            nc.sync.dma_start(w_new[t][:, copied[t]:], w_hbm[:, t, copied[t]:])
-        nc.sync.dma_start(m_new[0][:], m_hbm[:, 0, :])
+            if t > 0:
+                nc.sync.dma_start(w_new[t - 1][:, COPIED:], w_hbm[:, t - 1, COPIED:])
+        nc.sync.dma_start(w_new[3][:], w_hbm[:, 3, :])
+        m_new = {3: tile([P, T], F32, "m_new3")}
+        nc.sync.dma_start(m_new[3][:], m_hbm[:, 3, :])
 
         warm = tile([P, 1], F32, "warm")
         nc.gpsimd.memset(warm[:], 0.0)
         nc.scalar.activation(warm[:], warm[:], SIGMOID)
         ident = tile([P, P], F32, "ident")
         make_identity(nc, ident[:])
-        ones = tile([P, N], F32, "ones")
-        nc.gpsimd.memset(ones[:], 1.0)
+        beta = tile([P, N], F32, "beta")
+        nc.gpsimd.memset(beta[:], 1.0)
+        nc.gpsimd.tensor_scalar(beta[:], beta[:], BETA, 0.0, MULT, ADD)
 
         w_g = tile([P, LANES, N], F32, "w_g")
-        w_bf = tile([P, N * LANES], BF16, "w_bf")
-        for t in range(LANES):
+        w_bf = [tile([P, HALF * LANES], BF16, "w_bf%d" % h) for h in range(2)]
+        w_view = [w_bf[h][:].rearrange("p (c i t) -> p c t i", i=4, t=LANES) for h in range(2)]
+        for t in range(LANES - 1):
             nc.vector.tensor_copy(w_g[:, t, :], w_src[t][:].indirect(offsets[:]))
-            if t % 2 == 1:
-                nc.vector.tensor_copy(
-                    w_bf[:].rearrange("p (c t) -> p c t", t=LANES)[:, :, t - 1:t + 1],
-                    w_g[:, t - 1:t + 1, :].rearrange("p t c -> p c t"),
-                )
-        for t in range(LANES):
-            nc.scalar.activation(w_new[t][:, :copied[t]], w_src[t][:, :copied[t]], COPY)
+            if t == 1:
+                for h in range(2):
+                    nc.vector.tensor_copy(w_view[h][:, :, 0:2, :], w_g[:, 0:2, h * HALF:(h + 1) * HALF].rearrange("p t (c i) -> p c t i", i=4))
+        for h in range(2):
+            nc.vector.tensor_copy(w_g[:, 3, h * HALF:(h + 1) * HALF], w_src[3][:].indirect(offsets[:, h * (HALF // 16):(h + 1) * (HALF // 16)]))
+        for h in range(2):
+            slots = slice(h * HALF, (h + 1) * HALF)
+            nc.vector.tensor_copy(w_view[h][:, :, 2:4, :], w_g[:, 2:4, slots].rearrange("p t (c i) -> p c t i", i=4))
+        for t in range(LANES - 1):
+            nc.scalar.activation(w_new[t][:, :COPIED], w_src[t][:, :COPIED], COPY)
         w_q = tile([P, N], U32, "w_q")
         w_s = tile([P, N], U8, "w_s")
-        nc.vector.quantize_mx(w_q[:].bitcast(E4M3), w_s[:], w_bf[:])
+        for h in range(2):
+            slots = slice(h * HALF, (h + 1) * HALF)
+            nc.vector.quantize_mx(w_q[:, slots].bitcast(E4M3), w_s[:, slots], w_bf[h][:])
 
-        x_bf = tile([P, R * LANES], BF16, "x_bf")
-        x_view = x_bf[:].rearrange("p (t m j) -> p m j t", t=LANES, j=LANES)
+        x_bf = [tile([P, R * 2], BF16, "x_bf%d" % k) for k in range(2)]
         for h in range(2):
             for k in range(2):
                 nc.scalar.copy(
-                    x_view[:, h * (P // 2):(h + 1) * (P // 2), :, 2 * k:2 * k + 2],
+                    x_bf[k][:].rearrange("p (t m j) -> p m j t", t=2, j=LANES)[:, h * (P // 2):(h + 1) * (P // 2), :, :],
                     x_raw[h][:].rearrange("p j (m t) -> p m j t", t=LANES)[:, :, :, 2 * k:2 * k + 2],
                 )
         x_q = tile([P, R], U32, "x_q")
         x_s = tile([P, R], U8, "x_s")
         for k in range(2):
             cols = slice(k * 2 * P, (k + 1) * 2 * P)
-            nc.vector.quantize_mx(x_q[:, cols].bitcast(E4M3), x_s[:, cols], x_bf[:, k * 2 * P * LANES:(k + 1) * 2 * P * LANES])
+            nc.vector.quantize_mx(x_q[:, cols].bitcast(E4M3), x_s[:, cols], x_bf[k][:])
 
-        sig = tile([P, LANES, N], F32, "sig")
+        sig = [tile([P, LANES, HALF], F32, "sig%d" % h) for h in range(2)]
         yw = tile([P, LANES, N], F32, "yw")
         wt_neg = tile([P, LANES], F32, "wt_neg")
         nc.gpsimd.tensor_scalar(wt_neg[:], wt_sb[:], -1.0, 0.0, MULT, ADD)
         for t in range(2):
-            nc.scalar.activation(yw[:, t, :], y_sb[:, t, :], COPY, scale=wt_neg[:, t:t + 1])
+            nc.scalar.activation(yw[:, t, :], y_sb[0][:, t, :], COPY, scale=wt_neg[:, t:t + 1])
         for t in range(2, LANES):
-            nc.gpsimd.tensor_scalar(yw[:, t, :], y_sb[:, t, :], wt_neg[:, t:t + 1], 0.0, MULT, ADD)
-        for h in range(2):
-            slots = slice(h * HALF, (h + 1) * HALF)
-            for k in range(2):
+            nc.gpsimd.tensor_scalar(yw[:, t, :], y_sb[1][:, t - 2, :], wt_neg[:, t:t + 1], 0.0, MULT, ADD)
+        for k in range(2):
+            for h in range(2):
+                slots = slice(h * HALF, (h + 1) * HALF)
                 a = bank("a")
                 for e in range(2):
                     cols = slice((2 * k + e) * P, (2 * k + e + 1) * P)
                     nc.tensor.matmul_mx(a[:, e * HALF:(e + 1) * HALF], x_q[:, cols].bitcast(E4M3), x_s[:, cols], w_q[:, slots].bitcast(E4M3), w_s[:, slots], start=True, stop=True)
-                z = tile([P, 2, HALF], F32, "z%d%d" % (h, k), tag=["step0", "step1", "step2", "xm_bf"][2 * h + k])
-                nc.vector.tensor_tensor(z[:], a[:].rearrange("p (e n) -> p e n", e=2), y_sb[:, 2 * k:2 * k + 2, slots], MULT)
-                nc.scalar.activation(sig[:, 2 * k:2 * k + 2, slots], z[:], SIGMOID, scale=-1.0)
+                z = tile([P, 2, HALF], F32, "z%d%d" % (h, k), tag=["step0", "step1", "step2", "xm_bf0"][2 * k + h])
+                nc.vector.tensor_tensor(z[:], a[:].rearrange("p (e n) -> p e n", e=2), y_sb[k][:, :, slots], MULT)
+                nc.scalar.activation(sig[h][:, 2 * k:2 * k + 2, :], z[:], SIGMOID, scale=-1.0)
 
-        xm_bf = tile([P, D * LANES], BF16, "xm_bf")
-        xm_view = xm_bf[:].rearrange("p (t m j) -> p m j t", t=LANES, j=LANES)
         xm_cols = xm_raw[:].rearrange("p j (m t) -> p m j t", t=LANES)
-        nc.scalar.copy(xm_view[:, :, :, 0:2], xm_cols[:, :, :, 0:2])
-        g_bf = tile([P, N * LANES], BF16, "g_bf")
+        xm_bf = [tile([P, D * 2], BF16, "xm_bf0")]
+        nc.scalar.copy(xm_bf[0][:].rearrange("p (t m j) -> p m j t", t=2, j=LANES), xm_cols[:, :, :, 0:2])
+        g_bf = tile([P, N * LANES], BF16, "g_bf", tag="y_sb1")
         for h in range(2):
             slots = slice(h * HALF, (h + 1) * HALF)
             nc.vector.tensor_tensor(
-                g_bf[:, h * HALF * LANES:(h + 1) * HALF * LANES].rearrange("p (c i t) -> p c t i", i=2, t=LANES),
-                sig[:, :, slots].rearrange("p t (c i) -> p c t i", i=2),
-                yw[:, :, slots].rearrange("p t (c i) -> p c t i", i=2),
+                g_bf[:, h * HALF * LANES:(h + 1) * HALF * LANES].rearrange("p (c i t) -> p c t i", i=4, t=LANES),
+                sig[h][:].rearrange("p t (c i) -> p c t i", i=4),
+                yw[:, :, slots].rearrange("p t (c i) -> p c t i", i=4),
                 MULT,
             )
-        nc.scalar.copy(xm_view[:, :, :, 2:4], xm_cols[:, :, :, 2:4])
+        xm_bf.append(tile([P, D * 2], BF16, "xm_bf1", tag="sig0"))
+        nc.scalar.copy(xm_bf[1][:].rearrange("p (t m j) -> p m j t", t=2, j=LANES), xm_cols[:, :, :, 2:4])
         xm_q = tile([P, D], U32, "xm_q")
         xm_s = tile([P, D], U8, "xm_s")
         g_q = tile([P, N], U32, "g_q")
         g_s = tile([P, N], U8, "g_s")
         for k in range(2):
             cols = slice(k * 2 * P, (k + 1) * 2 * P)
-            nc.vector.quantize_mx(xm_q[:, cols].bitcast(E4M3), xm_s[:, cols], xm_bf[:, k * 2 * P * LANES:(k + 1) * 2 * P * LANES])
+            nc.vector.quantize_mx(xm_q[:, cols].bitcast(E4M3), xm_s[:, cols], xm_bf[k][:])
             if k == 0:
                 nc.vector.quantize_mx(g_q[:].bitcast(E5M2), g_s[:], g_bf[:])
 
-        dw_sb = tile([P, LANES - 1, N], F32, "dw_sb", tag="xm_raw")
-        u = tile([P, LANES - 1, N], F32, "u", tag="y_sb")
-        m_first = tile([P, N], F32, "m_first", tag="g_bf")
+        u = tile([P, LANES - 1, N], F32, "u")
+        m_first = tile([P, N], F32, "m_first", tag="y_sb1")
         nm_first = tile([P, N], F32, "nm_first")
         nc.vector.tensor_copy(m_first[:], m_src[0][:].indirect(offsets[:]))
         step = []
@@ -168,42 +174,42 @@ def tile_attend_gsig_pl_mom_kernel(tc, xT, wT, y, wt, xm, mT, offs, out_0, out_1
                 nc.vector.scalar_tensor_tensor(nm_first[:], m_first[:], BETA, dw[:], MULT, ADD)
                 nc.scalar.activation(step[t][:], nm_first[:], COPY, scale=-LR)
             else:
-                nc.scalar.activation(dw_sb[:, t - 1, :], dw[:], COPY, scale=1.0 / BETA)
-                nc.vector.tensor_tensor(u[:, t - 1, :], m_src[t][:].indirect(offsets[:]), dw_sb[:, t - 1, :], ADD)
+                dw_sb = tile([P, N], F32, "dw_sb%d" % t, tag=["m_new0", "m_new1", "xm_raw"][t - 1])
+                nc.scalar.activation(dw_sb[:], dw[:], COPY, scale=1.0 / BETA)
+                nc.vector.tensor_tensor(u[:, t - 1, :], m_src[t][:].indirect(offsets[:]), dw_sb[:], ADD)
                 nc.scalar.activation(step[t][:], u[:, t - 1, :], COPY, scale=-LR * BETA)
-        for t in range(1, LANES):
-            m_new.append(tile([P, T], F32, "m_new%d" % t, tag="g_bf" if t == 1 else None))
-            nc.scalar.activation(m_new[t][:], m_src[t][:], COPY)
+        for t in range(2):
+            m_new[t] = tile([P, T], F32, "m_new%d" % t)
+            nc.scalar.activation(m_new[t][:, :COPIED], m_src[t][:, :COPIED], COPY)
+            nc.sync.dma_start(m_new[t][:, COPIED:], m_hbm[:, t, COPIED:])
+        m_new[2] = tile([P, T], F32, "m_new2")
+        nc.sync.dma_start(m_new[2][:], m_hbm[:, 2, :])
 
-        turned = {}
+        PER = CHUNK // P
 
-        def turn_pair(e2, half_tags):
-            for k, tag in enumerate(half_tags):
-                per = BLOCKS // len(half_tags)
-                dst = tile([P, per, 2 * P], BF16, "turned%d_%d" % (e2, k), tag=tag)
-                for b0 in range(0, per, 2):
-                    acc = bank("t1")
-                    view = acc[:].rearrange("p (b e q) -> p b e q", b=2, e=2)
-                    for b in range(2):
-                        blk = k * per + b0 + b
-                        turned[(e2, blk)] = dst[:, b0 + b, :]
-                        for e in range(2):
-                            nc.tensor.transpose(view[:, b, e, :], w_new[2 * e2 + e][:, blk * P:(blk + 1) * P], ident[:])
-                    nc.scalar.copy(
-                        dst[:, b0:b0 + 2, :].rearrange("p b (q e) -> p b q e", e=2),
-                        acc[:].rearrange("p (b e q) -> p b q e", b=2, e=2),
-                    )
+        def turn(e2, c, tag):
+            dst = tile([P, PER, 2 * P], BF16, "turned%d_%d" % (e2, c), tag=tag)
+            for b0 in range(0, PER, 2):
+                acc = bank("t1")
+                view = acc[:].rearrange("p (b e q) -> p b e q", b=2, e=2)
+                for b in range(2):
+                    blk = c * PER + b0 + b
+                    for e in range(2):
+                        nc.tensor.transpose(view[:, b, e, :], w_new[2 * e2 + e][:, blk * P:(blk + 1) * P], ident[:])
+                nc.scalar.copy(
+                    dst[:, b0:b0 + 2, :].rearrange("p b (q e) -> p b q e", e=2),
+                    acc[:].rearrange("p (b e q) -> p b q e", b=2, e=2),
+                )
+            return dst
 
+        first = []
         for t in range(LANES):
             nc.vector.tensor_tensor(w_new[t][:].indirect(offsets[:]), w_g[:, t, :], step[t][:], ADD)
             nc.sync.dma_start(o0_hbm[:, t, :], w_new[t][:])
             if t == 1:
-                turn_pair(0, ["w_src0"])
+                first = [turn(0, c, "first%d" % c) for c in range(CHUNKS)]
 
-        beta = tile([P, N], F32, "beta", tag="step3")
-        nc.scalar.activation(beta[:], ones[:], COPY, scale=BETA)
-        turn_pair(1, ["w_src1", "w_src2"])
-        for t in range(LANES):
+        for t in range(LANES - 1):
             if t == 0:
                 nc.vector.tensor_copy(m_new[t][:].indirect(offsets[:]), nm_first[:])
             else:
@@ -212,15 +218,15 @@ def tile_attend_gsig_pl_mom_kernel(tc, xT, wT, y, wt, xm, mT, offs, out_0, out_1
 
         o_s = tile([P, CHUNK], U8, "o_s")
         words_hbm = out_2[0].rearrange("p c l -> p (c l)").bitcast(I32)
-        for c, (tag_in, tag_out) in enumerate(zip(["x_raw0", "x_raw1", "yw", "sig"], ["w_bf", "x_bf", "xm_bf", "g_bf"])):
+        for c, (tag_in, tag_out) in enumerate(zip(["x_raw0", "x_raw1", "y_sb0", "y_sb1"], ["w_bf0", "w_bf1", "x_bf0", "x_bf1"])):
+            pair = [first[c], turn(1, c, "second%d" % c)]
             o_bf = tile([P, CHUNK * LANES], BF16, "o_bf%d" % c, tag=tag_in)
-            for b0 in range(0, CHUNK // P, 2):
+            for b0 in range(0, PER, 2):
                 acc = bank("t2")
                 view = acc[:].rearrange("p (b u n) -> p b u n", b=2, u=2)
                 for b in range(2):
-                    blk = c * (CHUNK // P) + b0 + b
                     for e2 in range(2):
-                        nc.tensor.transpose(view[:, b, e2, :], turned[(e2, blk)].bitcast(F32), ident[:])
+                        nc.tensor.transpose(view[:, b, e2, :], pair[e2][:, b0 + b, :].bitcast(F32), ident[:])
                 nc.scalar.copy(
                     o_bf[:, b0 * P * LANES:(b0 + 2) * P * LANES].bitcast(F32).rearrange("p (b n u) -> p b n u", b=2, u=2),
                     acc[:].rearrange("p (b u n) -> p b n u", b=2, u=2),
@@ -232,3 +238,7 @@ def tile_attend_gsig_pl_mom_kernel(tc, xT, wT, y, wt, xm, mT, offs, out_0, out_1
         scales_hbm = out_3[0].bitcast(I32).rearrange("f (c n) -> c f n", c=CHUNKS)
         for q in range(4):
             nc.scalar.dma_start(scales_hbm[:, 4 * q:4 * q + 4, :], o_s[32 * q:32 * q + 16, :].bitcast(I32))
+        nm_last = tile([P, N], F32, "nm_last", tag="second%d" % (CHUNKS - 1))
+        nc.scalar.activation(nm_last[:], u[:, LANES - 2, :], COPY, scale=BETA)
+        nc.vector.tensor_copy(m_new[3][:].indirect(offsets[:]), nm_last[:])
+        nc.sync.dma_start(o1_hbm[:, 3, :], m_new[3][:])

@@ -85,17 +85,17 @@ def tile_attend_gsig_pl_mom_kernel(tc, xT, wT, y, wt, xm, mT, offs, out_0, out_1
 
         w_g = tile([P, LANES, N], F32, "w_g")
         w_bf = [tile([P, HALF * LANES], BF16, "w_bf%d" % h) for h in range(2)]
-        w_view = [w_bf[h][:].rearrange("p (c i t) -> p c t i", i=4, t=LANES) for h in range(2)]
+        w_view = [w_bf[h][:].rearrange("p (c t) -> p c t", t=LANES) for h in range(2)]
         for t in range(LANES - 1):
             nc.vector.tensor_copy(w_g[:, t, :], w_src[t][:].indirect(offsets[:]))
             if t == 1:
                 for h in range(2):
-                    nc.vector.tensor_copy(w_view[h][:, :, 0:2, :], w_g[:, 0:2, h * HALF:(h + 1) * HALF].rearrange("p t (c i) -> p c t i", i=4))
+                    nc.vector.tensor_copy(w_view[h][:, :, 0:2], w_g[:, 0:2, h * HALF:(h + 1) * HALF].rearrange("p t c -> p c t"))
         for h in range(2):
             nc.vector.tensor_copy(w_g[:, 3, h * HALF:(h + 1) * HALF], w_src[3][:].indirect(offsets[:, h * (HALF // 16):(h + 1) * (HALF // 16)]))
         for h in range(2):
             slots = slice(h * HALF, (h + 1) * HALF)
-            nc.vector.tensor_copy(w_view[h][:, :, 2:4, :], w_g[:, 2:4, slots].rearrange("p t (c i) -> p c t i", i=4))
+            nc.vector.tensor_copy(w_view[h][:, :, 2:4], w_g[:, 2:4, slots].rearrange("p t c -> p c t"))
         for t in range(LANES - 1):
             nc.scalar.activation(w_new[t][:, :COPIED], w_src[t][:, :COPIED], COPY)
         w_q = tile([P, N], U32, "w_q")
@@ -218,7 +218,8 @@ def tile_attend_gsig_pl_mom_kernel(tc, xT, wT, y, wt, xm, mT, offs, out_0, out_1
 
         o_s = tile([P, CHUNK], U8, "o_s")
         words_hbm = out_2[0].rearrange("p c l -> p (c l)").bitcast(I32)
-        for c, (tag_in, tag_out) in enumerate(zip(["x_raw0", "x_raw1", "y_sb0", "y_sb1"], ["w_bf0", "w_bf1", "x_bf0", "x_bf1"])):
+        o_q = tile([P, T], U32, "o_q", tag="yw")
+        for c, tag_in in enumerate(["x_raw0", "x_raw1", "y_sb0", "y_sb1"]):
             pair = [first[c], turn(1, c, "second%d" % c)]
             o_bf = tile([P, CHUNK * LANES], BF16, "o_bf%d" % c, tag=tag_in)
             for b0 in range(0, PER, 2):
@@ -231,13 +232,14 @@ def tile_attend_gsig_pl_mom_kernel(tc, xT, wT, y, wt, xm, mT, offs, out_0, out_1
                     o_bf[:, b0 * P * LANES:(b0 + 2) * P * LANES].bitcast(F32).rearrange("p (b n u) -> p b n u", b=2, u=2),
                     acc[:].rearrange("p (b u n) -> p b n u", b=2, u=2),
                 )
-            o_q = tile([P, CHUNK], U32, "o_q%d" % c, tag=tag_out)
             cols = slice(c * CHUNK, (c + 1) * CHUNK)
-            nc.vector.quantize_mx(o_q[:].bitcast(E4M3), o_s[4 * c:P, :], o_bf[:])
-            nc.sync.dma_start(words_hbm[:, cols], o_q[:].bitcast(I32))
+            nc.vector.quantize_mx(o_q[:, cols].bitcast(E4M3), o_s[4 * c:P, :], o_bf[:])
+            if c % 2 == 1:
+                both = slice((c - 1) * CHUNK, (c + 1) * CHUNK)
+                nc.sync.dma_start(words_hbm[:, both], o_q[:, both].bitcast(I32))
         scales_hbm = out_3[0].bitcast(I32).rearrange("f (c n) -> c f n", c=CHUNKS)
         for q in range(4):
-            nc.scalar.dma_start(scales_hbm[:, 4 * q:4 * q + 4, :], o_s[32 * q:32 * q + 16, :].bitcast(I32))
+            nc.sync.dma_start(scales_hbm[:, 4 * q:4 * q + 4, :], o_s[32 * q:32 * q + 16, :].bitcast(I32))
         nm_last = tile([P, N], F32, "nm_last", tag="second%d" % (CHUNKS - 1))
         nc.scalar.activation(nm_last[:], u[:, LANES - 2, :], COPY, scale=BETA)
         nc.vector.tensor_copy(m_new[3][:].indirect(offsets[:]), nm_last[:])

@@ -72,7 +72,7 @@ def tile_attend_gsig_pl_mom_kernel(tc, xT, wT, y, wt, xm, mT, offs, out_0, out_1
                 nc.sync.dma_start(w_new[t - 1][:, COPIED:], w_hbm[:, t - 1, COPIED:])
         nc.sync.dma_start(w_new[3][:], w_hbm[:, 3, :])
         m_new = {3: tile([P, T], F32, "m_new3")}
-        nc.sync.dma_start(m_new[3][:], m_hbm[:, 3, :])
+        nc.sync.dma_start(m_new[3][:, :COPIED], m_hbm[:, 3, :COPIED])
 
         warm = tile([P, 1], F32, "warm")
         nc.gpsimd.memset(warm[:], 0.0)
@@ -139,7 +139,7 @@ def tile_attend_gsig_pl_mom_kernel(tc, xT, wT, y, wt, xm, mT, offs, out_0, out_1
         xm_cols = xm_raw[:].rearrange("p j (m t) -> p m j t", t=LANES)
         xm_bf = [tile([P, D * 2], BF16, "xm_bf0")]
         nc.scalar.copy(xm_bf[0][:].rearrange("p (t m j) -> p m j t", t=2, j=LANES), xm_cols[:, :, :, 0:2])
-        g_bf = tile([P, N * LANES], BF16, "g_bf", tag="y_sb1")
+        g_bf = tile([P, N * LANES], BF16, "g_bf")
         for h in range(2):
             slots = slice(h * HALF, (h + 1) * HALF)
             nc.vector.tensor_tensor(
@@ -154,16 +154,15 @@ def tile_attend_gsig_pl_mom_kernel(tc, xT, wT, y, wt, xm, mT, offs, out_0, out_1
         xm_s = tile([P, D], U8, "xm_s")
         g_q = tile([P, N], U32, "g_q")
         g_s = tile([P, N], U8, "g_s")
+        m_first = tile([P, N], F32, "m_first", tag="x_bf0")
         for k in range(2):
             cols = slice(k * 2 * P, (k + 1) * 2 * P)
             nc.vector.quantize_mx(xm_q[:, cols].bitcast(E4M3), xm_s[:, cols], xm_bf[k][:])
             if k == 0:
                 nc.vector.quantize_mx(g_q[:].bitcast(E5M2), g_s[:], g_bf[:])
+                nc.vector.tensor_copy(m_first[:], m_src[0][:].indirect(offsets[:]))
 
-        u = tile([P, LANES - 1, N], F32, "u")
-        m_first = tile([P, N], F32, "m_first", tag="y_sb1")
-        nm_first = tile([P, N], F32, "nm_first")
-        nc.vector.tensor_copy(m_first[:], m_src[0][:].indirect(offsets[:]))
+        u = tile([P, LANES, N], F32, "u")
         step = []
         for t in range(LANES):
             cols = slice(t * P, (t + 1) * P)
@@ -171,19 +170,19 @@ def tile_attend_gsig_pl_mom_kernel(tc, xT, wT, y, wt, xm, mT, offs, out_0, out_1
             nc.tensor.matmul_mx(dw[:], xm_q[:, cols].bitcast(E4M3), xm_s[:, cols], g_q[:].bitcast(E5M2), g_s[:], start=True, stop=True)
             step.append(tile([P, N], F32, "step%d" % t))
             if t == 0:
-                nc.vector.scalar_tensor_tensor(nm_first[:], m_first[:], BETA, dw[:], MULT, ADD)
-                nc.scalar.activation(step[t][:], nm_first[:], COPY, scale=-LR)
+                nc.vector.scalar_tensor_tensor(u[:, t, :], dw[:], 1.0 / BETA, m_first[:], MULT, ADD)
             else:
                 dw_sb = tile([P, N], F32, "dw_sb%d" % t, tag=["m_new0", "m_new1", "xm_raw"][t - 1])
                 nc.scalar.activation(dw_sb[:], dw[:], COPY, scale=1.0 / BETA)
-                nc.vector.tensor_tensor(u[:, t - 1, :], m_src[t][:].indirect(offsets[:]), dw_sb[:], ADD)
-                nc.scalar.activation(step[t][:], u[:, t - 1, :], COPY, scale=-LR * BETA)
+                nc.vector.tensor_tensor(u[:, t, :], m_src[t][:].indirect(offsets[:]), dw_sb[:], ADD)
+            nc.scalar.activation(step[t][:], u[:, t, :], COPY, scale=-LR * BETA)
         for t in range(2):
             m_new[t] = tile([P, T], F32, "m_new%d" % t)
             nc.scalar.activation(m_new[t][:, :COPIED], m_src[t][:, :COPIED], COPY)
             nc.sync.dma_start(m_new[t][:, COPIED:], m_hbm[:, t, COPIED:])
         m_new[2] = tile([P, T], F32, "m_new2")
         nc.sync.dma_start(m_new[2][:], m_hbm[:, 2, :])
+        nc.sync.dma_start(m_new[3][:, COPIED:], m_hbm[:, 3, COPIED:])
 
         PER = CHUNK // P
 
@@ -210,13 +209,11 @@ def tile_attend_gsig_pl_mom_kernel(tc, xT, wT, y, wt, xm, mT, offs, out_0, out_1
                 first = [turn(0, c, "first%d" % c) for c in range(CHUNKS)]
 
         for t in range(LANES - 1):
-            if t == 0:
-                nc.vector.tensor_copy(m_new[t][:].indirect(offsets[:]), nm_first[:])
-            else:
-                nc.vector.tensor_tensor(m_new[t][:].indirect(offsets[:]), u[:, t - 1, :], beta[:], MULT)
+            nc.vector.tensor_tensor(m_new[t][:].indirect(offsets[:]), u[:, t, :], beta[:], MULT)
             nc.sync.dma_start(o1_hbm[:, t, :], m_new[t][:])
+        nc.vector.tensor_tensor(m_new[3][:].indirect(offsets[:, :HALF // 16]), u[:, 3, :HALF], beta[:, :HALF], MULT)
 
-        o_s = tile([P, CHUNK], U8, "o_s")
+        o_s = tile([P, T], U8, "o_s", tag="x_bf1")
         words_hbm = out_2[0].rearrange("p c l -> p (c l)").bitcast(I32)
         o_q = tile([P, T], U32, "o_q", tag="yw")
         for c, tag_in in enumerate(["x_raw0", "x_raw1", "y_sb0", "y_sb1"]):
@@ -233,14 +230,14 @@ def tile_attend_gsig_pl_mom_kernel(tc, xT, wT, y, wt, xm, mT, offs, out_0, out_1
                     acc[:].rearrange("p (b u n) -> p b n u", b=2, u=2),
                 )
             cols = slice(c * CHUNK, (c + 1) * CHUNK)
-            nc.vector.quantize_mx(o_q[:, cols].bitcast(E4M3), o_s[4 * c:P, :], o_bf[:])
+            nc.vector.quantize_mx(o_q[:, cols].bitcast(E4M3), o_s[:, cols], o_bf[:])
             if c % 2 == 1:
                 both = slice((c - 1) * CHUNK, (c + 1) * CHUNK)
                 nc.sync.dma_start(words_hbm[:, both], o_q[:, both].bitcast(I32))
-        scales_hbm = out_3[0].bitcast(I32).rearrange("f (c n) -> c f n", c=CHUNKS)
+        scales_hbm = out_3[0].bitcast(I32)
         for q in range(4):
-            nc.sync.dma_start(scales_hbm[:, 4 * q:4 * q + 4, :], o_s[32 * q:32 * q + 16, :].bitcast(I32))
-        nm_last = tile([P, N], F32, "nm_last", tag="second%d" % (CHUNKS - 1))
-        nc.scalar.activation(nm_last[:], u[:, LANES - 2, :], COPY, scale=BETA)
-        nc.vector.tensor_copy(m_new[3][:].indirect(offsets[:]), nm_last[:])
+            nc.sync.dma_start(scales_hbm[4 * q:4 * q + 4, :], o_s[32 * q:32 * q + 4, :].bitcast(I32))
+        beta_last = tile([P, HALF], F32, "beta_last", tag="second%d" % (CHUNKS - 1))
+        nc.scalar.activation(beta_last[:], beta[:, :HALF], COPY)
+        nc.vector.tensor_tensor(m_new[3][:].indirect(offsets[:, HALF // 16:]), u[:, 3, HALF:], beta_last[:], MULT)
         nc.sync.dma_start(o1_hbm[:, 3, :], m_new[3][:])

@@ -56,13 +56,14 @@ def tile_attend_gsig_pl_mom_kernel(tc, xT, wT, y, wt, xm, mT, offs, out_0, out_1
                 nc.sync.dma_start(offsets[:], offs)
                 nc.sync.dma_start(wt_sb[:], wt[0].rearrange("(p t) o -> p (t o)", t=LANES))
         x_hbm = planes(xT[0])
-        x_raw = [tile([P, LANES, R // 2], F32, "x_raw%d" % h) for h in range(2)]
-        for h in range(2):
-            nc.sync.dma_start(x_raw[h][:], x_hbm[:, :, h * (R // 2):(h + 1) * (R // 2)])
-        y_sb = [tile([P, 2, N], F32, "y_sb%d" % k) for k in range(2)]
+        x_raw = [tile([P, LANES, R // 4], F32, "x_raw%d" % h) for h in range(4)]
+        for h in range(4):
+            nc.sync.dma_start(x_raw[h][:], x_hbm[:, :, h * (R // 4):(h + 1) * (R // 4)])
+        y_sb = [[tile([P, 2, HALF], F32, "y_sb%d%d" % (h, k)) for k in range(2)] for h in range(2)]
         xm_raw = tile([P, LANES, D], F32, "xm_raw")
         for h in range(2):
-            nc.sync.dma_start(y_sb[h][:], planes(y[0])[:, 2 * h:2 * h + 2, :])
+            for k in range(2):
+                nc.sync.dma_start(y_sb[h][k][:], planes(y[0])[:, 2 * k:2 * k + 2, h * HALF:(h + 1) * HALF])
         nc.sync.dma_start(xm_raw[:], planes(xm[0]))
         m_src = [tile([P, T], F32, "m_src%d" % t) for t in range(LANES)]
         w_new = [tile([P, T], F32, "w_new%d" % t) for t in range(LANES)]
@@ -105,10 +106,10 @@ def tile_attend_gsig_pl_mom_kernel(tc, xT, wT, y, wt, xm, mT, offs, out_0, out_1
             nc.vector.quantize_mx(w_q[:, slots].bitcast(E4M3), w_s[:, slots], w_bf[h][:])
 
         x_bf = [tile([P, R * 2], BF16, "x_bf%d" % k) for k in range(2)]
-        for h in range(2):
+        for h in range(4):
             for k in range(2):
                 nc.scalar.copy(
-                    x_bf[k][:].rearrange("p (t m j) -> p m j t", t=2, j=LANES)[:, h * (P // 2):(h + 1) * (P // 2), :, :],
+                    x_bf[k][:].rearrange("p (t m j) -> p m j t", t=2, j=LANES)[:, h * (P // 4):(h + 1) * (P // 4), :, :],
                     x_raw[h][:].rearrange("p j (m t) -> p m j t", t=LANES)[:, :, :, 2 * k:2 * k + 2],
                 )
         x_q = tile([P, R], U32, "x_q")
@@ -121,19 +122,24 @@ def tile_attend_gsig_pl_mom_kernel(tc, xT, wT, y, wt, xm, mT, offs, out_0, out_1
         yw = tile([P, LANES, N], F32, "yw")
         wt_neg = tile([P, LANES], F32, "wt_neg")
         nc.gpsimd.tensor_scalar(wt_neg[:], wt_sb[:], -1.0, 0.0, MULT, ADD)
-        for t in range(2):
-            nc.scalar.activation(yw[:, t, :], y_sb[0][:, t, :], COPY, scale=wt_neg[:, t:t + 1])
-        for t in range(2, LANES):
-            nc.gpsimd.tensor_scalar(yw[:, t, :], y_sb[1][:, t - 2, :], wt_neg[:, t:t + 1], 0.0, MULT, ADD)
-        for k in range(2):
-            for h in range(2):
-                slots = slice(h * HALF, (h + 1) * HALF)
-                a = bank("a")
-                for e in range(2):
-                    cols = slice((2 * k + e) * P, (2 * k + e + 1) * P)
-                    nc.tensor.matmul_mx(a[:, e * HALF:(e + 1) * HALF], x_q[:, cols].bitcast(E4M3), x_s[:, cols], w_q[:, slots].bitcast(E4M3), w_s[:, slots], start=True, stop=True)
-                z = tile([P, 2, HALF], F32, "z%d%d" % (h, k), tag=["step0", "step1", "step2", "xm_bf0"][2 * k + h])
-                nc.vector.tensor_tensor(z[:], a[:].rearrange("p (e n) -> p e n", e=2), y_sb[k][:, :, slots], MULT)
+        for h in range(2):
+            slots = slice(h * HALF, (h + 1) * HALF)
+            for t in range(LANES):
+                if h == 0 and t < 2:
+                    nc.scalar.activation(yw[:, t, slots], y_sb[h][t // 2][:, t % 2, :], COPY, scale=wt_neg[:, t:t + 1])
+                else:
+                    nc.gpsimd.tensor_scalar(yw[:, t, slots], y_sb[h][t // 2][:, t % 2, :], wt_neg[:, t:t + 1], 0.0, MULT, ADD)
+        for h in range(2):
+            slots = slice(h * HALF, (h + 1) * HALF)
+            for k in range(2):
+                z = tile([P, 2, HALF], F32, "z%d%d" % (h, k), tag=["x_bf1", "step0", "step1", "xm_bf0"][2 * h + k])
+                count = 1 if h == k else 2
+                for e0 in range(0, 2, count):
+                    a = bank("a")
+                    for e in range(count):
+                        cols = slice((2 * k + e0 + e) * P, (2 * k + e0 + e + 1) * P)
+                        nc.tensor.matmul_mx(a[:, e * HALF:(e + 1) * HALF], x_q[:, cols].bitcast(E4M3), x_s[:, cols], w_q[:, slots].bitcast(E4M3), w_s[:, slots], start=True, stop=True)
+                    nc.vector.tensor_tensor(z[:, e0:e0 + count, :], a[:, :count * HALF].rearrange("p (e n) -> p e n", e=count), y_sb[h][k][:, e0:e0 + count, :], MULT)
                 nc.scalar.activation(sig[h][:, 2 * k:2 * k + 2, :], z[:], SIGMOID, scale=-1.0)
 
         xm_cols = xm_raw[:].rearrange("p j (m t) -> p m j t", t=LANES)
@@ -154,13 +160,14 @@ def tile_attend_gsig_pl_mom_kernel(tc, xT, wT, y, wt, xm, mT, offs, out_0, out_1
         xm_s = tile([P, D], U8, "xm_s")
         g_q = tile([P, N], U32, "g_q")
         g_s = tile([P, N], U8, "g_s")
-        m_first = tile([P, N], F32, "m_first", tag="x_bf0")
+        m_first = [tile([P, HALF], F32, "m_first%d" % h, tag=["m_new1", "x_bf0"][h]) for h in range(2)]
         for k in range(2):
             cols = slice(k * 2 * P, (k + 1) * 2 * P)
             nc.vector.quantize_mx(xm_q[:, cols].bitcast(E4M3), xm_s[:, cols], xm_bf[k][:])
             if k == 0:
                 nc.vector.quantize_mx(g_q[:].bitcast(E5M2), g_s[:], g_bf[:])
-                nc.vector.tensor_copy(m_first[:], m_src[0][:].indirect(offsets[:]))
+                for h in range(2):
+                    nc.vector.tensor_copy(m_first[h][:], m_src[0][:].indirect(offsets[:, h * (HALF // 16):(h + 1) * (HALF // 16)]))
 
         u = tile([P, LANES, N], F32, "u")
         step = []
@@ -170,9 +177,11 @@ def tile_attend_gsig_pl_mom_kernel(tc, xT, wT, y, wt, xm, mT, offs, out_0, out_1
             nc.tensor.matmul_mx(dw[:], xm_q[:, cols].bitcast(E4M3), xm_s[:, cols], g_q[:].bitcast(E5M2), g_s[:], start=True, stop=True)
             step.append(tile([P, N], F32, "step%d" % t))
             if t == 0:
-                nc.vector.scalar_tensor_tensor(u[:, t, :], dw[:], 1.0 / BETA, m_first[:], MULT, ADD)
+                for h in range(2):
+                    slots = slice(h * HALF, (h + 1) * HALF)
+                    nc.vector.scalar_tensor_tensor(u[:, t, slots], dw[:, slots], 1.0 / BETA, m_first[h][:], MULT, ADD)
             else:
-                dw_sb = tile([P, N], F32, "dw_sb%d" % t, tag=["m_new0", "m_new1", "xm_raw"][t - 1])
+                dw_sb = tile([P, N], F32, "dw_sb%d" % t, tag=["m_new0", "m_new1", "x_bf0"][t - 1])
                 nc.scalar.activation(dw_sb[:], dw[:], COPY, scale=1.0 / BETA)
                 nc.vector.tensor_tensor(u[:, t, :], m_src[t][:].indirect(offsets[:]), dw_sb[:], ADD)
             nc.scalar.activation(step[t][:], u[:, t, :], COPY, scale=-LR * BETA)
@@ -216,7 +225,7 @@ def tile_attend_gsig_pl_mom_kernel(tc, xT, wT, y, wt, xm, mT, offs, out_0, out_1
         o_s = tile([P, T], U8, "o_s", tag="x_bf1")
         words_hbm = out_2[0].rearrange("p c l -> p (c l)").bitcast(I32)
         o_q = tile([P, T], U32, "o_q", tag="yw")
-        for c, tag_in in enumerate(["x_raw0", "x_raw1", "y_sb0", "y_sb1"]):
+        for c, tag_in in enumerate(["sig1", "g_bf", "xm_raw", "sig0"]):
             pair = [first[c], turn(1, c, "second%d" % c)]
             o_bf = tile([P, CHUNK * LANES], BF16, "o_bf%d" % c, tag=tag_in)
             for b0 in range(0, PER, 2):

@@ -114,9 +114,10 @@ def tile_attend_gsig_pl_mom_kernel(tc, xT, wT, y, wt, xm, mT, offs, out_0, out_1
                 )
         x_q = tile([P, R], U32, "x_q")
         x_s = tile([P, R], U8, "x_s")
-        for k in range(2):
-            cols = slice(k * 2 * P, (k + 1) * 2 * P)
-            nc.vector.quantize_mx(x_q[:, cols].bitcast(E4M3), x_s[:, cols], x_bf[k][:])
+        for t in range(2):
+            cols = slice(t * P, (t + 1) * P)
+            nc.vector.quantize_mx(x_q[:, cols].bitcast(E4M3), x_s[:, cols], x_bf[0][:, t * LANES * P:(t + 1) * LANES * P])
+        nc.vector.quantize_mx(x_q[:, 2 * P:].bitcast(E4M3), x_s[:, 2 * P:], x_bf[1][:])
 
         sig = [tile([P, LANES, HALF], F32, "sig%d" % h) for h in range(2)]
         yw = tile([P, LANES, N], F32, "yw")
@@ -240,9 +241,9 @@ def tile_attend_gsig_pl_mom_kernel(tc, xT, wT, y, wt, xm, mT, offs, out_0, out_1
                 )
             cols = slice(c * CHUNK, (c + 1) * CHUNK)
             nc.vector.quantize_mx(o_q[:, cols].bitcast(E4M3), o_s[:, cols], o_bf[:])
-            if c % 2 == 1:
-                both = slice((c - 1) * CHUNK, (c + 1) * CHUNK)
-                nc.sync.dma_start(words_hbm[:, both], o_q[:, both].bitcast(I32))
+            if c > 0:
+                done = slice(0 if c == 1 else c * CHUNK, (c + 1) * CHUNK)
+                nc.sync.dma_start(words_hbm[:, done], o_q[:, done].bitcast(I32))
         scales_hbm = out_3[0].bitcast(I32)
         for q in range(4):
             nc.sync.dma_start(scales_hbm[4 * q:4 * q + 4, :], o_s[32 * q:32 * q + 4, :].bitcast(I32))

@@ -81,8 +81,7 @@ def tile_attend_gsig_pl_mom_kernel(tc, xT, wT, y, wt, xm, mT, offs, out_0, out_1
         ident = tile([P, P], F32, "ident")
         make_identity(nc, ident[:])
         beta = tile([P, N], F32, "beta")
-        nc.gpsimd.memset(beta[:], 1.0)
-        nc.gpsimd.tensor_scalar(beta[:], beta[:], BETA, 0.0, MULT, ADD)
+        nc.gpsimd.memset(beta[:], -1.0 / LR)
 
         w_g = tile([P, LANES, N], F32, "w_g")
         w_bf = [tile([P, HALF * LANES], BF16, "w_bf%d" % h) for h in range(2)]
@@ -161,31 +160,31 @@ def tile_attend_gsig_pl_mom_kernel(tc, xT, wT, y, wt, xm, mT, offs, out_0, out_1
         xm_s = tile([P, D], U8, "xm_s")
         g_q = tile([P, N], U32, "g_q")
         g_s = tile([P, N], U8, "g_s")
-        m_first = [tile([P, HALF], F32, "m_first%d" % h, tag=["m_new1", "x_bf0"][h]) for h in range(2)]
-        for k in range(2):
-            cols = slice(k * 2 * P, (k + 1) * 2 * P)
-            nc.vector.quantize_mx(xm_q[:, cols].bitcast(E4M3), xm_s[:, cols], xm_bf[k][:])
-            if k == 0:
-                nc.vector.quantize_mx(g_q[:].bitcast(E5M2), g_s[:], g_bf[:])
-                for h in range(2):
-                    nc.vector.tensor_copy(m_first[h][:], m_src[0][:].indirect(offsets[:, h * (HALF // 16):(h + 1) * (HALF // 16)]))
+        m_first = [tile([P, HALF], F32, "m_first%d" % h, tag=["x_bf0", "m_new1"][h]) for h in range(2)]
+        nc.vector.quantize_mx(g_q[:, :HALF].bitcast(E5M2), g_s[:, :HALF], g_bf[:, :HALF * LANES])
+        nc.vector.quantize_mx(xm_q[:, :P].bitcast(E4M3), xm_s[:, :P], xm_bf[0][:, :LANES * P])
+        nc.vector.quantize_mx(g_q[:, HALF:].bitcast(E5M2), g_s[:, HALF:], g_bf[:, HALF * LANES:])
+        nc.vector.quantize_mx(xm_q[:, P:2 * P].bitcast(E4M3), xm_s[:, P:2 * P], xm_bf[0][:, LANES * P:])
+        for h in range(2):
+            nc.vector.tensor_copy(m_first[h][:], m_src[0][:].indirect(offsets[:, h * (HALF // 16):(h + 1) * (HALF // 16)]))
+        nc.vector.quantize_mx(xm_q[:, 2 * P:].bitcast(E4M3), xm_s[:, 2 * P:], xm_bf[1][:])
 
-        u = tile([P, LANES, N], F32, "u")
         step = []
         for t in range(LANES):
             cols = slice(t * P, (t + 1) * P)
             dw = bank("dw")
             nc.tensor.matmul_mx(dw[:], xm_q[:, cols].bitcast(E4M3), xm_s[:, cols], g_q[:].bitcast(E5M2), g_s[:], start=True, stop=True)
-            step.append(tile([P, N], F32, "step%d" % t))
+            u = tile([P, N], F32, "u%d" % t, tag=["m_new0", "x_raw1", "x_raw2", "x_raw3"][t])
             if t == 0:
                 for h in range(2):
                     slots = slice(h * HALF, (h + 1) * HALF)
-                    nc.vector.scalar_tensor_tensor(u[:, t, slots], dw[:, slots], 1.0 / BETA, m_first[h][:], MULT, ADD)
+                    nc.vector.scalar_tensor_tensor(u[:, slots], dw[:, slots], 1.0 / BETA, m_first[h][:], MULT, ADD)
             else:
-                dw_sb = tile([P, N], F32, "dw_sb%d" % t, tag=["m_new0", "m_new1", "x_bf0"][t - 1])
+                dw_sb = tile([P, N], F32, "dw_sb%d" % t, tag=["step3", "m_new1", "step3"][t - 1])
                 nc.scalar.activation(dw_sb[:], dw[:], COPY, scale=1.0 / BETA)
-                nc.vector.tensor_tensor(u[:, t, :], m_src[t][:].indirect(offsets[:]), dw_sb[:], ADD)
-            nc.scalar.activation(step[t][:], u[:, t, :], COPY, scale=-LR * BETA)
+                nc.vector.tensor_tensor(u[:], m_src[t][:].indirect(offsets[:]), dw_sb[:], ADD)
+            step.append(tile([P, N], F32, "step%d" % t))
+            nc.scalar.activation(step[t][:], u[:], COPY, scale=-LR * BETA)
         for t in range(2):
             m_new[t] = tile([P, T], F32, "m_new%d" % t)
             nc.scalar.activation(m_new[t][:, :COPIED], m_src[t][:, :COPIED], COPY)
@@ -219,9 +218,9 @@ def tile_attend_gsig_pl_mom_kernel(tc, xT, wT, y, wt, xm, mT, offs, out_0, out_1
                 first = [turn(0, c, "first%d" % c) for c in range(CHUNKS)]
 
         for t in range(LANES - 1):
-            nc.vector.tensor_tensor(m_new[t][:].indirect(offsets[:]), u[:, t, :], beta[:], MULT)
+            nc.vector.tensor_tensor(m_new[t][:].indirect(offsets[:]), step[t][:], beta[:], MULT)
             nc.sync.dma_start(o1_hbm[:, t, :], m_new[t][:])
-        nc.vector.tensor_tensor(m_new[3][:].indirect(offsets[:, :HALF // 16]), u[:, 3, :HALF], beta[:, :HALF], MULT)
+        nc.vector.tensor_tensor(m_new[3][:].indirect(offsets[:, :HALF // 16]), step[3][:, :HALF], beta[:, :HALF], MULT)
 
         o_s = tile([P, T], U8, "o_s", tag="x_bf1")
         words_hbm = out_2[0].rearrange("p c l -> p (c l)").bitcast(I32)
@@ -249,5 +248,5 @@ def tile_attend_gsig_pl_mom_kernel(tc, xT, wT, y, wt, xm, mT, offs, out_0, out_1
             nc.sync.dma_start(scales_hbm[4 * q:4 * q + 4, :], o_s[32 * q:32 * q + 4, :].bitcast(I32))
         beta_last = tile([P, HALF], F32, "beta_last", tag="second%d" % (CHUNKS - 1))
         nc.scalar.activation(beta_last[:], beta[:, :HALF], COPY)
-        nc.vector.tensor_tensor(m_new[3][:].indirect(offsets[:, HALF // 16:]), u[:, 3, HALF:], beta_last[:], MULT)
+        nc.vector.tensor_tensor(m_new[3][:].indirect(offsets[:, HALF // 16:]), step[3][:, HALF:], beta_last[:], MULT)
         nc.sync.dma_start(o1_hbm[:, 3, :], m_new[3][:])

@@ -220,7 +220,6 @@ def tile_attend_gsig_pl_mom_kernel(tc, xT, wT, y, wt, xm, mT, offs, out_0, out_1
         for t in range(LANES - 1):
             nc.vector.tensor_tensor(m_new[t][:].indirect(offsets[:]), step[t][:], beta[:], MULT)
             nc.sync.dma_start(o1_hbm[:, t, :], m_new[t][:])
-        nc.vector.tensor_tensor(m_new[3][:].indirect(offsets[:, :HALF // 16]), step[3][:, :HALF], beta[:, :HALF], MULT)
 
         o_s = tile([P, T], U8, "o_s", tag="x_bf1")
         words_hbm = out_2[0].rearrange("p c l -> p (c l)").bitcast(I32)
@@ -243,6 +242,10 @@ def tile_attend_gsig_pl_mom_kernel(tc, xT, wT, y, wt, xm, mT, offs, out_0, out_1
             if c > 0:
                 done = slice(0 if c == 1 else c * CHUNK, (c + 1) * CHUNK)
                 nc.sync.dma_start(words_hbm[:, done], o_q[:, done].bitcast(I32))
+            if c == 1:
+                beta_mid = tile([P, HALF], F32, "beta_mid", tag="second1")
+                nc.scalar.activation(beta_mid[:], beta[:, :HALF], COPY)
+                nc.vector.tensor_tensor(m_new[3][:].indirect(offsets[:, :HALF // 16]), step[3][:, :HALF], beta_mid[:], MULT)
         scales_hbm = out_3[0].bitcast(I32)
         for q in range(4):
             nc.sync.dma_start(scales_hbm[4 * q:4 * q + 4, :], o_s[32 * q:32 * q + 4, :].bitcast(I32))

@@ -1,7 +1,6 @@
 from contextlib import ExitStack
 
 import concourse.mybir as mybir
-from concourse.masks import make_identity
 
 F32 = mybir.dt.float32
 BF16 = mybir.dt.bfloat16
@@ -24,16 +23,15 @@ BETA = 0.9
 FLOPS = 2 * 2 * D * R * N
 
 HALF = N // 2
-BLOCKS = T // P
 CHUNKS = 4
 CHUNK = T // CHUNKS
-COPIED = 7 * T // 8
 
 
 def tile_attend_gsig_pl_mom_kernel(tc, xT, wT, y, wt, xm, mT, offs, out_0, out_1, out_2, out_3):
     nc = tc.nc
     with ExitStack() as ctx:
         sb = ctx.enter_context(tc.tile_pool(name="sb", bufs=1))
+        late = ctx.enter_context(tc.tile_pool(name="late", bufs=1))
         ps = ctx.enter_context(tc.psum_pool(name="ps", bufs=8))
 
         def tile(shape, dtype, name, tag=None):
@@ -66,24 +64,20 @@ def tile_attend_gsig_pl_mom_kernel(tc, xT, wT, y, wt, xm, mT, offs, out_0, out_1
                 nc.sync.dma_start(y_sb[h][k][:], planes(y[0])[:, 2 * k:2 * k + 2, h * HALF:(h + 1) * HALF])
         nc.sync.dma_start(xm_raw[:], planes(xm[0]))
         m_src = [tile([P, T], F32, "m_src%d" % t) for t in range(LANES)]
-        w_new = [tile([P, T], F32, "w_new%d" % t) for t in range(LANES)]
+        w_new = [tile([P, T], F32, "w_new%d" % t) for t in range(LANES - 1)]
+        w_new.append(tile([P, T], F32, "w_new3"))
         for t in range(LANES):
+            if t == 3:
+                nc.sync.dma_start(w_new[3][:], w_hbm[:, 3, :])
             nc.sync.dma_start(m_src[t][:], m_hbm[:, t, :])
-            if t > 0:
-                nc.sync.dma_start(w_new[t - 1][:, COPIED:], w_hbm[:, t - 1, COPIED:])
-        nc.sync.dma_start(w_new[3][:], w_hbm[:, 3, :])
         m_new = {3: tile([P, T], F32, "m_new3")}
-        nc.sync.dma_start(m_new[3][:, :COPIED], m_hbm[:, 3, :COPIED])
+        nc.sync.dma_start(m_new[3][:], m_hbm[:, 3, :])
 
         warm = tile([P, 1], F32, "warm")
         nc.gpsimd.memset(warm[:], 0.0)
         nc.scalar.activation(warm[:], warm[:], SIGMOID)
-        ident = tile([P, P], F32, "ident")
-        make_identity(nc, ident[:])
-        beta = tile([P, N], F32, "beta")
-        nc.gpsimd.memset(beta[:], -1.0 / LR)
 
-        w_g = tile([P, LANES, N], F32, "w_g")
+        w_g = late.tile([P, LANES, N], F32, name="w_g", offset=2 * T)
         w_bf = [tile([P, HALF * LANES], BF16, "w_bf%d" % h) for h in range(2)]
         w_view = [w_bf[h][:].rearrange("p (c t) -> p c t", t=LANES) for h in range(2)]
         for t in range(LANES - 1):
@@ -97,7 +91,7 @@ def tile_attend_gsig_pl_mom_kernel(tc, xT, wT, y, wt, xm, mT, offs, out_0, out_1
             slots = slice(h * HALF, (h + 1) * HALF)
             nc.vector.tensor_copy(w_view[h][:, :, 2:4], w_g[:, 2:4, slots].rearrange("p t c -> p c t"))
         for t in range(LANES - 1):
-            nc.scalar.activation(w_new[t][:, :COPIED], w_src[t][:, :COPIED], COPY)
+            nc.scalar.activation(w_new[t][:], w_src[t][:], COPY)
         w_q = tile([P, N], U32, "w_q")
         w_s = tile([P, N], U8, "w_s")
         for h in range(2):
@@ -160,96 +154,104 @@ def tile_attend_gsig_pl_mom_kernel(tc, xT, wT, y, wt, xm, mT, offs, out_0, out_1
         xm_s = tile([P, D], U8, "xm_s")
         g_q = tile([P, N], U32, "g_q")
         g_s = tile([P, N], U8, "g_s")
-        m_first = [tile([P, HALF], F32, "m_first%d" % h, tag=["x_bf0", "m_new1"][h]) for h in range(2)]
+        halves = [offsets[:, h * (HALF // 16):(h + 1) * (HALF // 16)] for h in range(2)]
+        m_g = {0: tile([P, N], F32, "m_g0", tag="m_new1")}
         nc.vector.quantize_mx(g_q[:, :HALF].bitcast(E5M2), g_s[:, :HALF], g_bf[:, :HALF * LANES])
         nc.vector.quantize_mx(xm_q[:, :P].bitcast(E4M3), xm_s[:, :P], xm_bf[0][:, :LANES * P])
         nc.vector.quantize_mx(g_q[:, HALF:].bitcast(E5M2), g_s[:, HALF:], g_bf[:, HALF * LANES:])
         nc.vector.quantize_mx(xm_q[:, P:2 * P].bitcast(E4M3), xm_s[:, P:2 * P], xm_bf[0][:, LANES * P:])
-        for h in range(2):
-            nc.vector.tensor_copy(m_first[h][:], m_src[0][:].indirect(offsets[:, h * (HALF // 16):(h + 1) * (HALF // 16)]))
+        nc.vector.tensor_scalar(m_g[0][:], m_src[0][:].indirect(offsets[:]), -LR * BETA, 0.0, MULT, ADD)
         nc.vector.quantize_mx(xm_q[:, 2 * P:].bitcast(E4M3), xm_s[:, 2 * P:], xm_bf[1][:])
 
-        step = []
+        m_new[0] = tile([P, T], F32, "m_new0")
+        nc.scalar.activation(m_new[0][:], m_src[0][:], COPY)
+
+        dw = []
         for t in range(LANES):
             cols = slice(t * P, (t + 1) * P)
-            dw = bank("dw")
-            nc.tensor.matmul_mx(dw[:], xm_q[:, cols].bitcast(E4M3), xm_s[:, cols], g_q[:].bitcast(E5M2), g_s[:], start=True, stop=True)
-            u = tile([P, N], F32, "u%d" % t, tag=["m_new0", "x_raw1", "x_raw2", "x_raw3"][t])
-            if t == 0:
-                for h in range(2):
-                    slots = slice(h * HALF, (h + 1) * HALF)
-                    nc.vector.scalar_tensor_tensor(u[:, slots], dw[:, slots], 1.0 / BETA, m_first[h][:], MULT, ADD)
-            else:
-                dw_sb = tile([P, N], F32, "dw_sb%d" % t, tag=["step3", "m_new1", "step3"][t - 1])
-                nc.scalar.activation(dw_sb[:], dw[:], COPY, scale=1.0 / BETA)
-                nc.vector.tensor_tensor(u[:], m_src[t][:].indirect(offsets[:]), dw_sb[:], ADD)
-            step.append(tile([P, N], F32, "step%d" % t))
-            nc.scalar.activation(step[t][:], u[:], COPY, scale=-LR * BETA)
-        for t in range(2):
-            m_new[t] = tile([P, T], F32, "m_new%d" % t)
-            nc.scalar.activation(m_new[t][:, :COPIED], m_src[t][:, :COPIED], COPY)
-            nc.sync.dma_start(m_new[t][:, COPIED:], m_hbm[:, t, COPIED:])
-        m_new[2] = tile([P, T], F32, "m_new2")
-        nc.sync.dma_start(m_new[2][:], m_hbm[:, 2, :])
-        nc.sync.dma_start(m_new[3][:, COPIED:], m_hbm[:, 3, COPIED:])
+            dw.append(bank("dw"))
+            nc.tensor.matmul_mx(dw[t][:], xm_q[:, cols].bitcast(E4M3), xm_s[:, cols], g_q[:].bitcast(E5M2), g_s[:], start=True, stop=True)
+        step = [tile([P, N], F32, "step%d" % t) for t in range(LANES)]
 
-        PER = CHUNK // P
+        def make_step(t):
+            nc.vector.scalar_tensor_tensor(step[t][:], dw[t][:], -LR, m_g[t][:], MULT, ADD)
 
-        def turn(e2, c, tag):
-            dst = tile([P, PER, 2 * P], BF16, "turned%d_%d" % (e2, c), tag=tag)
-            for b0 in range(0, PER, 2):
-                acc = bank("t1")
-                view = acc[:].rearrange("p (b e q) -> p b e q", b=2, e=2)
-                for b in range(2):
-                    blk = c * PER + b0 + b
-                    for e in range(2):
-                        nc.tensor.transpose(view[:, b, e, :], w_new[2 * e2 + e][:, blk * P:(blk + 1) * P], ident[:])
-                nc.scalar.copy(
-                    dst[:, b0:b0 + 2, :].rearrange("p b (q e) -> p b q e", e=2),
-                    acc[:].rearrange("p (b e q) -> p b q e", b=2, e=2),
-                )
-            return dst
+        def scalar_scatter(window, values, scale, dst):
+            for h in range(2):
+                nc.scalar.activation(window[:].indirect(halves[h]), values[:, h * HALF:(h + 1) * HALF], COPY, scale=scale)
+            nc.sync.dma_start(dst, window[:])
 
-        first = []
-        for t in range(LANES):
+        def vector_scatter(t):
             nc.vector.tensor_tensor(w_new[t][:].indirect(offsets[:]), w_g[:, t, :], step[t][:], ADD)
             nc.sync.dma_start(o0_hbm[:, t, :], w_new[t][:])
-            if t == 1:
-                first = [turn(0, c, "first%d" % c) for c in range(CHUNKS)]
 
-        for t in range(LANES - 1):
-            nc.vector.tensor_tensor(m_new[t][:].indirect(offsets[:]), step[t][:], beta[:], MULT)
-            nc.sync.dma_start(o1_hbm[:, t, :], m_new[t][:])
+        def gather_m(t, tag):
+            m_g[t] = tile([P, N], F32, "m_g%d" % t, tag=tag)
+            nc.vector.tensor_scalar(m_g[t][:], m_src[t][:].indirect(offsets[:]), -LR * BETA, 0.0, MULT, ADD)
+
+        def new_w(t, tag):
+            w_dense = tile([P, N], F32, "w_dense%d" % t, tag=tag)
+            nc.vector.tensor_tensor(w_dense[:], w_g[:, t, :], step[t][:], ADD)
+            scalar_scatter(w_new[t], w_dense, 1.0, o0_hbm[:, t, :])
+
+        def copy_m(t, cols):
+            nc.vector.tensor_copy(m_new[t][:, cols], m_src[t][:, cols])
+
+        def scatter_m(t):
+            scalar_scatter(m_new[t], step[t], -1.0 / LR, o1_hbm[:, t, :])
+
+        def pair_up(t):
+            nc.vector.tensor_copy(pairs[:, t // 2, :, t % 2], w_new[t][:])
+
+        make_step(0)
+        scatter_m(0)
+        gather_m(1, "m_g1")
+        new_w(0, "y_sb00")
+        make_step(1)
+        m_new[1] = tile([P, T], F32, "m_new1")
+        copy_m(1, slice(0, 7 * T // 8))
+        new_w(1, "y_sb01")
+        copy_m(1, slice(7 * T // 8, T))
+        scatter_m(1)
+        gather_m(2, "m_g1")
+        gather_m(3, "m_g3")
+        make_step(2)
+        make_step(3)
+        vector_scatter(2)
+        new_w(3, "y_sb10")
+        scatter_m(3)
+        pairs = late.tile([P, 2, T, 2], BF16, name="pairs", offset=4 * T)
+        m_new[2] = late.tile([P, T], F32, name="m_new2", offset=0)
+        pair_up(0)
+        copy_m(2, slice(0, T))
+        pair_up(2)
+        nc.scalar.activation(m_new[2][:].indirect(halves[0]), step[2][:, :HALF], COPY, scale=-1.0 / LR)
+        pair_up(1)
+        pair_up(3)
 
         o_s = tile([P, T], U8, "o_s", tag="x_bf1")
         words_hbm = out_2[0].rearrange("p c l -> p (c l)").bitcast(I32)
         o_q = tile([P, T], U32, "o_q", tag="yw")
-        for c, tag_in in enumerate(["sig1", "g_bf", "xm_raw", "sig0"]):
-            pair = [first[c], turn(1, c, "second%d" % c)]
-            o_bf = tile([P, CHUNK * LANES], BF16, "o_bf%d" % c, tag=tag_in)
-            for b0 in range(0, PER, 2):
-                acc = bank("t2")
-                view = acc[:].rearrange("p (b u n) -> p b u n", b=2, u=2)
-                for b in range(2):
-                    for e2 in range(2):
-                        nc.tensor.transpose(view[:, b, e2, :], pair[e2][:, b0 + b, :].bitcast(F32), ident[:])
-                nc.scalar.copy(
-                    o_bf[:, b0 * P * LANES:(b0 + 2) * P * LANES].bitcast(F32).rearrange("p (b n u) -> p b n u", b=2, u=2),
-                    acc[:].rearrange("p (b u n) -> p b n u", b=2, u=2),
+        words = pairs[:].rearrange("p u c e -> p u (c e)").bitcast(F32)
+        o_bf = []
+        for c in range(CHUNKS + 1):
+            if c < CHUNKS:
+                o_bf.append(tile([P, CHUNK * LANES], BF16, "o_bf%d" % c, tag="w_src%d" % c))
+                nc.vector.tensor_copy(
+                    o_bf[c][:].bitcast(F32).rearrange("p (n u) -> p n u", u=2),
+                    words[:, :, c * CHUNK:(c + 1) * CHUNK].rearrange("p u n -> p n u"),
                 )
-            cols = slice(c * CHUNK, (c + 1) * CHUNK)
-            nc.vector.quantize_mx(o_q[:, cols].bitcast(E4M3), o_s[:, cols], o_bf[:])
             if c > 0:
-                done = slice(0 if c == 1 else c * CHUNK, (c + 1) * CHUNK)
-                nc.sync.dma_start(words_hbm[:, done], o_q[:, done].bitcast(I32))
-            if c == 1:
-                beta_mid = tile([P, HALF], F32, "beta_mid", tag="second1")
-                nc.scalar.activation(beta_mid[:], beta[:, :HALF], COPY)
-                nc.vector.tensor_tensor(m_new[3][:].indirect(offsets[:, :HALF // 16]), step[3][:, :HALF], beta_mid[:], MULT)
+                cols = slice((c - 1) * CHUNK, c * CHUNK)
+                nc.vector.quantize_mx(o_q[:, cols].bitcast(E4M3), o_s[:, cols], o_bf[c - 1][:])
+                if c != 2:
+                    done = slice((c - 2 if c == 3 else c - 1) * CHUNK, c * CHUNK)
+                    nc.sync.dma_start(words_hbm[:, done], o_q[:, done].bitcast(I32))
+                if c == 1:
+                    m_last = tile([P, HALF], F32, "m_last", tag="w_src0")
+                    nc.vector.tensor_scalar(m_last[:], step[2][:, HALF:], -1.0 / LR, 0.0, MULT, ADD)
+                    nc.scalar.activation(m_new[2][:].indirect(halves[1]), m_last[:], COPY)
+                    nc.sync.dma_start(o1_hbm[:, 2, :], m_new[2][:])
         scales_hbm = out_3[0].bitcast(I32)
         for q in range(4):
             nc.sync.dma_start(scales_hbm[4 * q:4 * q + 4, :], o_s[32 * q:32 * q + 4, :].bitcast(I32))
-        beta_last = tile([P, HALF], F32, "beta_last", tag="second%d" % (CHUNKS - 1))
-        nc.scalar.activation(beta_last[:], beta[:, :HALF], COPY)
-        nc.vector.tensor_tensor(m_new[3][:].indirect(offsets[:, HALF // 16:]), step[3][:, HALF:], beta_last[:], MULT)
-        nc.sync.dma_start(o1_hbm[:, 3, :], m_new[3][:])

@@ -65,19 +65,18 @@ def tile_attend_gsig_pl_mom_kernel(tc, xT, wT, y, wt, xm, mT, offs, out_0, out_1
         nc.sync.dma_start(xm_raw[:], planes(xm[0]))
         m_src = [tile([P, T], F32, "m_src%d" % t) for t in range(LANES)]
         w_new = [tile([P, T], F32, "w_new%d" % t) for t in range(LANES - 1)]
-        w_new.append(tile([P, T], F32, "w_new3"))
+        m_new = {}
         for t in range(LANES):
-            if t == 3:
-                nc.sync.dma_start(w_new[3][:], w_hbm[:, 3, :])
             nc.sync.dma_start(m_src[t][:], m_hbm[:, t, :])
-        m_new = {3: tile([P, T], F32, "m_new3")}
-        nc.sync.dma_start(m_new[3][:], m_hbm[:, 3, :])
+            if t % 2 == 1:
+                m_new[t] = tile([P, T], F32, "m_new%d" % t)
+                nc.sync.dma_start(m_new[t][:], m_hbm[:, t, :])
 
         warm = tile([P, 1], F32, "warm")
         nc.gpsimd.memset(warm[:], 0.0)
         nc.scalar.activation(warm[:], warm[:], SIGMOID)
 
-        w_g = late.tile([P, LANES, N], F32, name="w_g", offset=2 * T)
+        w_g = late.tile([P, LANES, N], F32, name="w_g", offset=0)
         w_bf = [tile([P, HALF * LANES], BF16, "w_bf%d" % h) for h in range(2)]
         w_view = [w_bf[h][:].rearrange("p (c t) -> p c t", t=LANES) for h in range(2)]
         for t in range(LANES - 1):
@@ -105,6 +104,8 @@ def tile_attend_gsig_pl_mom_kernel(tc, xT, wT, y, wt, xm, mT, offs, out_0, out_1
                     x_bf[k][:].rearrange("p (t m j) -> p m j t", t=2, j=LANES)[:, h * (P // 4):(h + 1) * (P // 4), :, :],
                     x_raw[h][:].rearrange("p j (m t) -> p m j t", t=LANES)[:, :, :, 2 * k:2 * k + 2],
                 )
+        w_new.append(tile([P, T], F32, "w_new3", tag="x_raw3"))
+        nc.scalar.activation(w_new[3][:], w_src[3][:], COPY)
         x_q = tile([P, R], U32, "x_q")
         x_s = tile([P, R], U8, "x_s")
         for t in range(2):
@@ -119,14 +120,11 @@ def tile_attend_gsig_pl_mom_kernel(tc, xT, wT, y, wt, xm, mT, offs, out_0, out_1
         for h in range(2):
             slots = slice(h * HALF, (h + 1) * HALF)
             for t in range(LANES):
-                if h == 0 and t < 2:
-                    nc.scalar.activation(yw[:, t, slots], y_sb[h][t // 2][:, t % 2, :], COPY, scale=wt_neg[:, t:t + 1])
-                else:
-                    nc.gpsimd.tensor_scalar(yw[:, t, slots], y_sb[h][t // 2][:, t % 2, :], wt_neg[:, t:t + 1], 0.0, MULT, ADD)
+                nc.gpsimd.tensor_scalar(yw[:, t, slots], y_sb[h][t // 2][:, t % 2, :], wt_neg[:, t:t + 1], 0.0, MULT, ADD)
         for h in range(2):
             slots = slice(h * HALF, (h + 1) * HALF)
             for k in range(2):
-                z = tile([P, 2, HALF], F32, "z%d%d" % (h, k), tag=["x_bf1", "step0", "step1", "xm_bf0"][2 * h + k])
+                z = tile([P, 2, HALF], F32, "z%d%d" % (h, k), tag=["x_bf1", "nm0", "step1", "xm_bf0"][2 * h + k])
                 count = 1 if h == k else 2
                 for e0 in range(0, 2, count):
                     a = bank("a")
@@ -155,14 +153,12 @@ def tile_attend_gsig_pl_mom_kernel(tc, xT, wT, y, wt, xm, mT, offs, out_0, out_1
         g_q = tile([P, N], U32, "g_q")
         g_s = tile([P, N], U8, "g_s")
         halves = [offsets[:, h * (HALF // 16):(h + 1) * (HALF // 16)] for h in range(2)]
-        m_g = {0: tile([P, N], F32, "m_g0", tag="m_new1")}
         nc.vector.quantize_mx(g_q[:, :HALF].bitcast(E5M2), g_s[:, :HALF], g_bf[:, :HALF * LANES])
         nc.vector.quantize_mx(xm_q[:, :P].bitcast(E4M3), xm_s[:, :P], xm_bf[0][:, :LANES * P])
         nc.vector.quantize_mx(g_q[:, HALF:].bitcast(E5M2), g_s[:, HALF:], g_bf[:, HALF * LANES:])
         nc.vector.quantize_mx(xm_q[:, P:2 * P].bitcast(E4M3), xm_s[:, P:2 * P], xm_bf[0][:, LANES * P:])
-        nc.vector.tensor_scalar(m_g[0][:], m_src[0][:].indirect(offsets[:]), -LR * BETA, 0.0, MULT, ADD)
-        nc.vector.quantize_mx(xm_q[:, 2 * P:].bitcast(E4M3), xm_s[:, 2 * P:], xm_bf[1][:])
 
+        nc.vector.quantize_mx(xm_q[:, 2 * P:].bitcast(E4M3), xm_s[:, 2 * P:], xm_bf[1][:])
         m_new[0] = tile([P, T], F32, "m_new0")
         nc.scalar.activation(m_new[0][:], m_src[0][:], COPY)
 
@@ -171,63 +167,69 @@ def tile_attend_gsig_pl_mom_kernel(tc, xT, wT, y, wt, xm, mT, offs, out_0, out_1
             cols = slice(t * P, (t + 1) * P)
             dw.append(bank("dw"))
             nc.tensor.matmul_mx(dw[t][:], xm_q[:, cols].bitcast(E4M3), xm_s[:, cols], g_q[:].bitcast(E5M2), g_s[:], start=True, stop=True)
-        step = [tile([P, N], F32, "step%d" % t) for t in range(LANES)]
+        parts = [slice(h * HALF, (h + 1) * HALF) for h in range(2)]
+
+        def new_columns(t):
+            m_g = tile([P, N], F32, "m_g%d" % t)
+            nm = tile([P, N], F32, "nm%d" % t)
+            nw = tile([P, N], F32, "nw%d" % t)
+            for h in range(2):
+                nc.vector.tensor_copy(m_g[:, parts[h]], m_src[t][:].indirect(halves[h]))
+            for h in range(2):
+                nc.vector.scalar_tensor_tensor(nm[:, parts[h]], m_g[:, parts[h]], BETA, dw[t][:, parts[h]], MULT, ADD)
+            for h in range(2):
+                nc.vector.scalar_tensor_tensor(nw[:, parts[h]], nm[:, parts[h]], -LR, w_g[:, t, parts[h]], MULT, ADD)
+            return nm, nw
 
         def make_step(t):
-            nc.vector.scalar_tensor_tensor(step[t][:], dw[t][:], -LR, m_g[t][:], MULT, ADD)
+            m_g = tile([P, N], F32, "m_g%d" % t)
+            step = tile([P, N], F32, "step%d" % t)
+            nc.vector.tensor_scalar(m_g[:], m_src[t][:].indirect(offsets[:]), -LR * BETA, 0.0, MULT, ADD)
+            for h in (1, 0):
+                nc.vector.scalar_tensor_tensor(step[:, parts[h]], dw[t][:, parts[h]], -LR, m_g[:, parts[h]], MULT, ADD)
+            return step
 
-        def scalar_scatter(window, values, scale, dst):
-            for h in range(2):
-                nc.scalar.activation(window[:].indirect(halves[h]), values[:, h * HALF:(h + 1) * HALF], COPY, scale=scale)
-            nc.sync.dma_start(dst, window[:])
+        def scalar_scatter(window, values, h, scale=1.0):
+            nc.scalar.activation(window[:].indirect(halves[h]), values[:, parts[h]], COPY, scale=scale)
 
-        def vector_scatter(t):
-            nc.vector.tensor_tensor(w_new[t][:].indirect(offsets[:]), w_g[:, t, :], step[t][:], ADD)
+        def store_w(t):
             nc.sync.dma_start(o0_hbm[:, t, :], w_new[t][:])
 
-        def gather_m(t, tag):
-            m_g[t] = tile([P, N], F32, "m_g%d" % t, tag=tag)
-            nc.vector.tensor_scalar(m_g[t][:], m_src[t][:].indirect(offsets[:]), -LR * BETA, 0.0, MULT, ADD)
-
-        def new_w(t, tag):
-            w_dense = tile([P, N], F32, "w_dense%d" % t, tag=tag)
-            nc.vector.tensor_tensor(w_dense[:], w_g[:, t, :], step[t][:], ADD)
-            scalar_scatter(w_new[t], w_dense, 1.0, o0_hbm[:, t, :])
-
-        def copy_m(t, cols):
-            nc.vector.tensor_copy(m_new[t][:, cols], m_src[t][:, cols])
-
-        def scatter_m(t):
-            scalar_scatter(m_new[t], step[t], -1.0 / LR, o1_hbm[:, t, :])
+        def store_m(t):
+            nc.sync.dma_start(o1_hbm[:, t, :], m_new[t][:])
 
         def pair_up(t):
             nc.vector.tensor_copy(pairs[:, t // 2, :, t % 2], w_new[t][:])
 
-        make_step(0)
-        scatter_m(0)
-        gather_m(1, "m_g1")
-        new_w(0, "y_sb00")
-        make_step(1)
-        m_new[1] = tile([P, T], F32, "m_new1")
-        copy_m(1, slice(0, 7 * T // 8))
-        new_w(1, "y_sb01")
-        copy_m(1, slice(7 * T // 8, T))
-        scatter_m(1)
-        gather_m(2, "m_g1")
-        gather_m(3, "m_g3")
-        make_step(2)
-        make_step(3)
-        vector_scatter(2)
-        new_w(3, "y_sb10")
-        scatter_m(3)
-        pairs = late.tile([P, 2, T, 2], BF16, name="pairs", offset=4 * T)
-        m_new[2] = late.tile([P, T], F32, name="m_new2", offset=0)
-        pair_up(0)
-        copy_m(2, slice(0, T))
-        pair_up(2)
-        nc.scalar.activation(m_new[2][:].indirect(halves[0]), step[2][:, :HALF], COPY, scale=-1.0 / LR)
-        pair_up(1)
-        pair_up(3)
+        nm, nw = new_columns(0)
+        for h in range(2):
+            scalar_scatter(m_new[0], nm, h)
+            scalar_scatter(w_new[0], nw, h)
+        store_w(0)
+        step = make_step(1)
+        nc.vector.tensor_tensor(w_new[1][:].indirect(offsets[:]), w_g[:, 1, :], step[:], ADD)
+        store_w(1)
+        store_m(0)
+        for h in range(2):
+            scalar_scatter(m_new[1], step, h, -1.0 / LR)
+        store_m(1)
+        nm, nw = new_columns(2)
+        m_new[2] = tile([P, T], F32, "m_new2")
+        nc.vector.tensor_copy(m_new[2][:], m_src[2][:])
+        for h in range(2):
+            scalar_scatter(w_new[2], nw, h)
+            scalar_scatter(m_new[2], nm, h)
+        store_m(2)
+        step = make_step(3)
+        nc.vector.tensor_tensor(w_new[3][:].indirect(offsets[:]), w_g[:, 3, :], step[:], ADD)
+        store_w(3)
+        store_w(2)
+        for h in range(2):
+            scalar_scatter(m_new[3], step, h, -1.0 / LR)
+        store_m(3)
+        pairs = late.tile([P, 2, T, 2], BF16, name="pairs", offset=0)
+        for t in (0, 1, 3, 2):
+            pair_up(t)
 
         o_s = tile([P, T], U8, "o_s", tag="x_bf1")
         words_hbm = out_2[0].rearrange("p c l -> p (c l)").bitcast(I32)
@@ -237,21 +239,17 @@ def tile_attend_gsig_pl_mom_kernel(tc, xT, wT, y, wt, xm, mT, offs, out_0, out_1
         for c in range(CHUNKS + 1):
             if c < CHUNKS:
                 o_bf.append(tile([P, CHUNK * LANES], BF16, "o_bf%d" % c, tag="w_src%d" % c))
-                nc.vector.tensor_copy(
+                weave = nc.scalar.copy if c % 2 == 1 else nc.vector.tensor_copy
+                weave(
                     o_bf[c][:].bitcast(F32).rearrange("p (n u) -> p n u", u=2),
                     words[:, :, c * CHUNK:(c + 1) * CHUNK].rearrange("p u n -> p n u"),
                 )
             if c > 0:
                 cols = slice((c - 1) * CHUNK, c * CHUNK)
                 nc.vector.quantize_mx(o_q[:, cols].bitcast(E4M3), o_s[:, cols], o_bf[c - 1][:])
-                if c != 2:
-                    done = slice((c - 2 if c == 3 else c - 1) * CHUNK, c * CHUNK)
+                if c > 1:
+                    done = slice(0 if c == 2 else (c - 1) * CHUNK, c * CHUNK)
                     nc.sync.dma_start(words_hbm[:, done], o_q[:, done].bitcast(I32))
-                if c == 1:
-                    m_last = tile([P, HALF], F32, "m_last", tag="w_src0")
-                    nc.vector.tensor_scalar(m_last[:], step[2][:, HALF:], -1.0 / LR, 0.0, MULT, ADD)
-                    nc.scalar.activation(m_new[2][:].indirect(halves[1]), m_last[:], COPY)
-                    nc.sync.dma_start(o1_hbm[:, 2, :], m_new[2][:])
         scales_hbm = out_3[0].bitcast(I32)
         for q in range(4):
             nc.sync.dma_start(scales_hbm[4 * q:4 * q + 4, :], o_s[32 * q:32 * q + 4, :].bitcast(I32))

@@ -70,7 +70,8 @@ def tile_attend_gsig_pl_mom_kernel(tc, xT, wT, y, wt, xm, mT, offs, out_0, out_1
             nc.sync.dma_start(m_src[t][:], m_hbm[:, t, :])
             if t % 2 == 1:
                 m_new[t] = tile([P, T], F32, "m_new%d" % t)
-                nc.sync.dma_start(m_new[t][:], m_hbm[:, t, :])
+                cols = slice(0, T if t == 1 else T // 2)
+                nc.sync.dma_start(m_new[t][:, cols], m_hbm[:, t, cols])
 
         warm = tile([P, 1], F32, "warm")
         nc.gpsimd.memset(warm[:], 0.0)
@@ -105,7 +106,8 @@ def tile_attend_gsig_pl_mom_kernel(tc, xT, wT, y, wt, xm, mT, offs, out_0, out_1
                     x_raw[h][:].rearrange("p j (m t) -> p m j t", t=LANES)[:, :, :, 2 * k:2 * k + 2],
                 )
         w_new.append(tile([P, T], F32, "w_new3", tag="x_raw3"))
-        nc.scalar.activation(w_new[3][:], w_src[3][:], COPY)
+        nc.scalar.activation(w_new[3][:, :3 * T // 4], w_src[3][:, :3 * T // 4], COPY)
+        nc.sync.dma_start(w_new[3][:, 3 * T // 4:], w_hbm[:, 3, 3 * T // 4:])
         x_q = tile([P, R], U32, "x_q")
         x_s = tile([P, R], U8, "x_s")
         for t in range(2):
@@ -220,6 +222,7 @@ def tile_attend_gsig_pl_mom_kernel(tc, xT, wT, y, wt, xm, mT, offs, out_0, out_1
             scalar_scatter(w_new[2], nw, h)
             scalar_scatter(m_new[2], nm, h)
         store_m(2)
+        nc.scalar.activation(m_new[3][:, T // 2:], m_src[3][:, T // 2:], COPY)
         step = make_step(3)
         nc.vector.tensor_tensor(w_new[3][:].indirect(offsets[:]), w_g[:, 3, :], step[:], ADD)
         store_w(3)

@@ -65,13 +65,12 @@ def tile_attend_gsig_pl_mom_kernel(tc, xT, wT, y, wt, xm, mT, offs, out_0, out_1
         nc.sync.dma_start(xm_raw[:], planes(xm[0]))
         m_src = [tile([P, T], F32, "m_src%d" % t) for t in range(LANES)]
         w_new = [tile([P, T], F32, "w_new%d" % t) for t in range(LANES - 1)]
-        m_new = {}
+        m_new = [tile([P, T], F32, "m_new%d" % t) for t in range(LANES)]
         for t in range(LANES):
             nc.sync.dma_start(m_src[t][:], m_hbm[:, t, :])
-            if t % 2 == 1:
-                m_new[t] = tile([P, T], F32, "m_new%d" % t)
-                cols = slice(0, T if t == 1 else T // 2)
-                nc.sync.dma_start(m_new[t][:, cols], m_hbm[:, t, cols])
+            if t == 1:
+                nc.sync.dma_start(m_new[1][:], m_hbm[:, 1, :])
+        nc.sync.dma_start(m_new[2][:, :T // 2], m_hbm[:, 2, :T // 2])
 
         warm = tile([P, 1], F32, "warm")
         nc.gpsimd.memset(warm[:], 0.0)
@@ -122,7 +121,8 @@ def tile_attend_gsig_pl_mom_kernel(tc, xT, wT, y, wt, xm, mT, offs, out_0, out_1
         for h in range(2):
             slots = slice(h * HALF, (h + 1) * HALF)
             for t in range(LANES):
-                nc.gpsimd.tensor_scalar(yw[:, t, slots], y_sb[h][t // 2][:, t % 2, :], wt_neg[:, t:t + 1], 0.0, MULT, ADD)
+                engine = nc.vector if h == 0 and t < 2 else nc.gpsimd
+                engine.tensor_scalar(yw[:, t, slots], y_sb[h][t // 2][:, t % 2, :], wt_neg[:, t:t + 1], 0.0, MULT, ADD)
         for h in range(2):
             slots = slice(h * HALF, (h + 1) * HALF)
             for k in range(2):
@@ -161,7 +161,6 @@ def tile_attend_gsig_pl_mom_kernel(tc, xT, wT, y, wt, xm, mT, offs, out_0, out_1
         nc.vector.quantize_mx(xm_q[:, P:2 * P].bitcast(E4M3), xm_s[:, P:2 * P], xm_bf[0][:, LANES * P:])
 
         nc.vector.quantize_mx(xm_q[:, 2 * P:].bitcast(E4M3), xm_s[:, 2 * P:], xm_bf[1][:])
-        m_new[0] = tile([P, T], F32, "m_new0")
         nc.scalar.activation(m_new[0][:], m_src[0][:], COPY)
 
         dw = []
@@ -216,17 +215,19 @@ def tile_attend_gsig_pl_mom_kernel(tc, xT, wT, y, wt, xm, mT, offs, out_0, out_1
             scalar_scatter(m_new[1], step, h, -1.0 / LR)
         store_m(1)
         nm, nw = new_columns(2)
-        m_new[2] = tile([P, T], F32, "m_new2")
-        nc.vector.tensor_copy(m_new[2][:], m_src[2][:])
         for h in range(2):
             scalar_scatter(w_new[2], nw, h)
-            scalar_scatter(m_new[2], nm, h)
-        store_m(2)
-        nc.scalar.activation(m_new[3][:, T // 2:], m_src[3][:, T // 2:], COPY)
+        nc.scalar.activation(m_new[2][:, T // 2:], m_src[2][:, T // 2:], COPY)
         step = make_step(3)
         nc.vector.tensor_tensor(w_new[3][:].indirect(offsets[:]), w_g[:, 3, :], step[:], ADD)
         store_w(3)
         store_w(2)
+        for h in range(2):
+            scalar_scatter(m_new[2], nm, h)
+        store_m(2)
+        for h in range(2):
+            cols = slice(h * (T // 2), (h + 1) * (T // 2))
+            nc.vector.tensor_copy(m_new[3][:, cols], m_src[3][:, cols])
         for h in range(2):
             scalar_scatter(m_new[3], step, h, -1.0 / LR)
         store_m(3)

@@ -70,7 +70,7 @@ def tile_attend_gsig_pl_mom_kernel(tc, xT, wT, y, wt, xm, mT, offs, out_0, out_1
             nc.sync.dma_start(m_src[t][:], m_hbm[:, t, :])
             if t == 1:
                 nc.sync.dma_start(m_new[1][:], m_hbm[:, 1, :])
-        nc.sync.dma_start(m_new[2][:, :T // 2], m_hbm[:, 2, :T // 2])
+        nc.sync.dma_start(m_new[2][:, :3 * T // 4], m_hbm[:, 2, :3 * T // 4])
 
         warm = tile([P, 1], F32, "warm")
         nc.gpsimd.memset(warm[:], 0.0)
@@ -106,7 +106,6 @@ def tile_attend_gsig_pl_mom_kernel(tc, xT, wT, y, wt, xm, mT, offs, out_0, out_1
                 )
         w_new.append(tile([P, T], F32, "w_new3", tag="x_raw3"))
         nc.scalar.activation(w_new[3][:, :3 * T // 4], w_src[3][:, :3 * T // 4], COPY)
-        nc.sync.dma_start(w_new[3][:, 3 * T // 4:], w_hbm[:, 3, 3 * T // 4:])
         x_q = tile([P, R], U32, "x_q")
         x_s = tile([P, R], U8, "x_s")
         for t in range(2):
@@ -136,6 +135,7 @@ def tile_attend_gsig_pl_mom_kernel(tc, xT, wT, y, wt, xm, mT, offs, out_0, out_1
                     nc.vector.tensor_tensor(z[:, e0:e0 + count, :], a[:, :count * HALF].rearrange("p (e n) -> p e n", e=count), y_sb[h][k][:, e0:e0 + count, :], MULT)
                 nc.scalar.activation(sig[h][:, 2 * k:2 * k + 2, :], z[:], SIGMOID, scale=-1.0)
 
+        nc.vector.tensor_copy(w_new[3][:, 3 * T // 4:], w_src[3][:, 3 * T // 4:])
         xm_cols = xm_raw[:].rearrange("p j (m t) -> p m j t", t=LANES)
         xm_bf = [tile([P, D * 2], BF16, "xm_bf0")]
         nc.scalar.copy(xm_bf[0][:].rearrange("p (t m j) -> p m j t", t=2, j=LANES), xm_cols[:, :, :, 0:2])
@@ -150,24 +150,27 @@ def tile_attend_gsig_pl_mom_kernel(tc, xT, wT, y, wt, xm, mT, offs, out_0, out_1
             )
         xm_bf.append(tile([P, D * 2], BF16, "xm_bf1", tag="sig0"))
         nc.scalar.copy(xm_bf[1][:].rearrange("p (t m j) -> p m j t", t=2, j=LANES), xm_cols[:, :, :, 2:4])
-        xm_q = tile([P, D], U32, "xm_q")
-        xm_s = tile([P, D], U8, "xm_s")
+        xm_q = [tile([P, D // 2], U32, "xm_q0")]
+        xm_s = [tile([P, D // 2], U8, "xm_s%d" % k) for k in range(2)]
         g_q = tile([P, N], U32, "g_q")
         g_s = tile([P, N], U8, "g_s")
         halves = [offsets[:, h * (HALF // 16):(h + 1) * (HALF // 16)] for h in range(2)]
         nc.vector.quantize_mx(g_q[:, :HALF].bitcast(E5M2), g_s[:, :HALF], g_bf[:, :HALF * LANES])
-        nc.vector.quantize_mx(xm_q[:, :P].bitcast(E4M3), xm_s[:, :P], xm_bf[0][:, :LANES * P])
+        nc.vector.quantize_mx(xm_q[0][:, :P].bitcast(E4M3), xm_s[0][:, :P], xm_bf[0][:, :LANES * P])
         nc.vector.quantize_mx(g_q[:, HALF:].bitcast(E5M2), g_s[:, HALF:], g_bf[:, HALF * LANES:])
-        nc.vector.quantize_mx(xm_q[:, P:2 * P].bitcast(E4M3), xm_s[:, P:2 * P], xm_bf[0][:, LANES * P:])
+        nc.vector.quantize_mx(xm_q[0][:, P:].bitcast(E4M3), xm_s[0][:, P:], xm_bf[0][:, LANES * P:])
 
-        nc.vector.quantize_mx(xm_q[:, 2 * P:].bitcast(E4M3), xm_s[:, 2 * P:], xm_bf[1][:])
         nc.scalar.activation(m_new[0][:], m_src[0][:], COPY)
 
         dw = []
-        for t in range(LANES):
-            cols = slice(t * P, (t + 1) * P)
-            dw.append(bank("dw"))
-            nc.tensor.matmul_mx(dw[t][:], xm_q[:, cols].bitcast(E4M3), xm_s[:, cols], g_q[:].bitcast(E5M2), g_s[:], start=True, stop=True)
+
+        def products(k):
+            for e in range(2):
+                cols = slice(e * P, (e + 1) * P)
+                dw.append(bank("dw"))
+                nc.tensor.matmul_mx(dw[-1][:], xm_q[k][:, cols].bitcast(E4M3), xm_s[k][:, cols], g_q[:].bitcast(E5M2), g_s[:], start=True, stop=True)
+
+        products(0)
         parts = [slice(h * HALF, (h + 1) * HALF) for h in range(2)]
 
         def new_columns(t):
@@ -208,6 +211,9 @@ def tile_attend_gsig_pl_mom_kernel(tc, xT, wT, y, wt, xm, mT, offs, out_0, out_1
             scalar_scatter(w_new[0], nw, h)
         store_w(0)
         step = make_step(1)
+        xm_q.append(tile([P, D // 2], U32, "xm_q1", tag="m_src1"))
+        nc.vector.quantize_mx(xm_q[1][:].bitcast(E4M3), xm_s[1][:], xm_bf[1][:])
+        products(1)
         nc.vector.tensor_tensor(w_new[1][:].indirect(offsets[:]), w_g[:, 1, :], step[:], ADD)
         store_w(1)
         store_m(0)
@@ -217,7 +223,7 @@ def tile_attend_gsig_pl_mom_kernel(tc, xT, wT, y, wt, xm, mT, offs, out_0, out_1
         nm, nw = new_columns(2)
         for h in range(2):
             scalar_scatter(w_new[2], nw, h)
-        nc.scalar.activation(m_new[2][:, T // 2:], m_src[2][:, T // 2:], COPY)
+        nc.scalar.activation(m_new[2][:, 3 * T // 4:], m_src[2][:, 3 * T // 4:], COPY)
         step = make_step(3)
         nc.vector.tensor_tensor(w_new[3][:].indirect(offsets[:]), w_g[:, 3, :], step[:], ADD)
         store_w(3)
@@ -248,12 +254,15 @@ def tile_attend_gsig_pl_mom_kernel(tc, xT, wT, y, wt, xm, mT, offs, out_0, out_1
                     o_bf[c][:].bitcast(F32).rearrange("p (n u) -> p n u", u=2),
                     words[:, :, c * CHUNK:(c + 1) * CHUNK].rearrange("p u n -> p n u"),
                 )
-            if c > 0:
-                cols = slice((c - 1) * CHUNK, c * CHUNK)
-                nc.vector.quantize_mx(o_q[:, cols].bitcast(E4M3), o_s[:, cols], o_bf[c - 1][:])
-                if c > 1:
-                    done = slice(0 if c == 2 else (c - 1) * CHUNK, c * CHUNK)
-                    nc.sync.dma_start(words_hbm[:, done], o_q[:, done].bitcast(I32))
+        ends = [CHUNK, 2 * CHUNK, 3 * CHUNK, T - CHUNK // 2, T]
+        stored = 0
+        for k, end in enumerate(ends):
+            start = ends[k - 1] if k > 0 else 0
+            c = start // CHUNK
+            nc.vector.quantize_mx(o_q[:, start:end].bitcast(E4M3), o_s[:, start:end], o_bf[c][:, (start - c * CHUNK) * LANES:(end - c * CHUNK) * LANES])
+            if k in (1, 3, 4):
+                nc.sync.dma_start(words_hbm[:, stored:end], o_q[:, stored:end].bitcast(I32))
+                stored = end
         scales_hbm = out_3[0].bitcast(I32)
         for q in range(4):
             nc.sync.dma_start(scales_hbm[4 * q:4 * q + 4, :], o_s[32 * q:32 * q + 4, :].bitcast(I32))

@@ -203,7 +203,7 @@ def tile_attend_gsig_pl_mom_kernel(tc, xT, wT, y, wt, xm, mT, offs, out_0, out_1
             nc.sync.dma_start(o1_hbm[:, t, :], m_new[t][:])
 
         def pair_up(t):
-            nc.vector.tensor_copy(pairs[:, t // 2, :, t % 2], w_new[t][:])
+            nc.vector.tensor_copy(pairs[:, t, :], w_new[t][:])
 
         nm, nw = new_columns(0)
         for h in range(2):
@@ -237,32 +237,37 @@ def tile_attend_gsig_pl_mom_kernel(tc, xT, wT, y, wt, xm, mT, offs, out_0, out_1
         for h in range(2):
             scalar_scatter(m_new[3], step, h, -1.0 / LR)
         store_m(3)
-        pairs = late.tile([P, 2, T, 2], BF16, name="pairs", offset=0)
+        pairs = late.tile([P, LANES, T], BF16, name="pairs", offset=0)
         for t in (0, 1, 3, 2):
             pair_up(t)
 
         o_s = tile([P, T], U8, "o_s", tag="x_bf1")
         words_hbm = out_2[0].rearrange("p c l -> p (c l)").bitcast(I32)
         o_q = tile([P, T], U32, "o_q", tag="yw")
-        words = pairs[:].rearrange("p u c e -> p u (c e)").bitcast(F32)
-        o_bf = []
-        for c in range(CHUNKS + 1):
-            if c < CHUNKS:
-                o_bf.append(tile([P, CHUNK * LANES], BF16, "o_bf%d" % c, tag="w_src%d" % c))
-                weave = nc.scalar.copy if c % 2 == 1 else nc.vector.tensor_copy
-                weave(
-                    o_bf[c][:].bitcast(F32).rearrange("p (n u) -> p n u", u=2),
-                    words[:, :, c * CHUNK:(c + 1) * CHUNK].rearrange("p u n -> p n u"),
-                )
-        ends = [CHUNK, 2 * CHUNK, 3 * CHUNK, T - CHUNK // 2, T]
+        pieces = [(512, nc.vector.tensor_copy), (512, nc.vector.tensor_copy), (512, nc.scalar.copy), (256, nc.vector.tensor_copy), (256, nc.scalar.copy)]
+        waiting = []
         stored = 0
-        for k, end in enumerate(ends):
-            start = ends[k - 1] if k > 0 else 0
-            c = start // CHUNK
-            nc.vector.quantize_mx(o_q[:, start:end].bitcast(E4M3), o_s[:, start:end], o_bf[c][:, (start - c * CHUNK) * LANES:(end - c * CHUNK) * LANES])
-            if k in (1, 3, 4):
-                nc.sync.dma_start(words_hbm[:, stored:end], o_q[:, stored:end].bitcast(I32))
-                stored = end
+
+        def quantise(k, cols, o_bf):
+            nc.vector.quantize_mx(o_q[:, cols].bitcast(E4M3), o_s[:, cols], o_bf[:])
+
+        start = 0
+        for k, (width, weave) in enumerate(pieces):
+            cols = slice(start, start + width)
+            o_bf = tile([P, width * LANES], BF16, "o_bf%d" % k, tag=["w_src0", "w_src1", "w_src2", "w_src3", "m_src0"][k])
+            weave(
+                o_bf[:].rearrange("p (c i t) -> p c t i", i=4, t=LANES),
+                pairs[:, :, cols].rearrange("p t (c i) -> p c t i", i=4),
+            )
+            waiting.append((k, cols, o_bf))
+            if k == 1:
+                quantise(*waiting[0])
+            start = start + width
+        for k, cols, o_bf in waiting[1:]:
+            quantise(k, cols, o_bf)
+            if k != 2:
+                nc.sync.dma_start(words_hbm[:, stored:cols.stop], o_q[:, stored:cols.stop].bitcast(I32))
+                stored = cols.stop
         scales_hbm = out_3[0].bitcast(I32)
         for q in range(4):
             nc.sync.dma_start(scales_hbm[4 * q:4 * q + 4, :], o_s[32 * q:32 * q + 4, :].bitcast(I32))

@@ -1,4 +1,5 @@
 from contextlib import ExitStack
+from itertools import product as product_of
 
 import concourse.mybir as mybir
 
@@ -25,6 +26,7 @@ FLOPS = 2 * 2 * D * R * N
 HALF = N // 2
 CHUNKS = 4
 CHUNK = T // CHUNKS
+KIB = 1024
 
 
 def tile_attend_gsig_pl_mom_kernel(tc, xT, wT, y, wt, xm, mT, offs, out_0, out_1, out_2, out_3):
@@ -44,8 +46,10 @@ def tile_attend_gsig_pl_mom_kernel(tc, xT, wT, y, wt, xm, mT, offs, out_0, out_1
             return table.rearrange("(p t) c -> p t c", t=LANES)
 
         w_hbm, m_hbm, o0_hbm, o1_hbm = planes(wT), planes(mT), planes(out_0), planes(out_1)
+        parts = [slice(h * HALF, (h + 1) * HALF) for h in range(2)]
 
         offsets = sb.tile([P, N // 16], U16, name="offsets")
+        halves = [offsets[:, h * (HALF // 16):(h + 1) * (HALF // 16)] for h in range(2)]
         wt_sb = tile([P, LANES], F32, "wt_sb")
         w_src = [tile([P, T], F32, "w_src%d" % t) for t in range(LANES)]
         for t in range(LANES):
@@ -57,45 +61,46 @@ def tile_attend_gsig_pl_mom_kernel(tc, xT, wT, y, wt, xm, mT, offs, out_0, out_1
         x_raw = [tile([P, LANES, R // 4], F32, "x_raw%d" % h) for h in range(4)]
         for h in range(4):
             nc.sync.dma_start(x_raw[h][:], x_hbm[:, :, h * (R // 4):(h + 1) * (R // 4)])
-        y_sb = [[tile([P, 2, HALF], F32, "y_sb%d%d" % (h, k)) for k in range(2)] for h in range(2)]
-        xm_raw = tile([P, LANES, D], F32, "xm_raw")
+        y_sb = [tile([P, LANES, HALF], F32, "y_sb%d" % h) for h in range(2)]
         for h in range(2):
-            for k in range(2):
-                nc.sync.dma_start(y_sb[h][k][:], planes(y[0])[:, 2 * k:2 * k + 2, h * HALF:(h + 1) * HALF])
+            nc.sync.dma_start(y_sb[h][:], planes(y[0])[:, :, parts[h]])
+        xm_raw = tile([P, LANES, D], F32, "xm_raw")
         nc.sync.dma_start(xm_raw[:], planes(xm[0]))
         m_src = [tile([P, T], F32, "m_src%d" % t) for t in range(LANES)]
         w_new = [tile([P, T], F32, "w_new%d" % t) for t in range(LANES - 1)]
-        m_new = [tile([P, T], F32, "m_new%d" % t) for t in range(LANES)]
+        m_new = {1: tile([P, T], F32, "m_new1")}
         for t in range(LANES):
             nc.sync.dma_start(m_src[t][:], m_hbm[:, t, :])
             if t == 1:
                 nc.sync.dma_start(m_new[1][:], m_hbm[:, 1, :])
-        nc.sync.dma_start(m_new[2][:, :3 * T // 4], m_hbm[:, 2, :3 * T // 4])
+        m_win = [m_src[t][:] for t in range(LANES)]
 
         warm = tile([P, 1], F32, "warm")
         nc.gpsimd.memset(warm[:], 0.0)
         nc.scalar.activation(warm[:], warm[:], SIGMOID)
 
-        w_g = late.tile([P, LANES, N], F32, name="w_g", offset=0)
+        pairs = late.tile([P, 4 * T], BF16, name="pairs", offset=0)
+        w_g = [tile([P, 2, N], F32, "w_g0")[:], pairs[:, 2 * T:2 * T + 4 * N].bitcast(F32).rearrange("p (e c) -> p e c", e=2)]
         w_bf = [tile([P, HALF * LANES], BF16, "w_bf%d" % h) for h in range(2)]
         w_view = [w_bf[h][:].rearrange("p (c t) -> p c t", t=LANES) for h in range(2)]
+
+        def round_pair(k, h):
+            nc.vector.tensor_copy(w_view[h][:, :, 2 * k:2 * k + 2], w_g[k][:, :, parts[h]].rearrange("p t c -> p c t"))
+
         for t in range(LANES - 1):
-            nc.vector.tensor_copy(w_g[:, t, :], w_src[t][:].indirect(offsets[:]))
+            nc.vector.tensor_copy(w_g[t // 2][:, t % 2, :], w_src[t][:].indirect(offsets[:]))
             if t == 1:
                 for h in range(2):
-                    nc.vector.tensor_copy(w_view[h][:, :, 0:2], w_g[:, 0:2, h * HALF:(h + 1) * HALF].rearrange("p t c -> p c t"))
-        for h in range(2):
-            nc.vector.tensor_copy(w_g[:, 3, h * HALF:(h + 1) * HALF], w_src[3][:].indirect(offsets[:, h * (HALF // 16):(h + 1) * (HALF // 16)]))
-        for h in range(2):
-            slots = slice(h * HALF, (h + 1) * HALF)
-            nc.vector.tensor_copy(w_view[h][:, :, 2:4], w_g[:, 2:4, slots].rearrange("p t c -> p c t"))
-        for t in range(LANES - 1):
+                    round_pair(0, h)
             nc.scalar.activation(w_new[t][:], w_src[t][:], COPY)
+        for h in range(2):
+            nc.vector.tensor_copy(w_g[1][:, 1, parts[h]], w_src[3][:].indirect(halves[h]))
         w_q = tile([P, N], U32, "w_q")
         w_s = tile([P, N], U8, "w_s")
         for h in range(2):
-            slots = slice(h * HALF, (h + 1) * HALF)
-            nc.vector.quantize_mx(w_q[:, slots].bitcast(E4M3), w_s[:, slots], w_bf[h][:])
+            round_pair(1, h)
+        for h in range(2):
+            nc.vector.quantize_mx(w_q[:, parts[h]].bitcast(E4M3), w_s[:, parts[h]], w_bf[h][:])
 
         x_bf = [tile([P, R * 2], BF16, "x_bf%d" % k) for k in range(2)]
         for h in range(4):
@@ -105,7 +110,7 @@ def tile_attend_gsig_pl_mom_kernel(tc, xT, wT, y, wt, xm, mT, offs, out_0, out_1
                     x_raw[h][:].rearrange("p j (m t) -> p m j t", t=LANES)[:, :, :, 2 * k:2 * k + 2],
                 )
         w_new.append(tile([P, T], F32, "w_new3", tag="x_raw3"))
-        nc.scalar.activation(w_new[3][:, :3 * T // 4], w_src[3][:, :3 * T // 4], COPY)
+        nc.scalar.activation(w_new[3][:, :T // 2], w_src[3][:, :T // 2], COPY)
         x_q = tile([P, R], U32, "x_q")
         x_s = tile([P, R], U8, "x_s")
         for t in range(2):
@@ -113,85 +118,55 @@ def tile_attend_gsig_pl_mom_kernel(tc, xT, wT, y, wt, xm, mT, offs, out_0, out_1
             nc.vector.quantize_mx(x_q[:, cols].bitcast(E4M3), x_s[:, cols], x_bf[0][:, t * LANES * P:(t + 1) * LANES * P])
         nc.vector.quantize_mx(x_q[:, 2 * P:].bitcast(E4M3), x_s[:, 2 * P:], x_bf[1][:])
 
+        nc.vector.tensor_copy(w_new[3][:, T // 2:], w_src[3][:, T // 2:])
+
         sig = [tile([P, LANES, HALF], F32, "sig%d" % h) for h in range(2)]
-        yw = tile([P, LANES, N], F32, "yw")
+        yw = [tile([P, LANES, HALF], F32, "yw%d" % h) for h in range(2)]
         wt_neg = tile([P, LANES], F32, "wt_neg")
         nc.gpsimd.tensor_scalar(wt_neg[:], wt_sb[:], -1.0, 0.0, MULT, ADD)
+        for h, t in product_of(range(2), range(LANES)):
+            nc.gpsimd.tensor_scalar(yw[h][:, t, :], y_sb[h][:, t, :], wt_neg[:, t:t + 1], 0.0, MULT, ADD)
         for h in range(2):
-            slots = slice(h * HALF, (h + 1) * HALF)
-            for t in range(LANES):
-                engine = nc.vector if h == 0 and t < 2 else nc.gpsimd
-                engine.tensor_scalar(yw[:, t, slots], y_sb[h][t // 2][:, t % 2, :], wt_neg[:, t:t + 1], 0.0, MULT, ADD)
-        for h in range(2):
-            slots = slice(h * HALF, (h + 1) * HALF)
             for k in range(2):
-                z = tile([P, 2, HALF], F32, "z%d%d" % (h, k), tag=["x_bf1", "nm0", "step1", "xm_bf0"][2 * h + k])
-                count = 1 if h == k else 2
-                for e0 in range(0, 2, count):
-                    a = bank("a")
-                    for e in range(count):
-                        cols = slice((2 * k + e0 + e) * P, (2 * k + e0 + e + 1) * P)
-                        nc.tensor.matmul_mx(a[:, e * HALF:(e + 1) * HALF], x_q[:, cols].bitcast(E4M3), x_s[:, cols], w_q[:, slots].bitcast(E4M3), w_s[:, slots], start=True, stop=True)
-                    nc.vector.tensor_tensor(z[:, e0:e0 + count, :], a[:, :count * HALF].rearrange("p (e n) -> p e n", e=count), y_sb[h][k][:, e0:e0 + count, :], MULT)
+                z = tile([P, 2, HALF], F32, "z%d%d" % (h, k)) if h + k < 2 else late.tile([P, 2, HALF], F32, name="z11", offset=22 * KIB)
+                a = bank("a")
+                for e in range(2):
+                    cols = slice((2 * k + e) * P, (2 * k + e + 1) * P)
+                    nc.tensor.matmul_mx(a[:, e * HALF:(e + 1) * HALF], x_q[:, cols].bitcast(E4M3), x_s[:, cols], w_q[:, parts[h]].bitcast(E4M3), w_s[:, parts[h]], start=True, stop=True)
+                nc.vector.tensor_tensor(z[:], a[:].rearrange("p (e n) -> p e n", e=2), y_sb[h][:, 2 * k:2 * k + 2, :], MULT)
                 nc.scalar.activation(sig[h][:, 2 * k:2 * k + 2, :], z[:], SIGMOID, scale=-1.0)
 
-        nc.vector.tensor_copy(w_new[3][:, 3 * T // 4:], w_src[3][:, 3 * T // 4:])
         xm_cols = xm_raw[:].rearrange("p j (m t) -> p m j t", t=LANES)
-        xm_bf = [tile([P, D * 2], BF16, "xm_bf0")]
-        nc.scalar.copy(xm_bf[0][:].rearrange("p (t m j) -> p m j t", t=2, j=LANES), xm_cols[:, :, :, 0:2])
-        g_bf = tile([P, N * LANES], BF16, "g_bf")
-        for h in range(2):
-            slots = slice(h * HALF, (h + 1) * HALF)
-            nc.vector.tensor_tensor(
-                g_bf[:, h * HALF * LANES:(h + 1) * HALF * LANES].rearrange("p (c i t) -> p c t i", i=4, t=LANES),
-                sig[h][:].rearrange("p t (c i) -> p c t i", i=4),
-                yw[:, :, slots].rearrange("p t (c i) -> p c t i", i=4),
-                MULT,
-            )
-        xm_bf.append(tile([P, D * 2], BF16, "xm_bf1", tag="sig0"))
-        nc.scalar.copy(xm_bf[1][:].rearrange("p (t m j) -> p m j t", t=2, j=LANES), xm_cols[:, :, :, 2:4])
-        xm_q = [tile([P, D // 2], U32, "xm_q0")]
-        xm_s = [tile([P, D // 2], U8, "xm_s%d" % k) for k in range(2)]
+        xm_bf = {}
+        xm_q = tile([P, D], U32, "xm_q")
+        xm_s = tile([P, D], U8, "xm_s")
+        g_bf = {}
         g_q = tile([P, N], U32, "g_q")
         g_s = tile([P, N], U8, "g_s")
-        halves = [offsets[:, h * (HALF // 16):(h + 1) * (HALF // 16)] for h in range(2)]
-        nc.vector.quantize_mx(g_q[:, :HALF].bitcast(E5M2), g_s[:, :HALF], g_bf[:, :HALF * LANES])
-        nc.vector.quantize_mx(xm_q[0][:, :P].bitcast(E4M3), xm_s[0][:, :P], xm_bf[0][:, :LANES * P])
-        nc.vector.quantize_mx(g_q[:, HALF:].bitcast(E5M2), g_s[:, HALF:], g_bf[:, HALF * LANES:])
-        nc.vector.quantize_mx(xm_q[0][:, P:].bitcast(E4M3), xm_s[0][:, P:], xm_bf[0][:, LANES * P:])
 
-        nc.scalar.activation(m_new[0][:], m_src[0][:], COPY)
+        def round_xm(first, count, copy):
+            copy(xm_bf[first][:].rearrange("p (t m j) -> p m j t", t=count, j=LANES), xm_cols[:, :, :, first:first + count])
 
-        dw = []
+        def make_g(h):
+            g_bf[h] = tile([P, HALF * LANES], BF16, "g_bf%d" % h, tag="g_bf")
+            nc.vector.tensor_tensor(
+                g_bf[h][:].rearrange("p (c i t) -> p c t i", i=4, t=LANES),
+                sig[h][:].rearrange("p t (c i) -> p c t i", i=4),
+                yw[h][:].rearrange("p t (c i) -> p c t i", i=4),
+                MULT,
+            )
 
-        def products(k):
-            for e in range(2):
-                cols = slice(e * P, (e + 1) * P)
-                dw.append(bank("dw"))
-                nc.tensor.matmul_mx(dw[-1][:], xm_q[k][:, cols].bitcast(E4M3), xm_s[k][:, cols], g_q[:].bitcast(E5M2), g_s[:], start=True, stop=True)
+        def quantise_g(h):
+            nc.vector.quantize_mx(g_q[:, parts[h]].bitcast(E5M2), g_s[:, parts[h]], g_bf[h][:])
 
-        products(0)
-        parts = [slice(h * HALF, (h + 1) * HALF) for h in range(2)]
+        def quantise_xm(first, count):
+            cols = slice(first * P, (first + count) * P)
+            nc.vector.quantize_mx(xm_q[:, cols].bitcast(E4M3), xm_s[:, cols], xm_bf[first][:])
 
-        def new_columns(t):
-            m_g = tile([P, N], F32, "m_g%d" % t)
-            nm = tile([P, N], F32, "nm%d" % t)
-            nw = tile([P, N], F32, "nw%d" % t)
-            for h in range(2):
-                nc.vector.tensor_copy(m_g[:, parts[h]], m_src[t][:].indirect(halves[h]))
-            for h in range(2):
-                nc.vector.scalar_tensor_tensor(nm[:, parts[h]], m_g[:, parts[h]], BETA, dw[t][:, parts[h]], MULT, ADD)
-            for h in range(2):
-                nc.vector.scalar_tensor_tensor(nw[:, parts[h]], nm[:, parts[h]], -LR, w_g[:, t, parts[h]], MULT, ADD)
-            return nm, nw
-
-        def make_step(t):
-            m_g = tile([P, N], F32, "m_g%d" % t)
-            step = tile([P, N], F32, "step%d" % t)
-            nc.vector.tensor_scalar(m_g[:], m_src[t][:].indirect(offsets[:]), -LR * BETA, 0.0, MULT, ADD)
-            for h in (1, 0):
-                nc.vector.scalar_tensor_tensor(step[:, parts[h]], dw[t][:, parts[h]], -LR, m_g[:, parts[h]], MULT, ADD)
-            return step
+        def product(t, slots, dw):
+            cols = slice(t * P, (t + 1) * P)
+            nc.tensor.matmul_mx(dw[:, slots], xm_q[:, cols].bitcast(E4M3), xm_s[:, cols], g_q[:, slots].bitcast(E5M2), g_s[:, slots], start=True, stop=True)
+            return dw[:, slots]
 
         def scalar_scatter(window, values, h, scale=1.0):
             nc.scalar.activation(window[:].indirect(halves[h]), values[:, parts[h]], COPY, scale=scale)
@@ -202,72 +177,124 @@ def tile_attend_gsig_pl_mom_kernel(tc, xT, wT, y, wt, xm, mT, offs, out_0, out_1
         def store_m(t):
             nc.sync.dma_start(o1_hbm[:, t, :], m_new[t][:])
 
-        def pair_up(t):
-            nc.vector.tensor_copy(pairs[:, t, :], w_new[t][:])
+        def new_m(t, m_g, nm, dw, h):
+            nc.vector.scalar_tensor_tensor(nm[:, parts[h]], m_g[:, parts[h]], BETA, dw, MULT, ADD)
 
-        nm, nw = new_columns(0)
+        def new_w(t, nm, nw, h):
+            nc.vector.scalar_tensor_tensor(nw[:, parts[h]], nm[:, parts[h]], -LR, w_g[t // 2][:, t % 2, parts[h]], MULT, ADD)
+
+        xm_bf[1] = late.tile([P, 3 * LANES * P], BF16, name="xm_bf1", offset=20 * KIB, align_bytes=64)
+        round_xm(1, 3, nc.scalar.copy)
+        m_g = late.tile([P, N], F32, name="m_g0", offset=23 * KIB)
+        nm = {0: tile([P, N], F32, "nm0")}
+        nw = {0: tile([P, N], F32, "nw0")}
+        first = bank("dw")
         for h in range(2):
-            scalar_scatter(m_new[0], nm, h)
-            scalar_scatter(w_new[0], nw, h)
+            make_g(h)
+            if h == 0:
+                xm_bf[0] = tile([P, LANES * P], BF16, "xm_bf0", tag="w_q")
+                round_xm(0, 1, nc.vector.tensor_copy)
+            quantise_g(h)
+            if h == 0:
+                quantise_xm(0, 1)
+            dw = product(0, parts[h], first)
+            nc.scalar.activation(m_g[:, parts[h]], m_win[0].indirect(halves[h]), COPY)
+            new_m(0, m_g, nm[0], dw, h)
+            new_w(0, nm[0], nw[0], h)
+            scalar_scatter(w_new[0], nw[0], h)
+        quantise_xm(1, 3)
+        m_new[0] = late.tile([P, T], F32, name="m_new0", offset=16 * KIB)
+        nc.vector.tensor_copy(m_new[0][:], m_win[0])
+        for h in range(2):
+            scalar_scatter(m_new[0], nm[0], h)
         store_w(0)
-        step = make_step(1)
-        xm_q.append(tile([P, D // 2], U32, "xm_q1", tag="m_src1"))
-        nc.vector.quantize_mx(xm_q[1][:].bitcast(E4M3), xm_s[1][:], xm_bf[1][:])
-        products(1)
-        nc.vector.tensor_tensor(w_new[1][:].indirect(offsets[:]), w_g[:, 1, :], step[:], ADD)
-        store_w(1)
         store_m(0)
+
+        def place(t):
+            return pairs[:, t // 2 * 2 * T:(t // 2 + 1) * 2 * T].rearrange("p (c e) -> p c e", e=2)[:, :, t % 2]
+
+        def round_plane(t):
+            for c in range(CHUNKS):
+                cols = slice(c * CHUNK, (c + 1) * CHUNK)
+                nc.gpsimd.tensor_scalar(place(t)[:, cols], w_new[t][:, cols], 1.0, -0.0, MULT, ADD)
+
+        def gather_m(t, m_g, h):
+            nc.vector.tensor_copy(m_g[:, parts[h]], m_win[t].indirect(halves[h]))
+
+        def new_columns(t, m_g, tags):
+            nm[t] = tile([P, N], F32, "nm%d" % t, tag=tags[0])
+            nw[t] = tile([P, N], F32, "nw%d" % t, tag=tags[1])
+            dw = product(t, slice(0, N), bank("dw"))
+            for h in range(2):
+                new_m(t, m_g, nm[t], dw[:, parts[h]], h)
+            for h in range(2):
+                new_w(t, nm[t], nw[t], h)
+
+        round_plane(0)
+        m_g = late.tile([P, T], F32, name="m_g1", offset=24 * KIB)
         for h in range(2):
-            scalar_scatter(m_new[1], step, h, -1.0 / LR)
+            gather_m(1, m_g, h)
+        new_columns(1, m_g, (None, None))
+        m_g = late.tile([P, N], F32, name="m_g2", offset=31 * KIB)
+        gather_m(2, m_g, 0)
+        nc.vector.tensor_copy(w_new[1][:].indirect(offsets[:]), nw[1][:])
+        store_w(1)
+        round_plane(1)
+        for h in range(2):
+            scalar_scatter(m_new[1], nm[1], h)
         store_m(1)
-        nm, nw = new_columns(2)
+        gather_m(2, m_g, 1)
+        new_columns(2, m_g, ("z00", "sig0"))
         for h in range(2):
-            scalar_scatter(w_new[2], nw, h)
-        nc.scalar.activation(m_new[2][:, 3 * T // 4:], m_src[2][:, 3 * T // 4:], COPY)
-        step = make_step(3)
-        nc.vector.tensor_tensor(w_new[3][:].indirect(offsets[:]), w_g[:, 3, :], step[:], ADD)
-        store_w(3)
+            scalar_scatter(w_new[2], nw[2], h)
         store_w(2)
+        m_new[2] = late.tile([P, T], F32, name="m_new2", offset=32 * KIB)
+        nc.vector.tensor_copy(m_new[2][:], m_win[2])
         for h in range(2):
-            scalar_scatter(m_new[2], nm, h)
+            scalar_scatter(m_new[2], nm[2], h)
         store_m(2)
+        m_g = late.tile([P, N], F32, name="m_g3", offset=30 * KIB)
         for h in range(2):
-            cols = slice(h * (T // 2), (h + 1) * (T // 2))
-            nc.vector.tensor_copy(m_new[3][:, cols], m_src[3][:, cols])
+            gather_m(3, m_g, h)
+        new_columns(3, m_g, ("z10", "sig1"))
+        m_new[3] = late.tile([P, T], F32, name="m_new3", offset=24 * KIB)
+        nc.vector.tensor_copy(m_new[3][:], m_win[3])
+        nc.vector.tensor_copy(w_new[3][:].indirect(offsets[:]), nw[3][:])
         for h in range(2):
-            scalar_scatter(m_new[3], step, h, -1.0 / LR)
-        store_m(3)
-        pairs = late.tile([P, LANES, T], BF16, name="pairs", offset=0)
-        for t in (0, 1, 3, 2):
-            pair_up(t)
+            scalar_scatter(m_new[3], nm[3], h)
+        store_w(3)
+        for t in (2, 3):
+            nc.vector.tensor_copy(place(t), w_new[t][:])
 
-        o_s = tile([P, T], U8, "o_s", tag="x_bf1")
+        words = pairs[:].bitcast(U32).rearrange("p (u c) -> p u c", u=2)
+        o_s = tile([P, T], U8, "o_s")
+        o_q = tile([P, T], U32, "o_q", tag="xm_raw")
         words_hbm = out_2[0].rearrange("p c l -> p (c l)").bitcast(I32)
-        o_q = tile([P, T], U32, "o_q", tag="yw")
-        pieces = [(512, nc.vector.tensor_copy), (512, nc.vector.tensor_copy), (512, nc.scalar.copy), (256, nc.vector.tensor_copy), (256, nc.scalar.copy)]
-        waiting = []
-        stored = 0
+        o_bf = [tile([P, CHUNK * LANES], BF16, "o_bf%d" % c, tag="w_src%d" % c) for c in range(CHUNKS)]
 
-        def quantise(k, cols, o_bf):
-            nc.vector.quantize_mx(o_q[:, cols].bitcast(E4M3), o_s[:, cols], o_bf[:])
-
-        start = 0
-        for k, (width, weave) in enumerate(pieces):
-            cols = slice(start, start + width)
-            o_bf = tile([P, width * LANES], BF16, "o_bf%d" % k, tag=["w_src0", "w_src1", "w_src2", "w_src3", "m_src0"][k])
-            weave(
-                o_bf[:].rearrange("p (c i t) -> p c t i", i=4, t=LANES),
-                pairs[:, :, cols].rearrange("p t (c i) -> p c t i", i=4),
+        def weave(c):
+            (nc.vector.tensor_copy if c < 2 else nc.scalar.copy)(
+                o_bf[c][:].bitcast(U32).rearrange("p (c u) -> p c u", u=2),
+                words[:, :, c * CHUNK:(c + 1) * CHUNK].rearrange("p u c -> p c u"),
             )
-            waiting.append((k, cols, o_bf))
-            if k == 1:
-                quantise(*waiting[0])
-            start = start + width
-        for k, cols, o_bf in waiting[1:]:
-            quantise(k, cols, o_bf)
-            if k != 2:
-                nc.sync.dma_start(words_hbm[:, stored:cols.stop], o_q[:, stored:cols.stop].bitcast(I32))
-                stored = cols.stop
+
+        def quantise(c):
+            cols = slice(c * CHUNK, (c + 1) * CHUNK)
+            nc.vector.quantize_mx(o_q[:, cols].bitcast(E4M3), o_s[:, cols], o_bf[c][:])
+
+        def store_words(first, last):
+            cols = slice(first * CHUNK, last * CHUNK)
+            nc.sync.dma_start(words_hbm[:, cols], o_q[:, cols].bitcast(I32))
+
+        weave(0)
+        for c in range(CHUNKS):
+            if c + 1 < CHUNKS:
+                weave(c + 1)
+            quantise(c)
+        store_m(3)
+        store_words(0, 2)
+        store_words(2, 3)
+        store_words(3, 4)
         scales_hbm = out_3[0].bitcast(I32)
         for q in range(4):
             nc.sync.dma_start(scales_hbm[4 * q:4 * q + 4, :], o_s[32 * q:32 * q + 4, :].bitcast(I32))

@@ -27,6 +27,7 @@ HALF = N // 2
 CHUNKS = 4
 CHUNK = T // CHUNKS
 KIB = 1024
+SPLIT = 3 * T // 4
 
 
 def tile_attend_gsig_pl_mom_kernel(tc, xT, wT, y, wt, xm, mT, offs, out_0, out_1, out_2, out_3):
@@ -40,7 +41,7 @@ def tile_attend_gsig_pl_mom_kernel(tc, xT, wT, y, wt, xm, mT, offs, out_0, out_1
             return sb.tile(shape, dtype, name=name, tag=tag or name, align_bytes=64)
 
         def bank(name):
-            return ps.tile([P, 512], F32, name=name, tag="bank")
+            return ps.tile([P, 512], F32, name=name, tag=name, bufs=4 if name == "a" else 1)
 
         def planes(table):
             return table.rearrange("(p t) c -> p t c", t=LANES)
@@ -68,11 +69,13 @@ def tile_attend_gsig_pl_mom_kernel(tc, xT, wT, y, wt, xm, mT, offs, out_0, out_1
         nc.sync.dma_start(xm_raw[:], planes(xm[0]))
         m_src = [tile([P, T], F32, "m_src%d" % t) for t in range(LANES)]
         w_new = [tile([P, T], F32, "w_new%d" % t) for t in range(LANES - 1)]
-        m_new = {1: tile([P, T], F32, "m_new1")}
+        m_new = {t: tile([P, T], F32, "m_new%d" % t) for t in (1, 2)}
         for t in range(LANES):
             nc.sync.dma_start(m_src[t][:], m_hbm[:, t, :])
             if t == 1:
-                nc.sync.dma_start(m_new[1][:], m_hbm[:, 1, :])
+                nc.sync.dma_start(m_new[1][:, :SPLIT], m_hbm[:, 1, :SPLIT])
+            if t == 2:
+                nc.sync.dma_start(m_new[2][:], m_hbm[:, 2, :])
         m_win = [m_src[t][:] for t in range(LANES)]
 
         warm = tile([P, 1], F32, "warm")
@@ -80,7 +83,7 @@ def tile_attend_gsig_pl_mom_kernel(tc, xT, wT, y, wt, xm, mT, offs, out_0, out_1
         nc.scalar.activation(warm[:], warm[:], SIGMOID)
 
         pairs = late.tile([P, 4 * T], BF16, name="pairs", offset=0)
-        w_g = [tile([P, 2, N], F32, "w_g0")[:], pairs[:, 2 * T:2 * T + 4 * N].bitcast(F32).rearrange("p (e c) -> p e c", e=2)]
+        w_g = [pairs[:, k * 2 * T:k * 2 * T + 4 * N].bitcast(F32).rearrange("p (e c) -> p e c", e=2) for k in range(2)]
         w_bf = [tile([P, HALF * LANES], BF16, "w_bf%d" % h) for h in range(2)]
         w_view = [w_bf[h][:].rearrange("p (c t) -> p c t", t=LANES) for h in range(2)]
 
@@ -128,7 +131,7 @@ def tile_attend_gsig_pl_mom_kernel(tc, xT, wT, y, wt, xm, mT, offs, out_0, out_1
             nc.gpsimd.tensor_scalar(yw[h][:, t, :], y_sb[h][:, t, :], wt_neg[:, t:t + 1], 0.0, MULT, ADD)
         for h in range(2):
             for k in range(2):
-                z = tile([P, 2, HALF], F32, "z%d%d" % (h, k)) if h + k < 2 else late.tile([P, 2, HALF], F32, name="z11", offset=22 * KIB)
+                z = tile([P, 2, HALF], F32, "z%d%d" % (h, k)) if h + k < 2 else late.tile([P, 14, P], F32, name="z11", offset=17 * KIB)[:, :4, :].rearrange("p (e a) b -> p e (a b)", e=2)
                 a = bank("a")
                 for e in range(2):
                     cols = slice((2 * k + e) * P, (2 * k + e + 1) * P)
@@ -148,7 +151,7 @@ def tile_attend_gsig_pl_mom_kernel(tc, xT, wT, y, wt, xm, mT, offs, out_0, out_1
             copy(xm_bf[first][:].rearrange("p (t m j) -> p m j t", t=count, j=LANES), xm_cols[:, :, :, first:first + count])
 
         def make_g(h):
-            g_bf[h] = tile([P, HALF * LANES], BF16, "g_bf%d" % h, tag="g_bf")
+            g_bf[h] = tile([P, HALF * LANES], BF16, "g_bf%d" % h)
             nc.vector.tensor_tensor(
                 g_bf[h][:].rearrange("p (c i t) -> p c t i", i=4, t=LANES),
                 sig[h][:].rearrange("p t (c i) -> p c t i", i=4),
@@ -178,33 +181,35 @@ def tile_attend_gsig_pl_mom_kernel(tc, xT, wT, y, wt, xm, mT, offs, out_0, out_1
             nc.sync.dma_start(o1_hbm[:, t, :], m_new[t][:])
 
         def new_m(t, m_g, nm, dw, h):
-            nc.vector.scalar_tensor_tensor(nm[:, parts[h]], m_g[:, parts[h]], BETA, dw, MULT, ADD)
+            nc.vector.scalar_tensor_tensor(nm[:, parts[h]], m_g, BETA, dw, MULT, ADD)
 
         def new_w(t, nm, nw, h):
             nc.vector.scalar_tensor_tensor(nw[:, parts[h]], nm[:, parts[h]], -LR, w_g[t // 2][:, t % 2, parts[h]], MULT, ADD)
 
-        xm_bf[1] = late.tile([P, 3 * LANES * P], BF16, name="xm_bf1", offset=20 * KIB, align_bytes=64)
-        round_xm(1, 3, nc.scalar.copy)
+        xm_bf[0] = late.tile([P, LANES * P], BF16, name="xm_bf0", offset=17 * KIB, align_bytes=64)
+        round_xm(0, 1, nc.scalar.copy)
         m_g = late.tile([P, N], F32, name="m_g0", offset=23 * KIB)
         nm = {0: tile([P, N], F32, "nm0")}
         nw = {0: tile([P, N], F32, "nw0")}
-        first = bank("dw")
         for h in range(2):
             make_g(h)
-            if h == 0:
-                xm_bf[0] = tile([P, LANES * P], BF16, "xm_bf0", tag="w_q")
-                round_xm(0, 1, nc.vector.tensor_copy)
+        dw = []
+        for h in range(2):
             quantise_g(h)
             if h == 0:
                 quantise_xm(0, 1)
-            dw = product(0, parts[h], first)
+            dw.append(product(0, parts[h], bank(("dw", "dw3")[h])))
             nc.scalar.activation(m_g[:, parts[h]], m_win[0].indirect(halves[h]), COPY)
-            new_m(0, m_g, nm[0], dw, h)
+        for h in range(2):
+            new_m(0, m_g[:, parts[h]], nm[0], dw[h], h)
+        for h in range(2):
             new_w(0, nm[0], nw[0], h)
             scalar_scatter(w_new[0], nw[0], h)
-        quantise_xm(1, 3)
+        xm_bf[1] = late.tile([P, 3 * LANES * P], BF16, name="xm_bf1", offset=24 * KIB, align_bytes=64)
+        round_xm(1, 3, nc.vector.tensor_copy)
         m_new[0] = late.tile([P, T], F32, name="m_new0", offset=16 * KIB)
         nc.vector.tensor_copy(m_new[0][:], m_win[0])
+        quantise_xm(1, 3)
         for h in range(2):
             scalar_scatter(m_new[0], nm[0], h)
         store_w(0)
@@ -214,56 +219,64 @@ def tile_attend_gsig_pl_mom_kernel(tc, xT, wT, y, wt, xm, mT, offs, out_0, out_1
             return pairs[:, t // 2 * 2 * T:(t // 2 + 1) * 2 * T].rearrange("p (c e) -> p c e", e=2)[:, :, t % 2]
 
         def round_plane(t):
-            for c in range(CHUNKS):
-                cols = slice(c * CHUNK, (c + 1) * CHUNK)
-                nc.gpsimd.tensor_scalar(place(t)[:, cols], w_new[t][:, cols], 1.0, -0.0, MULT, ADD)
+            nc.gpsimd.tensor_scalar(place(t), w_new[t][:], 1.0, -0.0, MULT, ADD)
 
         def gather_m(t, m_g, h):
-            nc.vector.tensor_copy(m_g[:, parts[h]], m_win[t].indirect(halves[h]))
+            nc.vector.tensor_copy(m_g[h], m_win[t].indirect(halves[h]))
 
-        def new_columns(t, m_g, tags):
-            nm[t] = tile([P, N], F32, "nm%d" % t, tag=tags[0])
-            nw[t] = tile([P, N], F32, "nw%d" % t, tag=tags[1])
-            dw = product(t, slice(0, N), bank("dw"))
+        def halved(columns):
+            return [columns[:, parts[h]] for h in range(2)]
+
+        def momentum(t, m_g, dw, tag):
+            nm[t] = tile([P, N], F32, "nm%d" % t, tag=tag)
+            product(t, slice(0, N), dw)
             for h in range(2):
-                new_m(t, m_g, nm[t], dw[:, parts[h]], h)
+                new_m(t, m_g[h], nm[t], dw[:, parts[h]], h)
+
+        def weights(t, columns):
+            nw[t] = columns
             for h in range(2):
                 new_w(t, nm[t], nw[t], h)
 
-        round_plane(0)
-        m_g = late.tile([P, T], F32, name="m_g1", offset=24 * KIB)
+        m_g = halved(late.tile([P, 6 * N], F32, name="m_g1", offset=24 * KIB))
         for h in range(2):
             gather_m(1, m_g, h)
-        new_columns(1, m_g, (None, None))
-        m_g = late.tile([P, N], F32, name="m_g2", offset=31 * KIB)
-        gather_m(2, m_g, 0)
+        momentum(1, m_g, bank("dw"), None)
+        nc.vector.tensor_copy(m_new[1][:, SPLIT:], m_src[1][:, SPLIT:])
+        weights(1, tile([P, N], F32, "nw1"))
+        round_plane(0)
+        m_g2 = [late.tile([P, HALF], F32, name="m_g2", offset=33 * KIB)[:]]
+        gather_m(2, m_g2, 0)
         nc.vector.tensor_copy(w_new[1][:].indirect(offsets[:]), nw[1][:])
         store_w(1)
         round_plane(1)
         for h in range(2):
             scalar_scatter(m_new[1], nm[1], h)
         store_m(1)
-        gather_m(2, m_g, 1)
-        new_columns(2, m_g, ("z00", "sig0"))
-        for h in range(2):
-            scalar_scatter(w_new[2], nw[2], h)
-        store_w(2)
-        m_new[2] = late.tile([P, T], F32, name="m_new2", offset=32 * KIB)
-        nc.vector.tensor_copy(m_new[2][:], m_win[2])
+        m_g2.append(tile([P, HALF], F32, "later", tag="nw1")[:])
+        m_g3 = late.tile([P, N], F32, name="m_g3", offset=33 * KIB)
+        gather_m(2, m_g2, 1)
+        momentum(2, m_g2, bank("dw"), "z00")
         for h in range(2):
             scalar_scatter(m_new[2], nm[2], h)
         store_m(2)
-        m_g = late.tile([P, N], F32, name="m_g3", offset=30 * KIB)
+        nc.vector.tensor_scalar(m_g3[:], m_win[3].indirect(offsets[:]), -LR * BETA, 0.0, MULT, ADD)
+        dw = product(3, slice(0, N), bank("dw3"))
+        step = tile([P, N], F32, "step", tag="z10")
         for h in range(2):
-            gather_m(3, m_g, h)
-        new_columns(3, m_g, ("z10", "sig1"))
-        m_new[3] = late.tile([P, T], F32, name="m_new3", offset=24 * KIB)
+            nc.vector.scalar_tensor_tensor(step[:, parts[h]], dw[:, parts[h]], -LR, m_g3[:, parts[h]], MULT, ADD)
+        weights(2, late.tile([P, N], F32, name="nw2", offset=32 * KIB))
+        for h in range(2):
+            scalar_scatter(w_new[2], nw[2], h)
+        m_new[3] = late.tile([P, T], F32, name="m_new3", offset=34 * KIB)
         nc.vector.tensor_copy(m_new[3][:], m_win[3])
-        nc.vector.tensor_copy(w_new[3][:].indirect(offsets[:]), nw[3][:])
+        nc.vector.tensor_tensor(w_new[3][:].indirect(offsets[:]), w_g[1][:, 1, :], step[:], ADD)
         for h in range(2):
-            scalar_scatter(m_new[3], nm[3], h)
+            scalar_scatter(m_new[3], step, h, -1.0 / LR)
+        nc.scalar.dma_start(o1_hbm[:, 3, :], m_new[3][:])
         store_w(3)
-        for t in (2, 3):
+        store_w(2)
+        for t in (3, 2):
             nc.vector.tensor_copy(place(t), w_new[t][:])
 
         words = pairs[:].bitcast(U32).rearrange("p (u c) -> p u c", u=2)
@@ -291,7 +304,6 @@ def tile_attend_gsig_pl_mom_kernel(tc, xT, wT, y, wt, xm, mT, offs, out_0, out_1
             if c + 1 < CHUNKS:
                 weave(c + 1)
             quantise(c)
-        store_m(3)
         store_words(0, 2)
         store_words(2, 3)
         store_words(3, 4)

@@ -113,7 +113,7 @@ def tile_attend_gsig_pl_mom_kernel(tc, xT, wT, y, wt, xm, mT, offs, out_0, out_1
                     x_raw[h][:].rearrange("p j (m t) -> p m j t", t=LANES)[:, :, :, 2 * k:2 * k + 2],
                 )
         w_new.append(tile([P, T], F32, "w_new3", tag="x_raw3"))
-        nc.scalar.activation(w_new[3][:, :T // 2], w_src[3][:, :T // 2], COPY)
+        nc.scalar.activation(w_new[3][:, :SPLIT], w_src[3][:, :SPLIT], COPY)
         x_q = tile([P, R], U32, "x_q")
         x_s = tile([P, R], U8, "x_s")
         for t in range(2):
@@ -121,14 +121,15 @@ def tile_attend_gsig_pl_mom_kernel(tc, xT, wT, y, wt, xm, mT, offs, out_0, out_1
             nc.vector.quantize_mx(x_q[:, cols].bitcast(E4M3), x_s[:, cols], x_bf[0][:, t * LANES * P:(t + 1) * LANES * P])
         nc.vector.quantize_mx(x_q[:, 2 * P:].bitcast(E4M3), x_s[:, 2 * P:], x_bf[1][:])
 
-        nc.vector.tensor_copy(w_new[3][:, T // 2:], w_src[3][:, T // 2:])
+        nc.vector.tensor_copy(w_new[3][:, SPLIT:], w_src[3][:, SPLIT:])
 
         sig = [tile([P, LANES, HALF], F32, "sig%d" % h) for h in range(2)]
         yw = [tile([P, LANES, HALF], F32, "yw%d" % h) for h in range(2)]
         wt_neg = tile([P, LANES], F32, "wt_neg")
         nc.gpsimd.tensor_scalar(wt_neg[:], wt_sb[:], -1.0, 0.0, MULT, ADD)
         for h, t in product_of(range(2), range(LANES)):
-            nc.gpsimd.tensor_scalar(yw[h][:, t, :], y_sb[h][:, t, :], wt_neg[:, t:t + 1], 0.0, MULT, ADD)
+            engine = nc.vector if h == 0 and t < 2 else nc.gpsimd
+            engine.tensor_scalar(yw[h][:, t, :], y_sb[h][:, t, :], wt_neg[:, t:t + 1], 0.0, MULT, ADD)
         for h in range(2):
             for k in range(2):
                 z = tile([P, 2, HALF], F32, "z%d%d" % (h, k)) if h + k < 2 else late.tile([P, 14, P], F32, name="z11", offset=17 * KIB)[:, :4, :].rearrange("p (e a) b -> p e (a b)", e=2)
@@ -141,7 +142,7 @@ def tile_attend_gsig_pl_mom_kernel(tc, xT, wT, y, wt, xm, mT, offs, out_0, out_1
 
         xm_cols = xm_raw[:].rearrange("p j (m t) -> p m j t", t=LANES)
         xm_bf = {}
-        xm_q = tile([P, D], U32, "xm_q")
+        xm_q = {0: tile([P, D // 2], U32, "xm_q0")}
         xm_s = tile([P, D], U8, "xm_s")
         g_bf = {}
         g_q = tile([P, N], U32, "g_q")
@@ -164,11 +165,11 @@ def tile_attend_gsig_pl_mom_kernel(tc, xT, wT, y, wt, xm, mT, offs, out_0, out_1
 
         def quantise_xm(first, count):
             cols = slice(first * P, (first + count) * P)
-            nc.vector.quantize_mx(xm_q[:, cols].bitcast(E4M3), xm_s[:, cols], xm_bf[first][:])
+            nc.vector.quantize_mx(xm_q[first][:].bitcast(E4M3), xm_s[:, cols], xm_bf[first][:])
 
         def product(t, slots, dw):
             cols = slice(t * P, (t + 1) * P)
-            nc.tensor.matmul_mx(dw[:, slots], xm_q[:, cols].bitcast(E4M3), xm_s[:, cols], g_q[:, slots].bitcast(E5M2), g_s[:, slots], start=True, stop=True)
+            nc.tensor.matmul_mx(dw[:, slots], xm_q[t // 2 * 2][:, t % 2 * P:(t % 2 + 1) * P].bitcast(E4M3), xm_s[:, cols], g_q[:, slots].bitcast(E5M2), g_s[:, slots], start=True, stop=True)
             return dw[:, slots]
 
         def scalar_scatter(window, values, h, scale=1.0):
@@ -186,9 +187,9 @@ def tile_attend_gsig_pl_mom_kernel(tc, xT, wT, y, wt, xm, mT, offs, out_0, out_1
         def new_w(t, nm, nw, h):
             nc.vector.scalar_tensor_tensor(nw[:, parts[h]], nm[:, parts[h]], -LR, w_g[t // 2][:, t % 2, parts[h]], MULT, ADD)
 
-        xm_bf[0] = late.tile([P, LANES * P], BF16, name="xm_bf0", offset=17 * KIB, align_bytes=64)
-        round_xm(0, 1, nc.scalar.copy)
-        m_g = late.tile([P, N], F32, name="m_g0", offset=23 * KIB)
+        xm_bf[0] = late.tile([P, 2 * LANES * P], BF16, name="xm_bf0", offset=17 * KIB, align_bytes=64)
+        round_xm(0, 2, nc.scalar.copy)
+        m_g = late.tile([P, 2 * N], F32, name="m_g0", offset=23 * KIB)
         nm = {0: tile([P, N], F32, "nm0")}
         nw = {0: tile([P, N], F32, "nw0")}
         for h in range(2):
@@ -197,7 +198,7 @@ def tile_attend_gsig_pl_mom_kernel(tc, xT, wT, y, wt, xm, mT, offs, out_0, out_1
         for h in range(2):
             quantise_g(h)
             if h == 0:
-                quantise_xm(0, 1)
+                quantise_xm(0, 2)
             dw.append(product(0, parts[h], bank(("dw", "dw3")[h])))
             nc.scalar.activation(m_g[:, parts[h]], m_win[0].indirect(halves[h]), COPY)
         for h in range(2):
@@ -205,11 +206,10 @@ def tile_attend_gsig_pl_mom_kernel(tc, xT, wT, y, wt, xm, mT, offs, out_0, out_1
         for h in range(2):
             new_w(0, nm[0], nw[0], h)
             scalar_scatter(w_new[0], nw[0], h)
-        xm_bf[1] = late.tile([P, 3 * LANES * P], BF16, name="xm_bf1", offset=24 * KIB, align_bytes=64)
-        round_xm(1, 3, nc.vector.tensor_copy)
+        xm_bf[2] = tile([P, 2 * LANES * P], BF16, "xm_bf2", tag="g_bf1")
+        round_xm(2, 2, nc.vector.tensor_copy)
         m_new[0] = late.tile([P, T], F32, name="m_new0", offset=16 * KIB)
         nc.vector.tensor_copy(m_new[0][:], m_win[0])
-        quantise_xm(1, 3)
         for h in range(2):
             scalar_scatter(m_new[0], nm[0], h)
         store_w(0)
@@ -238,11 +238,13 @@ def tile_attend_gsig_pl_mom_kernel(tc, xT, wT, y, wt, xm, mT, offs, out_0, out_1
             for h in range(2):
                 new_w(t, nm[t], nw[t], h)
 
-        m_g = halved(late.tile([P, 6 * N], F32, name="m_g1", offset=24 * KIB))
+        m_g = halved(late.tile([P, 6 * N], F32, name="m_g1", offset=25 * KIB))
+        nc.vector.tensor_copy(m_new[1][:, SPLIT:], m_src[1][:, SPLIT:])
+        xm_q[2] = late.tile([P, D // 2], U32, name="xm_q2", offset=24 * KIB, align_bytes=64)
+        quantise_xm(2, 2)
         for h in range(2):
             gather_m(1, m_g, h)
         momentum(1, m_g, bank("dw"), None)
-        nc.vector.tensor_copy(m_new[1][:, SPLIT:], m_src[1][:, SPLIT:])
         weights(1, tile([P, N], F32, "nw1"))
         round_plane(0)
         m_g2 = [late.tile([P, HALF], F32, name="m_g2", offset=33 * KIB)[:]]
@@ -283,30 +285,21 @@ def tile_attend_gsig_pl_mom_kernel(tc, xT, wT, y, wt, xm, mT, offs, out_0, out_1
         o_s = tile([P, T], U8, "o_s")
         o_q = tile([P, T], U32, "o_q", tag="xm_raw")
         words_hbm = out_2[0].rearrange("p c l -> p (c l)").bitcast(I32)
-        o_bf = [tile([P, CHUNK * LANES], BF16, "o_bf%d" % c, tag="w_src%d" % c) for c in range(CHUNKS)]
-
-        def weave(c):
-            (nc.vector.tensor_copy if c < 2 else nc.scalar.copy)(
-                o_bf[c][:].bitcast(U32).rearrange("p (c u) -> p c u", u=2),
-                words[:, :, c * CHUNK:(c + 1) * CHUNK].rearrange("p u c -> p c u"),
-            )
-
-        def quantise(c):
-            cols = slice(c * CHUNK, (c + 1) * CHUNK)
-            nc.vector.quantize_mx(o_q[:, cols].bitcast(E4M3), o_s[:, cols], o_bf[c][:])
-
-        def store_words(first, last):
-            cols = slice(first * CHUNK, last * CHUNK)
-            nc.sync.dma_start(words_hbm[:, cols], o_q[:, cols].bitcast(I32))
-
-        weave(0)
-        for c in range(CHUNKS):
-            if c + 1 < CHUNKS:
-                weave(c + 1)
-            quantise(c)
-        store_words(0, 2)
-        store_words(2, 3)
-        store_words(3, 4)
+        pieces = [(512, nc.vector.tensor_copy), (512, nc.vector.tensor_copy), (256, nc.vector.tensor_copy), (512, nc.scalar.copy), (256, nc.scalar.copy)]
+        woven = []
+        start = 0
+        for k, (width, copy) in enumerate(pieces):
+            cols = slice(start, start + width)
+            o_bf = tile([P, width * LANES], BF16, "o_bf%d" % k, tag=("w_src0", "w_src1", "w_src2", "w_src3", "m_src0")[k])
+            copy(o_bf[:].bitcast(U32).rearrange("p (c u) -> p c u", u=2), words[:, :, cols].rearrange("p u c -> p c u"))
+            woven.append((cols, o_bf))
+            start = cols.stop
+        stored = 0
+        for k, (cols, o_bf) in enumerate(woven):
+            nc.vector.quantize_mx(o_q[:, cols].bitcast(E4M3), o_s[:, cols], o_bf[:])
+            if k in (1, 3, 4):
+                nc.sync.dma_start(words_hbm[:, stored:cols.stop], o_q[:, stored:cols.stop].bitcast(I32))
+                stored = cols.stop
         scales_hbm = out_3[0].bitcast(I32)
         for q in range(4):
             nc.sync.dma_start(scales_hbm[4 * q:4 * q + 4, :], o_s[32 * q:32 * q + 4, :].bitcast(I32))

@@ -203,15 +203,16 @@ def tile_attend_gsig_pl_mom_kernel(tc, xT, wT, y, wt, xm, mT, offs, out_0, out_1
             nc.scalar.activation(m_g[:, parts[h]], m_win[0].indirect(halves[h]), COPY)
         for h in range(2):
             new_m(0, m_g[:, parts[h]], nm[0], dw[h], h)
+        m_new[0] = late.tile([P, T], F32, name="m_new0", offset=16 * KIB)
         for h in range(2):
             new_w(0, nm[0], nw[0], h)
+            if h == 0:
+                nc.vector.tensor_copy(m_new[0][:], m_win[0])
+        for h in range(2):
             scalar_scatter(w_new[0], nw[0], h)
+            scalar_scatter(m_new[0], nm[0], h)
         xm_bf[2] = tile([P, 2 * LANES * P], BF16, "xm_bf2", tag="g_bf1")
         round_xm(2, 2, nc.vector.tensor_copy)
-        m_new[0] = late.tile([P, T], F32, name="m_new0", offset=16 * KIB)
-        nc.vector.tensor_copy(m_new[0][:], m_win[0])
-        for h in range(2):
-            scalar_scatter(m_new[0], nm[0], h)
         store_w(0)
         store_m(0)
 

@@ -27,6 +27,8 @@ HALF = N // 2
 CHUNKS = 4
 CHUNK = T // CHUNKS
 KIB = 1024
+TAIL = 256
+BODY = T - TAIL
 SPLIT = 3 * T // 4
 
 
@@ -220,7 +222,7 @@ def tile_attend_gsig_pl_mom_kernel(tc, xT, wT, y, wt, xm, mT, offs, out_0, out_1
             return pairs[:, t // 2 * 2 * T:(t // 2 + 1) * 2 * T].rearrange("p (c e) -> p c e", e=2)[:, :, t % 2]
 
         def round_plane(t):
-            nc.gpsimd.tensor_scalar(place(t), w_new[t][:], 1.0, -0.0, MULT, ADD)
+            nc.gpsimd.tensor_scalar(place(t)[:, :BODY], w_new[t][:, :BODY], 1.0, -0.0, MULT, ADD)
 
         def gather_m(t, m_g, h):
             nc.vector.tensor_copy(m_g[h], m_win[t].indirect(halves[h]))
@@ -241,12 +243,12 @@ def tile_attend_gsig_pl_mom_kernel(tc, xT, wT, y, wt, xm, mT, offs, out_0, out_1
 
         m_g = halved(late.tile([P, 6 * N], F32, name="m_g1", offset=25 * KIB))
         nc.vector.tensor_copy(m_new[1][:, SPLIT:], m_src[1][:, SPLIT:])
-        xm_q[2] = late.tile([P, D // 2], U32, name="xm_q2", offset=24 * KIB, align_bytes=64)
-        quantise_xm(2, 2)
         for h in range(2):
             gather_m(1, m_g, h)
         momentum(1, m_g, bank("dw"), None)
         weights(1, tile([P, N], F32, "nw1"))
+        xm_q[2] = late.tile([P, D // 2], U32, name="xm_q2", offset=26 * KIB, align_bytes=64)
+        quantise_xm(2, 2)
         round_plane(0)
         m_g2 = [late.tile([P, HALF], F32, name="m_g2", offset=33 * KIB)[:]]
         gather_m(2, m_g2, 0)
@@ -257,13 +259,13 @@ def tile_attend_gsig_pl_mom_kernel(tc, xT, wT, y, wt, xm, mT, offs, out_0, out_1
             scalar_scatter(m_new[1], nm[1], h)
         store_m(1)
         m_g2.append(tile([P, HALF], F32, "later", tag="nw1")[:])
-        m_g3 = late.tile([P, N], F32, name="m_g3", offset=33 * KIB)
+        m_g3 = late.tile([P, 5 * HALF], F32, name="m_g3", offset=30 * KIB)[:, :N]
         gather_m(2, m_g2, 1)
         momentum(2, m_g2, bank("dw"), "z00")
         for h in range(2):
             scalar_scatter(m_new[2], nm[2], h)
         store_m(2)
-        nc.vector.tensor_scalar(m_g3[:], m_win[3].indirect(offsets[:]), -LR * BETA, 0.0, MULT, ADD)
+        nc.vector.tensor_scalar(m_g3, m_win[3].indirect(offsets[:]), -LR * BETA, 0.0, MULT, ADD)
         dw = product(3, slice(0, N), bank("dw3"))
         step = tile([P, N], F32, "step", tag="z10")
         for h in range(2):
@@ -272,15 +274,21 @@ def tile_attend_gsig_pl_mom_kernel(tc, xT, wT, y, wt, xm, mT, offs, out_0, out_1
         for h in range(2):
             scalar_scatter(w_new[2], nw[2], h)
         m_new[3] = late.tile([P, T], F32, name="m_new3", offset=34 * KIB)
-        nc.vector.tensor_copy(m_new[3][:], m_win[3])
         nc.vector.tensor_tensor(w_new[3][:].indirect(offsets[:]), w_g[1][:, 1, :], step[:], ADD)
+        nc.vector.tensor_copy(m_new[3][:], m_win[3])
         for h in range(2):
             scalar_scatter(m_new[3], step, h, -1.0 / LR)
         nc.scalar.dma_start(o1_hbm[:, 3, :], m_new[3][:])
         store_w(3)
         store_w(2)
+        tail = late.tile([P, LANES * TAIL], BF16, name="tail", offset=30 * KIB)
+        tail_place = tail[:].rearrange("p (u c e) -> p u c e", u=2, e=2)
+        for t in (0, 1):
+            nc.vector.tensor_copy(tail_place[:, 0, :, t], w_new[t][:, BODY:])
         for t in (3, 2):
-            nc.vector.tensor_copy(place(t), w_new[t][:])
+            nc.vector.tensor_copy(place(t)[:, :BODY], w_new[t][:, :BODY])
+        for t in (3, 2):
+            nc.vector.tensor_copy(tail_place[:, 1, :, t - 2], w_new[t][:, BODY:])
 
         words = pairs[:].bitcast(U32).rearrange("p (u c) -> p u c", u=2)
         o_s = tile([P, T], U8, "o_s")
@@ -292,7 +300,7 @@ def tile_attend_gsig_pl_mom_kernel(tc, xT, wT, y, wt, xm, mT, offs, out_0, out_1
         for k, (width, copy) in enumerate(pieces):
             cols = slice(start, start + width)
             o_bf = tile([P, width * LANES], BF16, "o_bf%d" % k, tag=("w_src0", "w_src1", "w_src2", "w_src3", "m_src0")[k])
-            copy(o_bf[:].bitcast(U32).rearrange("p (c u) -> p c u", u=2), words[:, :, cols].rearrange("p u c -> p c u"))
+            copy(o_bf[:].bitcast(U32).rearrange("p (c u) -> p c u", u=2), (words[:, :, cols] if cols.stop <= BODY else tail[:].bitcast(U32).rearrange("p (u c) -> p u c", u=2)).rearrange("p u c -> p c u"))
             woven.append((cols, o_bf))
             start = cols.stop
         stored = 0

@@ -43,7 +43,7 @@ def tile_attend_gsig_pl_mom_kernel(tc, xT, wT, y, wt, xm, mT, offs, out_0, out_1
             return sb.tile(shape, dtype, name=name, tag=tag or name, align_bytes=64)
 
         def bank(name):
-            return ps.tile([P, 512], F32, name=name, tag=name, bufs=4 if name == "a" else 1)
+            return ps.tile([P, 512], F32, name=name, tag=name, bufs=5 if name == "a" else 1)
 
         def planes(table):
             return table.rearrange("(p t) c -> p t c", t=LANES)
@@ -75,7 +75,7 @@ def tile_attend_gsig_pl_mom_kernel(tc, xT, wT, y, wt, xm, mT, offs, out_0, out_1
         for t in range(LANES):
             nc.sync.dma_start(m_src[t][:], m_hbm[:, t, :])
             if t == 1:
-                nc.sync.dma_start(m_new[1][:, :SPLIT], m_hbm[:, 1, :SPLIT])
+                nc.sync.dma_start(m_new[1][:, :T // 2], m_hbm[:, 1, :T // 2])
             if t == 2:
                 nc.sync.dma_start(m_new[2][:], m_hbm[:, 2, :])
         m_win = [m_src[t][:] for t in range(LANES)]
@@ -135,11 +135,14 @@ def tile_attend_gsig_pl_mom_kernel(tc, xT, wT, y, wt, xm, mT, offs, out_0, out_1
         for h in range(2):
             for k in range(2):
                 z = tile([P, 2, HALF], F32, "z%d%d" % (h, k)) if h + k < 2 else late.tile([P, 14, P], F32, name="z11", offset=17 * KIB)[:, :4, :].rearrange("p (e a) b -> p e (a b)", e=2)
-                a = bank("a")
-                for e in range(2):
-                    cols = slice((2 * k + e) * P, (2 * k + e + 1) * P)
-                    nc.tensor.matmul_mx(a[:, e * HALF:(e + 1) * HALF], x_q[:, cols].bitcast(E4M3), x_s[:, cols], w_q[:, parts[h]].bitcast(E4M3), w_s[:, parts[h]], start=True, stop=True)
-                nc.vector.tensor_tensor(z[:], a[:].rearrange("p (e n) -> p e n", e=2), y_sb[h][:, 2 * k:2 * k + 2, :], MULT)
+                count = 1 if h + k == 0 else 2
+                for first in range(0, 2, count):
+                    a = bank("a")
+                    for e in range(count):
+                        cols = slice((2 * k + first + e) * P, (2 * k + first + e + 1) * P)
+                        nc.tensor.matmul_mx(a[:, e * HALF:(e + 1) * HALF], x_q[:, cols].bitcast(E4M3), x_s[:, cols], w_q[:, parts[h]].bitcast(E4M3), w_s[:, parts[h]], start=True, stop=True)
+                    lanes = slice(first, first + count)
+                    nc.vector.tensor_tensor(z[:, lanes, :], a[:, :count * HALF].rearrange("p (e n) -> p e n", e=count), y_sb[h][:, 2 * k + first:2 * k + first + count, :], MULT)
                 nc.scalar.activation(sig[h][:, 2 * k:2 * k + 2, :], z[:], SIGMOID, scale=-1.0)
 
         xm_cols = xm_raw[:].rearrange("p j (m t) -> p m j t", t=LANES)
@@ -242,7 +245,7 @@ def tile_attend_gsig_pl_mom_kernel(tc, xT, wT, y, wt, xm, mT, offs, out_0, out_1
                 new_w(t, nm[t], nw[t], h)
 
         m_g = halved(late.tile([P, 6 * N], F32, name="m_g1", offset=25 * KIB))
-        nc.vector.tensor_copy(m_new[1][:, SPLIT:], m_src[1][:, SPLIT:])
+        nc.vector.tensor_copy(m_new[1][:, T // 2:], m_src[1][:, T // 2:])
         for h in range(2):
             gather_m(1, m_g, h)
         momentum(1, m_g, bank("dw"), None)

@@ -27,6 +27,7 @@ HALF = N // 2
 CHUNKS = 4
 CHUNK = T // CHUNKS
 KIB = 1024
+SHARE = 384
 TAIL = 256
 BODY = T - TAIL
 SPLIT = 3 * T // 4
@@ -75,7 +76,7 @@ def tile_attend_gsig_pl_mom_kernel(tc, xT, wT, y, wt, xm, mT, offs, out_0, out_1
         for t in range(LANES):
             nc.sync.dma_start(m_src[t][:], m_hbm[:, t, :])
             if t == 1:
-                nc.sync.dma_start(m_new[1][:, :T // 2], m_hbm[:, 1, :T // 2])
+                nc.sync.dma_start(m_new[1][:, :SPLIT], m_hbm[:, 1, :SPLIT])
             if t == 2:
                 nc.sync.dma_start(m_new[2][:], m_hbm[:, 2, :])
         m_win = [m_src[t][:] for t in range(LANES)]
@@ -245,7 +246,7 @@ def tile_attend_gsig_pl_mom_kernel(tc, xT, wT, y, wt, xm, mT, offs, out_0, out_1
                 new_w(t, nm[t], nw[t], h)
 
         m_g = halved(late.tile([P, 6 * N], F32, name="m_g1", offset=25 * KIB))
-        nc.vector.tensor_copy(m_new[1][:, T // 2:], m_src[1][:, T // 2:])
+        nc.vector.tensor_copy(m_new[1][:, SPLIT:], m_src[1][:, SPLIT:])
         for h in range(2):
             gather_m(1, m_g, h)
         momentum(1, m_g, bank("dw"), None)
@@ -273,31 +274,33 @@ def tile_attend_gsig_pl_mom_kernel(tc, xT, wT, y, wt, xm, mT, offs, out_0, out_1
         step = tile([P, N], F32, "step", tag="z10")
         for h in range(2):
             nc.vector.scalar_tensor_tensor(step[:, parts[h]], dw[:, parts[h]], -LR, m_g3[:, parts[h]], MULT, ADD)
-        weights(2, late.tile([P, N], F32, name="nw2", offset=32 * KIB))
-        for h in range(2):
-            scalar_scatter(w_new[2], nw[2], h)
+        short = late.tile([P, N - SHARE], F32, name="short", offset=33 * KIB + 512)
+        nc.vector.tensor_scalar(short[:], nm[2][:, SHARE:], -LR, 0.0, MULT, ADD)
+        nw[2] = late.tile([P, SHARE], F32, name="nw2", offset=32 * KIB)
+        nc.vector.scalar_tensor_tensor(nw[2][:], nm[2][:, :SHARE], -LR, w_g[1][:, 0, :SHARE], MULT, ADD)
+        nc.vector.tensor_tensor(w_new[2][:].indirect(offsets[:, SHARE // 16:]), w_g[1][:, 0, SHARE:], short[:], ADD)
+        nc.scalar.activation(w_new[2][:].indirect(offsets[:, :SHARE // 16]), nw[2][:], COPY)
         m_new[3] = late.tile([P, T], F32, name="m_new3", offset=34 * KIB)
-        nc.vector.tensor_tensor(w_new[3][:].indirect(offsets[:]), w_g[1][:, 1, :], step[:], ADD)
         nc.vector.tensor_copy(m_new[3][:], m_win[3])
+        nc.vector.tensor_tensor(w_new[3][:].indirect(offsets[:]), w_g[1][:, 1, :], step[:], ADD)
         for h in range(2):
             scalar_scatter(m_new[3], step, h, -1.0 / LR)
-        nc.scalar.dma_start(o1_hbm[:, 3, :], m_new[3][:])
-        store_w(3)
         store_w(2)
+        store_w(3)
+        store_m(3)
         tail = late.tile([P, LANES * TAIL], BF16, name="tail", offset=30 * KIB)
         tail_place = tail[:].rearrange("p (u c e) -> p u c e", u=2, e=2)
-        for t in (0, 1):
-            nc.vector.tensor_copy(tail_place[:, 0, :, t], w_new[t][:, BODY:])
-        for t in (3, 2):
-            nc.vector.tensor_copy(place(t)[:, :BODY], w_new[t][:, :BODY])
-        for t in (3, 2):
-            nc.vector.tensor_copy(tail_place[:, 1, :, t - 2], w_new[t][:, BODY:])
+        for cols in (slice(0, T // 2), slice(T // 2, BODY)):
+            for t in (3, 2):
+                nc.vector.tensor_copy(place(t)[:, cols], w_new[t][:, cols])
+        for t in range(LANES):
+            nc.vector.tensor_copy(tail_place[:, t // 2, :, t % 2], w_new[t][:, BODY:])
 
         words = pairs[:].bitcast(U32).rearrange("p (u c) -> p u c", u=2)
         o_s = tile([P, T], U8, "o_s")
         o_q = tile([P, T], U32, "o_q", tag="xm_raw")
         words_hbm = out_2[0].rearrange("p c l -> p (c l)").bitcast(I32)
-        pieces = [(512, nc.vector.tensor_copy), (512, nc.vector.tensor_copy), (256, nc.vector.tensor_copy), (512, nc.scalar.copy), (256, nc.scalar.copy)]
+        pieces = [(512, nc.scalar.copy), (512, nc.scalar.copy), (512, nc.vector.tensor_copy), (256, nc.scalar.copy), (256, nc.scalar.copy)]
         woven = []
         start = 0
         for k, (width, copy) in enumerate(pieces):

@@ -195,6 +195,8 @@ def tile_attend_gsig_pl_mom_kernel(tc, xT, wT, y, wt, xm, mT, offs, out_0, out_1
 
         xm_bf[0] = late.tile([P, 2 * LANES * P], BF16, name="xm_bf0", offset=17 * KIB, align_bytes=64)
         round_xm(0, 2, nc.scalar.copy)
+        m_new[0] = tile([P, T], F32, "m_new0", tag="z01")
+        nc.scalar.activation(m_new[0][:], m_src[0][:], COPY)
         m_g = late.tile([P, 2 * N], F32, name="m_g0", offset=23 * KIB)
         nm = {0: tile([P, N], F32, "nm0")}
         nw = {0: tile([P, N], F32, "nw0")}
@@ -206,19 +208,17 @@ def tile_attend_gsig_pl_mom_kernel(tc, xT, wT, y, wt, xm, mT, offs, out_0, out_1
             if h == 0:
                 quantise_xm(0, 2)
             dw.append(product(0, parts[h], bank(("dw", "dw3")[h])))
-            nc.scalar.activation(m_g[:, parts[h]], m_win[0].indirect(halves[h]), COPY)
+        for h in range(2):
+            nc.vector.tensor_copy(m_g[:, parts[h]], m_win[0].indirect(halves[h]))
         for h in range(2):
             new_m(0, m_g[:, parts[h]], nm[0], dw[h], h)
-        m_new[0] = late.tile([P, T], F32, name="m_new0", offset=16 * KIB)
         for h in range(2):
             new_w(0, nm[0], nw[0], h)
-            if h == 0:
-                nc.vector.tensor_copy(m_new[0][:], m_win[0])
-        for h in range(2):
             scalar_scatter(w_new[0], nw[0], h)
-            scalar_scatter(m_new[0], nm[0], h)
-        xm_bf[2] = tile([P, 2 * LANES * P], BF16, "xm_bf2", tag="g_bf1")
+        xm_bf[2] = late.tile([P, 2 * LANES * P], BF16, name="xm_bf2", offset=21 * KIB + 512, align_bytes=64)
         round_xm(2, 2, nc.vector.tensor_copy)
+        for h in range(2):
+            scalar_scatter(m_new[0], nm[0], h)
         store_w(0)
         store_m(0)
 

@@ -135,7 +135,7 @@ def tile_attend_gsig_pl_mom_kernel(tc, xT, wT, y, wt, xm, mT, offs, out_0, out_1
             engine.tensor_scalar(yw[h][:, t, :], y_sb[h][:, t, :], wt_neg[:, t:t + 1], 0.0, MULT, ADD)
         for h in range(2):
             for k in range(2):
-                z = tile([P, 2, HALF], F32, "z%d%d" % (h, k)) if h + k < 2 else late.tile([P, 14, P], F32, name="z11", offset=17 * KIB)[:, :4, :].rearrange("p (e a) b -> p e (a b)", e=2)
+                z = tile([P, 2, HALF], F32, "z%d%d" % (h, k)) if h + k < 2 else late.tile([P, 2, HALF], F32, name="z11", offset=18 * KIB)
                 count = 1 if h + k == 0 else 2
                 for first in range(0, 2, count):
                     a = bank("a")
@@ -197,7 +197,7 @@ def tile_attend_gsig_pl_mom_kernel(tc, xT, wT, y, wt, xm, mT, offs, out_0, out_1
         round_xm(0, 2, nc.scalar.copy)
         m_new[0] = tile([P, T], F32, "m_new0", tag="z01")
         nc.scalar.activation(m_new[0][:], m_src[0][:], COPY)
-        m_g = late.tile([P, 2 * N], F32, name="m_g0", offset=23 * KIB)
+        m_g = late.tile([P, N], F32, name="m_g0", offset=19 * KIB)
         nm = {0: tile([P, N], F32, "nm0")}
         nw = {0: tile([P, N], F32, "nw0")}
         for h in range(2):
@@ -215,7 +215,7 @@ def tile_attend_gsig_pl_mom_kernel(tc, xT, wT, y, wt, xm, mT, offs, out_0, out_1
         for h in range(2):
             new_w(0, nm[0], nw[0], h)
             scalar_scatter(w_new[0], nw[0], h)
-        xm_bf[2] = late.tile([P, 2 * LANES * P], BF16, name="xm_bf2", offset=21 * KIB + 512, align_bytes=64)
+        xm_bf[2] = late.tile([P, 2 * LANES * P], BF16, name="xm_bf2", offset=18 * KIB, align_bytes=64)
         round_xm(2, 2, nc.vector.tensor_copy)
         for h in range(2):
             scalar_scatter(m_new[0], nm[0], h)
@@ -245,16 +245,16 @@ def tile_attend_gsig_pl_mom_kernel(tc, xT, wT, y, wt, xm, mT, offs, out_0, out_1
             for h in range(2):
                 new_w(t, nm[t], nw[t], h)
 
-        m_g = halved(late.tile([P, 6 * N], F32, name="m_g1", offset=25 * KIB))
+        m_g = halved(late.tile([P, N], F32, name="m_g1", offset=20 * KIB))
         nc.vector.tensor_copy(m_new[1][:, SPLIT:], m_src[1][:, SPLIT:])
         for h in range(2):
             gather_m(1, m_g, h)
         momentum(1, m_g, bank("dw"), None)
         weights(1, tile([P, N], F32, "nw1"))
-        xm_q[2] = late.tile([P, D // 2], U32, name="xm_q2", offset=26 * KIB, align_bytes=64)
+        xm_q[2] = late.tile([P, D // 2], U32, name="xm_q2", offset=20 * KIB, align_bytes=64)
         quantise_xm(2, 2)
         round_plane(0)
-        m_g2 = [late.tile([P, HALF], F32, name="m_g2", offset=33 * KIB)[:]]
+        m_g2 = [late.tile([P, HALF], F32, name="m_g2", offset=21 * KIB)[:]]
         gather_m(2, m_g2, 0)
         nc.vector.tensor_copy(w_new[1][:].indirect(offsets[:]), nw[1][:])
         store_w(1)
@@ -263,7 +263,7 @@ def tile_attend_gsig_pl_mom_kernel(tc, xT, wT, y, wt, xm, mT, offs, out_0, out_1
             scalar_scatter(m_new[1], nm[1], h)
         store_m(1)
         m_g2.append(tile([P, HALF], F32, "later", tag="nw1")[:])
-        m_g3 = late.tile([P, 5 * HALF], F32, name="m_g3", offset=30 * KIB)[:, :N]
+        m_g3 = late.tile([P, N], F32, name="m_g3", offset=21 * KIB + 512)[:]
         gather_m(2, m_g2, 1)
         momentum(2, m_g2, bank("dw"), "z00")
         for h in range(2):
@@ -274,13 +274,13 @@ def tile_attend_gsig_pl_mom_kernel(tc, xT, wT, y, wt, xm, mT, offs, out_0, out_1
         step = tile([P, N], F32, "step", tag="z10")
         for h in range(2):
             nc.vector.scalar_tensor_tensor(step[:, parts[h]], dw[:, parts[h]], -LR, m_g3[:, parts[h]], MULT, ADD)
-        short = late.tile([P, N - SHARE], F32, name="short", offset=33 * KIB + 512)
+        short = late.tile([P, N - SHARE], F32, name="short", offset=21 * KIB + 256)
         nc.vector.tensor_scalar(short[:], nm[2][:, SHARE:], -LR, 0.0, MULT, ADD)
-        nw[2] = late.tile([P, SHARE], F32, name="nw2", offset=32 * KIB)
+        nw[2] = late.tile([P, SHARE], F32, name="nw2", offset=21 * KIB + 768)
         nc.vector.scalar_tensor_tensor(nw[2][:], nm[2][:, :SHARE], -LR, w_g[1][:, 0, :SHARE], MULT, ADD)
         nc.vector.tensor_tensor(w_new[2][:].indirect(offsets[:, SHARE // 16:]), w_g[1][:, 0, SHARE:], short[:], ADD)
         nc.scalar.activation(w_new[2][:].indirect(offsets[:, :SHARE // 16]), nw[2][:], COPY)
-        m_new[3] = late.tile([P, T], F32, name="m_new3", offset=34 * KIB)
+        m_new[3] = late.tile([P, T], F32, name="m_new3", offset=23 * KIB + 256)
         nc.vector.tensor_copy(m_new[3][:], m_win[3])
         nc.vector.tensor_tensor(w_new[3][:].indirect(offsets[:]), w_g[1][:, 1, :], step[:], ADD)
         for h in range(2):
@@ -288,7 +288,7 @@ def tile_attend_gsig_pl_mom_kernel(tc, xT, wT, y, wt, xm, mT, offs, out_0, out_1
         store_w(2)
         store_w(3)
         store_m(3)
-        tail = late.tile([P, LANES * TAIL], BF16, name="tail", offset=30 * KIB)
+        tail = late.tile([P, LANES * TAIL], BF16, name="tail", offset=19 * KIB + 768)
         tail_place = tail[:].rearrange("p (u c e) -> p u c e", u=2, e=2)
         for cols in (slice(0, T // 2), slice(T // 2, BODY)):
             for t in (3, 2):

@@ -1,7 +1,7 @@
 from contextlib import ExitStack
-from itertools import product as product_of
 
 import concourse.mybir as mybir
+from concourse.masks import make_identity
 
 F32 = mybir.dt.float32
 BF16 = mybir.dt.bfloat16
@@ -24,12 +24,8 @@ BETA = 0.9
 FLOPS = 2 * 2 * D * R * N
 
 HALF = N // 2
-CHUNKS = 4
-CHUNK = T // CHUNKS
 KIB = 1024
-SHARE = 384
-TAIL = 256
-BODY = T - TAIL
+ORDER = (2, 3, 0, 1)
 SPLIT = 3 * T // 4
 
 
@@ -37,149 +33,201 @@ def tile_attend_gsig_pl_mom_kernel(tc, xT, wT, y, wt, xm, mT, offs, out_0, out_1
     nc = tc.nc
     with ExitStack() as ctx:
         sb = ctx.enter_context(tc.tile_pool(name="sb", bufs=1))
-        late = ctx.enter_context(tc.tile_pool(name="late", bufs=1))
-        ps = ctx.enter_context(tc.psum_pool(name="ps", bufs=8))
+        mem = ctx.enter_context(tc.tile_pool(name="mem", bufs=1))
+        ps = ctx.enter_context(tc.psum_pool(name="ps", bufs=1))
 
-        def tile(shape, dtype, name, tag=None):
-            return sb.tile(shape, dtype, name=name, tag=tag or name, align_bytes=64)
+        def at(offset, shape, dtype, name):
+            return mem.tile(shape, dtype, name=name, offset=offset, align_bytes=64)
 
-        def bank(name):
-            return ps.tile([P, 512], F32, name=name, tag=name, bufs=5 if name == "a" else 1)
+        def bank(tag, bufs):
+            return ps.tile([P, 512], F32, name=tag, tag=tag, bufs=bufs)
 
         def planes(table):
             return table.rearrange("(p t) c -> p t c", t=LANES)
 
         w_hbm, m_hbm, o0_hbm, o1_hbm = planes(wT), planes(mT), planes(out_0), planes(out_1)
         parts = [slice(h * HALF, (h + 1) * HALF) for h in range(2)]
+        first, second, third, last = ORDER
 
         offsets = sb.tile([P, N // 16], U16, name="offsets")
         halves = [offsets[:, h * (HALF // 16):(h + 1) * (HALF // 16)] for h in range(2)]
-        wt_sb = tile([P, LANES], F32, "wt_sb")
-        w_src = [tile([P, T], F32, "w_src%d" % t) for t in range(LANES)]
+        wt_sb = sb.tile([P, LANES], F32, name="wt_sb")
+        w_src = [at(8 * KIB * t, [P, T], F32, "w_src%d" % t) for t in range(LANES)]
         for t in range(LANES):
             nc.sync.dma_start(w_src[t][:], w_hbm[:, t, :])
             if t == 0:
                 nc.sync.dma_start(offsets[:], offs)
-                nc.sync.dma_start(wt_sb[:], wt[0].rearrange("(p t) o -> p (t o)", t=LANES))
-        x_hbm = planes(xT[0])
-        x_raw = [tile([P, LANES, R // 4], F32, "x_raw%d" % h) for h in range(4)]
-        for h in range(4):
-            nc.sync.dma_start(x_raw[h][:], x_hbm[:, :, h * (R // 4):(h + 1) * (R // 4)])
-        y_sb = [tile([P, LANES, HALF], F32, "y_sb%d" % h) for h in range(2)]
-        for h in range(2):
-            nc.sync.dma_start(y_sb[h][:], planes(y[0])[:, :, parts[h]])
-        xm_raw = tile([P, LANES, D], F32, "xm_raw")
-        nc.sync.dma_start(xm_raw[:], planes(xm[0]))
-        m_src = [tile([P, T], F32, "m_src%d" % t) for t in range(LANES)]
-        w_new = [tile([P, T], F32, "w_new%d" % t) for t in range(LANES - 1)]
-        m_new = {t: tile([P, T], F32, "m_new%d" % t) for t in (1, 2)}
-        for t in range(LANES):
-            nc.sync.dma_start(m_src[t][:], m_hbm[:, t, :])
             if t == 1:
-                nc.sync.dma_start(m_new[1][:, :SPLIT], m_hbm[:, 1, :SPLIT])
-            if t == 2:
-                nc.sync.dma_start(m_new[2][:], m_hbm[:, 2, :])
-        m_win = [m_src[t][:] for t in range(LANES)]
+                nc.sync.dma_start(wt_sb[:], wt[0].rearrange("(p t) o -> p (t o)", t=LANES))
+        x_raw = at(129 * KIB, [P, LANES, R], F32, "x_raw")
+        nc.sync.dma_start(x_raw[:], planes(xT[0]))
+        y_sb = [at((137 + 4 * k) * KIB, [P, 2, N], F32, "y_sb%d" % k) for k in range(2)]
+        for k in range(2):
+            nc.sync.dma_start(y_sb[k][:], planes(y[0])[:, 2 * k:2 * k + 2, :])
+        xm_raw = at(145 * KIB, [P, LANES, D], F32, "xm_raw")
+        nc.sync.dma_start(xm_raw[:], planes(xm[0]))
+        m_src = {t: at((64 + 8 * t) * KIB, [P, T], F32, "m_src%d" % t) for t in ORDER}
+        m_new = {second: at(104 * KIB, [P, T], F32, "m_new_second")}
+        for t in ORDER:
+            nc.sync.dma_start(m_src[t][:], m_hbm[:, t, :])
+            if t == second:
+                nc.sync.dma_start(m_new[t][:], m_hbm[:, t, :])
 
-        warm = tile([P, 1], F32, "warm")
+        warm = sb.tile([P, 1], F32, name="warm")
         nc.gpsimd.memset(warm[:], 0.0)
         nc.scalar.activation(warm[:], warm[:], SIGMOID)
+        one = sb.tile([P, 1], F32, name="one")
+        nc.gpsimd.memset(one[:], 1.0)
+        ident = at(211 * KIB, [P, P], F32, "ident")
+        make_identity(nc, ident[:])
 
-        pairs = late.tile([P, 4 * T], BF16, name="pairs", offset=0)
-        w_g = [pairs[:, k * 2 * T:k * 2 * T + 4 * N].bitcast(F32).rearrange("p (e c) -> p e c", e=2) for k in range(2)]
-        w_bf = [tile([P, HALF * LANES], BF16, "w_bf%d" % h) for h in range(2)]
+        w_new = [at((32 + 8 * t) * KIB, [P, T], F32, "w_new%d" % t) for t in range(LANES)]
+        w_g = [at((177 + 4 * k) * KIB, [P, 2, N], F32, "w_g%d" % k) for k in range(2)]
+        w_bf = [at((185 + 2 * h) * KIB, [P, HALF * LANES], BF16, "w_bf%d" % h) for h in range(2)]
         w_view = [w_bf[h][:].rearrange("p (c t) -> p c t", t=LANES) for h in range(2)]
+        once, parked = {}, {}
 
         def round_pair(k, h):
             nc.vector.tensor_copy(w_view[h][:, :, 2 * k:2 * k + 2], w_g[k][:, :, parts[h]].rearrange("p t c -> p c t"))
 
+        def turn(dst, src):
+            for b in range(N // P):
+                nc.tensor.transpose(dst[:, b * P:(b + 1) * P], src[:, b * P:(b + 1) * P], ident[:])
+
+        def park(t):
+            turned = at((129 + 2 * t) * KIB, [P, N], F32, "turned%d" % t)
+            nc.scalar.copy(turned[:], once[t][:])
+            parked[t] = bank("parked%d" % t, 1)
+            turn(parked[t], turned)
+
         for t in range(LANES - 1):
             nc.vector.tensor_copy(w_g[t // 2][:, t % 2, :], w_src[t][:].indirect(offsets[:]))
+            nc.scalar.activation(w_new[t][:], w_src[t][:], COPY)
+            if t < 2:
+                once[t] = bank("once", 2)
+                turn(once[t], w_g[0][:, t, :])
             if t == 1:
                 for h in range(2):
                     round_pair(0, h)
-            nc.scalar.activation(w_new[t][:], w_src[t][:], COPY)
         for h in range(2):
             nc.vector.tensor_copy(w_g[1][:, 1, parts[h]], w_src[3][:].indirect(halves[h]))
-        w_q = tile([P, N], U32, "w_q")
-        w_s = tile([P, N], U8, "w_s")
+        nc.scalar.activation(w_new[3][:], w_src[3][:], COPY)
+        w_q = at(201 * KIB, [P, N], U32, "w_q")
+        w_s = at(209 * KIB, [P, N], U8, "w_s")
         for h in range(2):
             round_pair(1, h)
-        for h in range(2):
+
+        def quantise_w(h):
             nc.vector.quantize_mx(w_q[:, parts[h]].bitcast(E4M3), w_s[:, parts[h]], w_bf[h][:])
 
-        x_bf = [tile([P, R * 2], BF16, "x_bf%d" % k) for k in range(2)]
-        for h in range(4):
-            for k in range(2):
-                nc.scalar.copy(
-                    x_bf[k][:].rearrange("p (t m j) -> p m j t", t=2, j=LANES)[:, h * (P // 4):(h + 1) * (P // 4), :, :],
-                    x_raw[h][:].rearrange("p j (m t) -> p m j t", t=LANES)[:, :, :, 2 * k:2 * k + 2],
-                )
-        w_new.append(tile([P, T], F32, "w_new3", tag="x_raw3"))
-        nc.scalar.activation(w_new[3][:, :SPLIT], w_src[3][:, :SPLIT], COPY)
-        x_q = tile([P, R], U32, "x_q")
-        x_s = tile([P, R], U8, "x_s")
-        for t in range(2):
-            cols = slice(t * P, (t + 1) * P)
-            nc.vector.quantize_mx(x_q[:, cols].bitcast(E4M3), x_s[:, cols], x_bf[0][:, t * LANES * P:(t + 1) * LANES * P])
-        nc.vector.quantize_mx(x_q[:, 2 * P:].bitcast(E4M3), x_s[:, 2 * P:], x_bf[1][:])
+        def deal(dst, raw, k, copy, rows=slice(0, P)):
+            copy(dst.rearrange("p (t m j) -> p m j t", t=2, j=LANES)[:, rows, :, :], raw[:].rearrange("p j (m t) -> p m j t", t=LANES)[:, rows, :, 2 * k:2 * k + 2])
 
-        nc.vector.tensor_copy(w_new[3][:, SPLIT:], w_src[3][:, SPLIT:])
+        x_bf = [at((189 + 2 * k) * KIB, [P, R * 2], BF16, "x_bf%d" % k) for k in range(2)]
+        x_q = at(203 * KIB, [P, R], U32, "x_q")
+        x_s = at(209 * KIB + 512, [P, R], U8, "x_s")
 
-        sig = [tile([P, LANES, HALF], F32, "sig%d" % h) for h in range(2)]
-        yw = [tile([P, LANES, HALF], F32, "yw%d" % h) for h in range(2)]
-        wt_neg = tile([P, LANES], F32, "wt_neg")
+        def quantise_x(k):
+            cols = slice(2 * k * P, (2 * k + 2) * P)
+            nc.vector.quantize_mx(x_q[:, cols].bitcast(E4M3), x_s[:, cols], x_bf[k][:])
+
+        for h in range(2):
+            quantise_w(h)
+        deal(x_bf[0][:], x_raw, 0, nc.scalar.copy)
+        deal(x_bf[1][:], x_raw, 1, nc.vector.tensor_copy, slice(P // 2, P))
+        deal(x_bf[1][:], x_raw, 1, nc.scalar.copy, slice(0, P // 2))
+        quantise_x(0)
+
+        sig = [at((153 + 4 * h) * KIB, [P, LANES, HALF], F32, "sig%d" % h) for h in range(2)]
+        yw = at(161 * KIB, [P, LANES, N], F32, "yw")
+        wt_neg = at(191 * KIB, [P, LANES], F32, "wt_neg")
+        nc.vector.tensor_scalar(yw[:, 0, :], y_sb[0][:, 0, :], wt_sb[:, 0:1], -1.0, MULT, MULT)
+        quantise_x(1)
         nc.gpsimd.tensor_scalar(wt_neg[:], wt_sb[:], -1.0, 0.0, MULT, ADD)
-        for h, t in product_of(range(2), range(LANES)):
-            engine = nc.vector if h == 0 and t < 2 else nc.gpsimd
-            engine.tensor_scalar(yw[h][:, t, :], y_sb[h][:, t, :], wt_neg[:, t:t + 1], 0.0, MULT, ADD)
+        for t in range(1, LANES):
+            nc.gpsimd.tensor_scalar(yw[:, t, :], y_sb[t // 2][:, t % 2, :], wt_neg[:, t:t + 1], 0.0, MULT, ADD)
+        scores = {}
+
+        def score(h, k):
+            scores[h, k] = bank("sum", 4)
+            for e in range(2):
+                cols = slice((2 * k + e) * P, (2 * k + e + 1) * P)
+                nc.tensor.matmul_mx(scores[h, k][:, e * HALF:(e + 1) * HALF], x_q[:, cols].bitcast(E4M3), x_s[:, cols], w_q[:, parts[h]].bitcast(E4M3), w_s[:, parts[h]], start=True, stop=True)
+
+        def weigh(h, k):
+            z = at(((169 * KIB, 171 * KIB), (173 * KIB, 220 * KIB - 64))[h][k], [P, 2, HALF], F32, "z%d%d" % (h, k))
+            nc.vector.tensor_tensor(z[:], scores[h, k][:].rearrange("p (e n) -> p e n", e=2), y_sb[k][:, :, parts[h]], MULT)
+            nc.scalar.activation(sig[h][:, 2 * k:2 * k + 2, :], z[:], SIGMOID, scale=-1.0)
+
         for h in range(2):
             for k in range(2):
-                z = tile([P, 2, HALF], F32, "z%d%d" % (h, k)) if h + k < 2 else late.tile([P, 2, HALF], F32, name="z11", offset=18 * KIB)
-                count = 1 if h + k == 0 else 2
-                for first in range(0, 2, count):
-                    a = bank("a")
-                    for e in range(count):
-                        cols = slice((2 * k + first + e) * P, (2 * k + first + e + 1) * P)
-                        nc.tensor.matmul_mx(a[:, e * HALF:(e + 1) * HALF], x_q[:, cols].bitcast(E4M3), x_s[:, cols], w_q[:, parts[h]].bitcast(E4M3), w_s[:, parts[h]], start=True, stop=True)
-                    lanes = slice(first, first + count)
-                    nc.vector.tensor_tensor(z[:, lanes, :], a[:, :count * HALF].rearrange("p (e n) -> p e n", e=count), y_sb[h][:, 2 * k + first:2 * k + first + count, :], MULT)
-                nc.scalar.activation(sig[h][:, 2 * k:2 * k + 2, :], z[:], SIGMOID, scale=-1.0)
+                score(h, k)
+        for t in range(2):
+            park(t)
+        for h in range(2):
+            for k in range(2):
+                weigh(h, k)
 
-        xm_cols = xm_raw[:].rearrange("p j (m t) -> p m j t", t=LANES)
-        xm_bf = {}
-        xm_q = {0: tile([P, D // 2], U32, "xm_q0")}
-        xm_s = tile([P, D], U8, "xm_s")
-        g_bf = {}
-        g_q = tile([P, N], U32, "g_q")
-        g_s = tile([P, N], U8, "g_s")
-
-        def round_xm(first, count, copy):
-            copy(xm_bf[first][:].rearrange("p (t m j) -> p m j t", t=count, j=LANES), xm_cols[:, :, :, first:first + count])
-
-        def make_g(h):
-            g_bf[h] = tile([P, HALF * LANES], BF16, "g_bf%d" % h)
+        xm_both = at(216 * KIB, [P, D * 4], BF16, "xm_both")
+        xm_bf = [xm_both[:, 2 * D * k:2 * D * (k + 1)] for k in range(2)]
+        xm_q = at(205 * KIB, [P, D], U32, "xm_q")
+        xm_s = at(210 * KIB, [P, D], U8, "xm_s")
+        g_bf = [at((197 + 2 * h) * KIB, [P, HALF * LANES], BF16, "g_bf%d" % h) for h in range(2)]
+        g_q = at(207 * KIB, [P, N], U32, "g_q")
+        g_s = at(210 * KIB + 512, [P, N], U8, "g_s")
+        for k in (1, 0):
+            deal(xm_bf[k], xm_raw, k, nc.scalar.copy)
+        for h in range(2):
             nc.vector.tensor_tensor(
                 g_bf[h][:].rearrange("p (c i t) -> p c t i", i=4, t=LANES),
                 sig[h][:].rearrange("p t (c i) -> p c t i", i=4),
-                yw[h][:].rearrange("p t (c i) -> p c t i", i=4),
+                yw[:, :, parts[h]].rearrange("p t (c i) -> p c t i", i=4),
                 MULT,
             )
 
-        def quantise_g(h):
-            nc.vector.quantize_mx(g_q[:, parts[h]].bitcast(E5M2), g_s[:, parts[h]], g_bf[h][:])
+        def quantise_xm(k):
+            cols = slice(2 * k * P, (2 * k + 2) * P)
+            nc.vector.quantize_mx(xm_q[:, cols].bitcast(E4M3), xm_s[:, cols], xm_bf[k])
 
-        def quantise_xm(first, count):
-            cols = slice(first * P, (first + count) * P)
-            nc.vector.quantize_mx(xm_q[first][:].bitcast(E4M3), xm_s[:, cols], xm_bf[first][:])
+        nc.vector.quantize_mx(g_q[:, parts[0]].bitcast(E5M2), g_s[:, parts[0]], g_bf[0][:])
+        quantise_xm(1)
+        nc.vector.quantize_mx(g_q[:, parts[1]].bitcast(E5M2), g_s[:, parts[1]], g_bf[1][:])
+        quantise_xm(0)
+        m_new[first] = at(222 * KIB - 128, [P, T], F32, "m_new_first")
+        nc.scalar.activation(m_new[first][:], m_src[first][:], COPY)
 
-        def product(t, slots, dw):
+        nm, nw = {}, {}
+        m_g_at = {first: 185 * KIB, second: 187 * KIB, third: 112 * KIB, last: 189 * KIB}
+        nw_at = {first: 137 * KIB, second: 139 * KIB, third: 141 * KIB, last: 120 * KIB}
+        pairs = at(0, [P, 4 * T], BF16, "pairs")
+
+        def place(t):
+            return pairs[:, t // 2 * 2 * T:(t // 2 + 1) * 2 * T].rearrange("p (c e) -> p c e", e=2)[:, :, t % 2]
+
+        def round_plane(t, unit, cols=slice(0, T)):
+            nc.gpsimd.tensor_scalar(place(t)[:, cols], w_new[t][:, cols], unit, -0.0, MULT, ADD)
+
+        def columns(t):
             cols = slice(t * P, (t + 1) * P)
-            nc.tensor.matmul_mx(dw[:, slots], xm_q[t // 2 * 2][:, t % 2 * P:(t % 2 + 1) * P].bitcast(E4M3), xm_s[:, cols], g_q[:, slots].bitcast(E5M2), g_s[:, slots], start=True, stop=True)
-            return dw[:, slots]
+            dw = bank("sum", 4)
+            nc.tensor.matmul_mx(dw[:], xm_q[:, cols].bitcast(E4M3), xm_s[:, cols], g_q[:].bitcast(E5M2), g_s[:], start=True, stop=True)
+            m_g = at(m_g_at[t], [P, N], F32, "m_g%d" % t)
+            nm[t] = at((129 + 2 * t) * KIB, [P, N], F32, "nm%d" % t)
+            nw[t] = at(nw_at[t], [P, N], F32, "nw%d" % t)
+            old = parked[t][:] if t in parked else w_g[t // 2][:, t % 2, :]
+            for h in range(2):
+                nc.vector.tensor_copy(m_g[:, parts[h]], m_src[t][:].indirect(halves[h]))
+            for h in range(2):
+                nc.vector.scalar_tensor_tensor(nm[t][:, parts[h]], m_g[:, parts[h]], BETA, dw[:, parts[h]], MULT, ADD)
+            for h in range(2):
+                nc.vector.scalar_tensor_tensor(nw[t][:, parts[h]], nm[t][:, parts[h]], -LR, old[:, parts[h]], MULT, ADD)
 
-        def scalar_scatter(window, values, h, scale=1.0):
-            nc.scalar.activation(window[:].indirect(halves[h]), values[:, parts[h]], COPY, scale=scale)
+        def scalar_scatter(window, values, unit):
+            nc.scalar.activation(window[:].indirect(offsets[:]), values[:], COPY, scale=unit)
+
+        def vector_scatter(t):
+            nc.vector.tensor_copy(m_new[t][:].indirect(offsets[:]), nm[t][:])
+            nc.sync.dma_start(o1_hbm[:, t, :], m_new[t][:])
 
         def store_w(t):
             nc.sync.dma_start(o0_hbm[:, t, :], w_new[t][:])
@@ -187,126 +235,52 @@ def tile_attend_gsig_pl_mom_kernel(tc, xT, wT, y, wt, xm, mT, offs, out_0, out_1
         def store_m(t):
             nc.sync.dma_start(o1_hbm[:, t, :], m_new[t][:])
 
-        def new_m(t, m_g, nm, dw, h):
-            nc.vector.scalar_tensor_tensor(nm[:, parts[h]], m_g, BETA, dw, MULT, ADD)
-
-        def new_w(t, nm, nw, h):
-            nc.vector.scalar_tensor_tensor(nw[:, parts[h]], nm[:, parts[h]], -LR, w_g[t // 2][:, t % 2, parts[h]], MULT, ADD)
-
-        xm_bf[0] = late.tile([P, 2 * LANES * P], BF16, name="xm_bf0", offset=17 * KIB, align_bytes=64)
-        round_xm(0, 2, nc.scalar.copy)
-        m_new[0] = tile([P, T], F32, "m_new0", tag="z01")
-        nc.scalar.activation(m_new[0][:], m_src[0][:], COPY)
-        m_g = late.tile([P, N], F32, name="m_g0", offset=19 * KIB)
-        nm = {0: tile([P, N], F32, "nm0")}
-        nw = {0: tile([P, N], F32, "nw0")}
+        columns(first)
+        scalar_scatter(w_new[first], nw[first], one[:])
+        store_w(first)
+        scalar_scatter(m_new[first], nm[first], one[:])
+        round_plane(first, 1.0)
+        columns(second)
+        scalar_scatter(w_new[second], nw[second], one[:])
+        vector_scatter(second)
+        store_m(first)
+        store_w(second)
+        columns(third)
+        scalar_scatter(w_new[third], nw[third], one[:])
+        store_w(third)
+        m_new[third] = at(112 * KIB, [P, T], F32, "m_new_third")
+        nc.vector.tensor_copy(m_new[third][:], m_src[third][:])
+        one_late = at((64 + 8 * third) * KIB, [P, 1], F32, "one_late")
+        nc.gpsimd.memset(one_late[:], 1.0)
+        round_plane(second, one_late[:])
+        round_plane(third, one_late[:], slice(0, SPLIT))
+        one_last = at((64 + 8 * third) * KIB, [P, 1], F32, "one_last")
+        nc.gpsimd.memset(one_last[:], 1.0)
+        columns(last)
+        nc.vector.tensor_copy(w_new[last][:].indirect(offsets[:]), nw[last][:])
+        store_w(last)
+        scalar_scatter(m_new[third], nm[third], one[:])
+        store_m(third)
+        m_new[last] = at(120 * KIB, [P, T], F32, "m_new_last")
+        nc.vector.tensor_copy(m_new[last][:], m_src[last][:])
+        scalar_scatter(m_new[last], nm[last], one[:])
+        store_m(last)
         for h in range(2):
-            make_g(h)
-        dw = []
-        for h in range(2):
-            quantise_g(h)
-            if h == 0:
-                quantise_xm(0, 2)
-            dw.append(product(0, parts[h], bank(("dw", "dw3")[h])))
-        for h in range(2):
-            nc.vector.tensor_copy(m_g[:, parts[h]], m_win[0].indirect(halves[h]))
-        for h in range(2):
-            new_m(0, m_g[:, parts[h]], nm[0], dw[h], h)
-        for h in range(2):
-            new_w(0, nm[0], nw[0], h)
-            scalar_scatter(w_new[0], nw[0], h)
-        xm_bf[2] = late.tile([P, 2 * LANES * P], BF16, name="xm_bf2", offset=18 * KIB, align_bytes=64)
-        round_xm(2, 2, nc.vector.tensor_copy)
-        for h in range(2):
-            scalar_scatter(m_new[0], nm[0], h)
-        store_w(0)
-        store_m(0)
-
-        def place(t):
-            return pairs[:, t // 2 * 2 * T:(t // 2 + 1) * 2 * T].rearrange("p (c e) -> p c e", e=2)[:, :, t % 2]
-
-        def round_plane(t):
-            nc.gpsimd.tensor_scalar(place(t)[:, :BODY], w_new[t][:, :BODY], 1.0, -0.0, MULT, ADD)
-
-        def gather_m(t, m_g, h):
-            nc.vector.tensor_copy(m_g[h], m_win[t].indirect(halves[h]))
-
-        def halved(columns):
-            return [columns[:, parts[h]] for h in range(2)]
-
-        def momentum(t, m_g, dw, tag):
-            nm[t] = tile([P, N], F32, "nm%d" % t, tag=tag)
-            product(t, slice(0, N), dw)
-            for h in range(2):
-                new_m(t, m_g[h], nm[t], dw[:, parts[h]], h)
-
-        def weights(t, columns):
-            nw[t] = columns
-            for h in range(2):
-                new_w(t, nm[t], nw[t], h)
-
-        m_g = halved(late.tile([P, N], F32, name="m_g1", offset=20 * KIB))
-        nc.vector.tensor_copy(m_new[1][:, SPLIT:], m_src[1][:, SPLIT:])
-        for h in range(2):
-            gather_m(1, m_g, h)
-        momentum(1, m_g, bank("dw"), None)
-        weights(1, tile([P, N], F32, "nw1"))
-        xm_q[2] = late.tile([P, D // 2], U32, name="xm_q2", offset=20 * KIB, align_bytes=64)
-        quantise_xm(2, 2)
-        round_plane(0)
-        m_g2 = [late.tile([P, HALF], F32, name="m_g2", offset=21 * KIB)[:]]
-        gather_m(2, m_g2, 0)
-        nc.vector.tensor_copy(w_new[1][:].indirect(offsets[:]), nw[1][:])
-        store_w(1)
-        round_plane(1)
-        for h in range(2):
-            scalar_scatter(m_new[1], nm[1], h)
-        store_m(1)
-        m_g2.append(tile([P, HALF], F32, "later", tag="nw1")[:])
-        m_g3 = late.tile([P, N], F32, name="m_g3", offset=21 * KIB + 512)[:]
-        gather_m(2, m_g2, 1)
-        momentum(2, m_g2, bank("dw"), "z00")
-        for h in range(2):
-            scalar_scatter(m_new[2], nm[2], h)
-        store_m(2)
-        nc.vector.tensor_scalar(m_g3, m_win[3].indirect(offsets[:]), -LR * BETA, 0.0, MULT, ADD)
-        dw = product(3, slice(0, N), bank("dw3"))
-        step = tile([P, N], F32, "step", tag="z10")
-        for h in range(2):
-            nc.vector.scalar_tensor_tensor(step[:, parts[h]], dw[:, parts[h]], -LR, m_g3[:, parts[h]], MULT, ADD)
-        short = late.tile([P, N - SHARE], F32, name="short", offset=21 * KIB + 256)
-        nc.vector.tensor_scalar(short[:], nm[2][:, SHARE:], -LR, 0.0, MULT, ADD)
-        nw[2] = late.tile([P, SHARE], F32, name="nw2", offset=21 * KIB + 768)
-        nc.vector.scalar_tensor_tensor(nw[2][:], nm[2][:, :SHARE], -LR, w_g[1][:, 0, :SHARE], MULT, ADD)
-        nc.vector.tensor_tensor(w_new[2][:].indirect(offsets[:, SHARE // 16:]), w_g[1][:, 0, SHARE:], short[:], ADD)
-        nc.scalar.activation(w_new[2][:].indirect(offsets[:, :SHARE // 16]), nw[2][:], COPY)
-        m_new[3] = late.tile([P, T], F32, name="m_new3", offset=23 * KIB + 256)
-        nc.vector.tensor_copy(m_new[3][:], m_win[3])
-        nc.vector.tensor_tensor(w_new[3][:].indirect(offsets[:]), w_g[1][:, 1, :], step[:], ADD)
-        for h in range(2):
-            scalar_scatter(m_new[3], step, h, -1.0 / LR)
-        store_w(2)
-        store_w(3)
-        store_m(3)
-        tail = late.tile([P, LANES * TAIL], BF16, name="tail", offset=19 * KIB + 768)
-        tail_place = tail[:].rearrange("p (u c e) -> p u c e", u=2, e=2)
-        for cols in (slice(0, T // 2), slice(T // 2, BODY)):
-            for t in (3, 2):
-                nc.vector.tensor_copy(place(t)[:, cols], w_new[t][:, cols])
-        for t in range(LANES):
-            nc.vector.tensor_copy(tail_place[:, t // 2, :, t % 2], w_new[t][:, BODY:])
+            cols = slice(h * T // 2, (h + 1) * T // 2)
+            nc.vector.tensor_scalar(place(last)[:, cols], w_new[last][:, cols], one_last[:], -0.0, MULT, ADD)
+        nc.vector.tensor_scalar(place(third)[:, SPLIT:], w_new[third][:, SPLIT:], one_last[:], -0.0, MULT, ADD)
 
         words = pairs[:].bitcast(U32).rearrange("p (u c) -> p u c", u=2)
-        o_s = tile([P, T], U8, "o_s")
-        o_q = tile([P, T], U32, "o_q", tag="xm_raw")
+        o_s = at(212 * KIB, [P, T], U8, "o_s")
+        o_q = at(145 * KIB, [P, T], U32, "o_q")
         words_hbm = out_2[0].rearrange("p c l -> p (c l)").bitcast(I32)
-        pieces = [(512, nc.scalar.copy), (512, nc.scalar.copy), (512, nc.vector.tensor_copy), (256, nc.scalar.copy), (256, nc.scalar.copy)]
+        pieces = [(512, nc.vector.tensor_copy), (512, nc.vector.tensor_copy), (512, nc.scalar.copy), (256, nc.scalar.copy), (256, nc.scalar.copy)]
         woven = []
         start = 0
         for k, (width, copy) in enumerate(pieces):
             cols = slice(start, start + width)
-            o_bf = tile([P, width * LANES], BF16, "o_bf%d" % k, tag=("w_src0", "w_src1", "w_src2", "w_src3", "m_src0")[k])
-            copy(o_bf[:].bitcast(U32).rearrange("p (c u) -> p c u", u=2), (words[:, :, cols] if cols.stop <= BODY else tail[:].bitcast(U32).rearrange("p (u c) -> p u c", u=2)).rearrange("p u c -> p c u"))
+            o_bf = at(16 * KIB + 8 * start, [P, width * LANES], BF16, "o_bf%d" % k)
+            copy(o_bf[:].bitcast(U32).rearrange("p (c u) -> p c u", u=2), words[:, :, cols].rearrange("p u c -> p c u"))
             woven.append((cols, o_bf))
             start = cols.stop
         stored = 0

@@ -67,11 +67,13 @@ def tile_attend_gsig_pl_mom_kernel(tc, xT, wT, y, wt, xm, mT, offs, out_0, out_1
         xm_raw = at(145 * KIB, [P, LANES, D], F32, "xm_raw")
         nc.sync.dma_start(xm_raw[:], planes(xm[0]))
         m_src = {t: at((64 + 8 * t) * KIB, [P, T], F32, "m_src%d" % t) for t in ORDER}
-        m_new = {second: at(104 * KIB, [P, T], F32, "m_new_second")}
+        m_new = {second: at(104 * KIB, [P, T], F32, "m_new_second"), third: at(112 * KIB, [P, T], F32, "m_new_third")}
         for t in ORDER:
+            if t == third:
+                nc.sync.dma_start(m_new[t][:], m_hbm[:, t, :])
             nc.sync.dma_start(m_src[t][:], m_hbm[:, t, :])
             if t == second:
-                nc.sync.dma_start(m_new[t][:], m_hbm[:, t, :])
+                nc.sync.dma_start(m_new[t][:, :T // 2], m_hbm[:, t, :T // 2])
 
         warm = sb.tile([P, 1], F32, name="warm")
         nc.gpsimd.memset(warm[:], 0.0)
@@ -95,7 +97,7 @@ def tile_attend_gsig_pl_mom_kernel(tc, xT, wT, y, wt, xm, mT, offs, out_0, out_1
                 nc.tensor.transpose(dst[:, b * P:(b + 1) * P], src[:, b * P:(b + 1) * P], ident[:])
 
         def park(t):
-            turned = at((129 + 2 * t) * KIB, [P, N], F32, "turned%d" % t)
+            turned = at(129 * KIB, [P, N], F32, "turned%d" % t)
             nc.scalar.copy(turned[:], once[t][:])
             parked[t] = bank("parked%d" % t, 1)
             turn(parked[t], turned)
@@ -103,8 +105,8 @@ def tile_attend_gsig_pl_mom_kernel(tc, xT, wT, y, wt, xm, mT, offs, out_0, out_1
         for t in range(LANES - 1):
             nc.vector.tensor_copy(w_g[t // 2][:, t % 2, :], w_src[t][:].indirect(offsets[:]))
             nc.scalar.activation(w_new[t][:], w_src[t][:], COPY)
-            if t < 2:
-                once[t] = bank("once", 2)
+            if t == last:
+                once[t] = bank("once", 1)
                 turn(once[t], w_g[0][:, t, :])
             if t == 1:
                 for h in range(2):
@@ -162,8 +164,7 @@ def tile_attend_gsig_pl_mom_kernel(tc, xT, wT, y, wt, xm, mT, offs, out_0, out_1
         for h in range(2):
             for k in range(2):
                 score(h, k)
-        for t in range(2):
-            park(t)
+        park(last)
         for h in range(2):
             for k in range(2):
                 weigh(h, k)
@@ -175,8 +176,12 @@ def tile_attend_gsig_pl_mom_kernel(tc, xT, wT, y, wt, xm, mT, offs, out_0, out_1
         g_bf = [at((197 + 2 * h) * KIB, [P, HALF * LANES], BF16, "g_bf%d" % h) for h in range(2)]
         g_q = at(207 * KIB, [P, N], U32, "g_q")
         g_s = at(210 * KIB + 512, [P, N], U8, "g_s")
-        for k in (1, 0):
-            deal(xm_bf[k], xm_raw, k, nc.scalar.copy)
+        deal(xm_bf[1], xm_raw, 1, nc.scalar.copy)
+        m_first = at(185 * KIB, [P, N], F32, "m_g_first")
+        nc.scalar.activation(m_first[:, parts[1]], m_src[first][:].indirect(halves[1]), COPY)
+        deal(xm_bf[0], xm_raw, 0, nc.scalar.copy)
+        m_new[first] = at(222 * KIB - 128, [P, T], F32, "m_new_first")
+        nc.scalar.activation(m_new[first][:, :SPLIT], m_src[first][:, :SPLIT], COPY)
         for h in range(2):
             nc.vector.tensor_tensor(
                 g_bf[h][:].rearrange("p (c i t) -> p c t i", i=4, t=LANES),
@@ -193,12 +198,10 @@ def tile_attend_gsig_pl_mom_kernel(tc, xT, wT, y, wt, xm, mT, offs, out_0, out_1
         quantise_xm(1)
         nc.vector.quantize_mx(g_q[:, parts[1]].bitcast(E5M2), g_s[:, parts[1]], g_bf[1][:])
         quantise_xm(0)
-        m_new[first] = at(222 * KIB - 128, [P, T], F32, "m_new_first")
-        nc.scalar.activation(m_new[first][:], m_src[first][:], COPY)
 
         nm, nw = {}, {}
-        m_g_at = {first: 185 * KIB, second: 187 * KIB, third: 112 * KIB, last: 189 * KIB}
-        nw_at = {first: 137 * KIB, second: 139 * KIB, third: 141 * KIB, last: 120 * KIB}
+        m_g_at = {first: 185 * KIB, second: 187 * KIB, third: 193 * KIB, last: 120 * KIB}
+        nw_at = {first: 137 * KIB, second: 139 * KIB, third: 141 * KIB, last: 189 * KIB}
         pairs = at(0, [P, 4 * T], BF16, "pairs")
 
         def place(t):
@@ -211,16 +214,21 @@ def tile_attend_gsig_pl_mom_kernel(tc, xT, wT, y, wt, xm, mT, offs, out_0, out_1
             cols = slice(t * P, (t + 1) * P)
             dw = bank("sum", 4)
             nc.tensor.matmul_mx(dw[:], xm_q[:, cols].bitcast(E4M3), xm_s[:, cols], g_q[:].bitcast(E5M2), g_s[:], start=True, stop=True)
-            m_g = at(m_g_at[t], [P, N], F32, "m_g%d" % t)
+            m_g = m_first if t == first else at(m_g_at[t], [P, N], F32, "m_g%d" % t)
             nm[t] = at((129 + 2 * t) * KIB, [P, N], F32, "nm%d" % t)
             nw[t] = at(nw_at[t], [P, N], F32, "nw%d" % t)
             old = parked[t][:] if t in parked else w_g[t // 2][:, t % 2, :]
-            for h in range(2):
+            for h in range(1 if t == first else 2):
                 nc.vector.tensor_copy(m_g[:, parts[h]], m_src[t][:].indirect(halves[h]))
             for h in range(2):
                 nc.vector.scalar_tensor_tensor(nm[t][:, parts[h]], m_g[:, parts[h]], BETA, dw[:, parts[h]], MULT, ADD)
-            for h in range(2):
-                nc.vector.scalar_tensor_tensor(nw[t][:, parts[h]], nm[t][:, parts[h]], -LR, old[:, parts[h]], MULT, ADD)
+            if t in (second, third):
+                step = at(143 * KIB, [P, N], F32, "step%d" % t)
+                nc.gpsimd.tensor_scalar(step[:], nm[t][:], -LR, -0.0, MULT, ADD)
+                nc.gpsimd.tensor_tensor(nw[t][:], step[:], old, ADD)
+            else:
+                for h in range(2):
+                    nc.vector.scalar_tensor_tensor(nw[t][:, parts[h]], nm[t][:, parts[h]], -LR, old[:, parts[h]], MULT, ADD)
 
         def scalar_scatter(window, values, unit):
             nc.scalar.activation(window[:].indirect(offsets[:]), values[:], COPY, scale=unit)
@@ -238,43 +246,46 @@ def tile_attend_gsig_pl_mom_kernel(tc, xT, wT, y, wt, xm, mT, offs, out_0, out_1
         columns(first)
         scalar_scatter(w_new[first], nw[first], one[:])
         store_w(first)
+        nc.vector.tensor_copy(m_new[first][:, SPLIT:], m_src[first][:, SPLIT:])
         scalar_scatter(m_new[first], nm[first], one[:])
-        round_plane(first, 1.0)
+        nc.vector.tensor_copy(m_new[second][:, T // 2:], m_src[second][:, T // 2:])
         columns(second)
+        one_first = at(181 * KIB, [P, 1], F32, "one_first")
+        nc.gpsimd.memset(one_first[:], 1.0)
+        round_plane(first, one_first[:], slice(0, SPLIT))
         scalar_scatter(w_new[second], nw[second], one[:])
         vector_scatter(second)
         store_m(first)
         store_w(second)
         columns(third)
+        nc.vector.tensor_copy(m_new[third][:].indirect(halves[0]), nm[third][:, parts[0]])
+        nc.scalar.activation(m_new[third][:].indirect(halves[1]), nm[third][:, parts[1]], COPY)
+        store_m(third)
         scalar_scatter(w_new[third], nw[third], one[:])
         store_w(third)
-        m_new[third] = at(112 * KIB, [P, T], F32, "m_new_third")
-        nc.vector.tensor_copy(m_new[third][:], m_src[third][:])
-        one_late = at((64 + 8 * third) * KIB, [P, 1], F32, "one_late")
-        nc.gpsimd.memset(one_late[:], 1.0)
-        round_plane(second, one_late[:])
-        round_plane(third, one_late[:], slice(0, SPLIT))
-        one_last = at((64 + 8 * third) * KIB, [P, 1], F32, "one_last")
-        nc.gpsimd.memset(one_last[:], 1.0)
+        one_second = at(177 * KIB, [P, 1], F32, "one_second")
+        nc.gpsimd.memset(one_second[:], 1.0)
+        round_plane(first, one_second[:], slice(SPLIT, T))
         columns(last)
-        nc.vector.tensor_copy(w_new[last][:].indirect(offsets[:]), nw[last][:])
-        store_w(last)
-        scalar_scatter(m_new[third], nm[third], one[:])
-        store_m(third)
         m_new[last] = at(120 * KIB, [P, T], F32, "m_new_last")
         nc.vector.tensor_copy(m_new[last][:], m_src[last][:])
+        nc.vector.tensor_copy(w_new[last][:].indirect(offsets[:]), nw[last][:])
+        store_w(last)
+        one_late = at((64 + 8 * last) * KIB, [P, 1], F32, "one_late")
+        nc.gpsimd.memset(one_late[:], 1.0)
+        round_plane(second, one_late[:], slice(0, SPLIT))
         scalar_scatter(m_new[last], nm[last], one[:])
         store_m(last)
-        for h in range(2):
-            cols = slice(h * T // 2, (h + 1) * T // 2)
-            nc.vector.tensor_scalar(place(last)[:, cols], w_new[last][:, cols], one_last[:], -0.0, MULT, ADD)
-        nc.vector.tensor_scalar(place(third)[:, SPLIT:], w_new[third][:, SPLIT:], one_last[:], -0.0, MULT, ADD)
+        for cols in (slice(0, T // 2), slice(T // 2, T)):
+            nc.vector.tensor_scalar(place(third)[:, cols], w_new[third][:, cols], one_late[:], -0.0, MULT, ADD)
+            nc.vector.tensor_copy(place(last)[:, cols], w_new[last][:, cols])
+        nc.vector.tensor_scalar(place(second)[:, SPLIT:], w_new[second][:, SPLIT:], one_late[:], -0.0, MULT, ADD)
 
         words = pairs[:].bitcast(U32).rearrange("p (u c) -> p u c", u=2)
         o_s = at(212 * KIB, [P, T], U8, "o_s")
         o_q = at(145 * KIB, [P, T], U32, "o_q")
         words_hbm = out_2[0].rearrange("p c l -> p (c l)").bitcast(I32)
-        pieces = [(512, nc.vector.tensor_copy), (512, nc.vector.tensor_copy), (512, nc.scalar.copy), (256, nc.scalar.copy), (256, nc.scalar.copy)]
+        pieces = [(512, nc.scalar.copy), (512, nc.scalar.copy), (256, nc.vector.tensor_copy), (512, nc.scalar.copy), (256, nc.scalar.copy)]
         woven = []
         start = 0
         for k, (width, copy) in enumerate(pieces):

@@ -67,13 +67,14 @@ def tile_attend_gsig_pl_mom_kernel(tc, xT, wT, y, wt, xm, mT, offs, out_0, out_1
         xm_raw = at(145 * KIB, [P, LANES, D], F32, "xm_raw")
         nc.sync.dma_start(xm_raw[:], planes(xm[0]))
         m_src = {t: at((64 + 8 * t) * KIB, [P, T], F32, "m_src%d" % t) for t in ORDER}
-        m_new = {second: at(104 * KIB, [P, T], F32, "m_new_second"), third: at(112 * KIB, [P, T], F32, "m_new_third")}
+        m_new = {t: at((96 + 8 * k) * KIB, [P, T], F32, "m_new%d" % t) for k, t in enumerate((first, second, third))}
         for t in ORDER:
             if t == third:
                 nc.sync.dma_start(m_new[t][:], m_hbm[:, t, :])
             nc.sync.dma_start(m_src[t][:], m_hbm[:, t, :])
             if t == second:
-                nc.sync.dma_start(m_new[t][:, :T // 2], m_hbm[:, t, :T // 2])
+                nc.sync.dma_start(m_new[first][:, SPLIT:], m_hbm[:, first, SPLIT:])
+                nc.sync.dma_start(m_new[t][:, SPLIT:], m_hbm[:, t, SPLIT:])
 
         warm = sb.tile([P, 1], F32, name="warm")
         nc.gpsimd.memset(warm[:], 0.0)
@@ -97,7 +98,7 @@ def tile_attend_gsig_pl_mom_kernel(tc, xT, wT, y, wt, xm, mT, offs, out_0, out_1
                 nc.tensor.transpose(dst[:, b * P:(b + 1) * P], src[:, b * P:(b + 1) * P], ident[:])
 
         def park(t):
-            turned = at(129 * KIB, [P, N], F32, "turned%d" % t)
+            turned = at((129 if t == last else 133) * KIB, [P, N], F32, "turned%d" % t)
             nc.scalar.copy(turned[:], once[t][:])
             parked[t] = bank("parked%d" % t, 1)
             turn(parked[t], turned)
@@ -105,9 +106,9 @@ def tile_attend_gsig_pl_mom_kernel(tc, xT, wT, y, wt, xm, mT, offs, out_0, out_1
         for t in range(LANES - 1):
             nc.vector.tensor_copy(w_g[t // 2][:, t % 2, :], w_src[t][:].indirect(offsets[:]))
             nc.scalar.activation(w_new[t][:], w_src[t][:], COPY)
-            if t == last:
-                once[t] = bank("once", 1)
-                turn(once[t], w_g[0][:, t, :])
+            if t in (first, last):
+                once[t] = bank("once", 2)
+                turn(once[t], w_g[t // 2][:, t % 2, :])
             if t == 1:
                 for h in range(2):
                     round_pair(0, h)
@@ -164,23 +165,22 @@ def tile_attend_gsig_pl_mom_kernel(tc, xT, wT, y, wt, xm, mT, offs, out_0, out_1
         for h in range(2):
             for k in range(2):
                 score(h, k)
+        park(first)
         park(last)
         for h in range(2):
             for k in range(2):
                 weigh(h, k)
 
-        xm_both = at(216 * KIB, [P, D * 4], BF16, "xm_both")
-        xm_bf = [xm_both[:, 2 * D * k:2 * D * (k + 1)] for k in range(2)]
-        xm_q = at(205 * KIB, [P, D], U32, "xm_q")
+        xm_bf = {1: at(218 * KIB, [P, D * 2], BF16, "xm_bf1")[:]}
+        xm_q = {}
         xm_s = at(210 * KIB, [P, D], U8, "xm_s")
         g_bf = [at((197 + 2 * h) * KIB, [P, HALF * LANES], BF16, "g_bf%d" % h) for h in range(2)]
         g_q = at(207 * KIB, [P, N], U32, "g_q")
         g_s = at(210 * KIB + 512, [P, N], U8, "g_s")
         deal(xm_bf[1], xm_raw, 1, nc.scalar.copy)
         m_first = at(185 * KIB, [P, N], F32, "m_g_first")
-        nc.scalar.activation(m_first[:, parts[1]], m_src[first][:].indirect(halves[1]), COPY)
-        deal(xm_bf[0], xm_raw, 0, nc.scalar.copy)
-        m_new[first] = at(222 * KIB - 128, [P, T], F32, "m_new_first")
+        for h in range(2):
+            nc.scalar.activation(m_first[:, parts[h]], m_src[first][:].indirect(halves[h]), COPY)
         nc.scalar.activation(m_new[first][:, :SPLIT], m_src[first][:, :SPLIT], COPY)
         for h in range(2):
             nc.vector.tensor_tensor(
@@ -192,12 +192,18 @@ def tile_attend_gsig_pl_mom_kernel(tc, xT, wT, y, wt, xm, mT, offs, out_0, out_1
 
         def quantise_xm(k):
             cols = slice(2 * k * P, (2 * k + 2) * P)
-            nc.vector.quantize_mx(xm_q[:, cols].bitcast(E4M3), xm_s[:, cols], xm_bf[k])
+            xm_q[k] = at(205 * KIB if k == 1 else (64 + 8 * second) * KIB, [P, D // 2], U32, "xm_q%d" % k)
+            nc.vector.quantize_mx(xm_q[k][:].bitcast(E4M3), xm_s[:, cols], xm_bf[k])
 
         nc.vector.quantize_mx(g_q[:, parts[0]].bitcast(E5M2), g_s[:, parts[0]], g_bf[0][:])
         quantise_xm(1)
         nc.vector.quantize_mx(g_q[:, parts[1]].bitcast(E5M2), g_s[:, parts[1]], g_bf[1][:])
-        quantise_xm(0)
+        xm_bf[0] = at(199 * KIB, [P, D * 2], BF16, "xm_bf0")[:]
+        nc.gpsimd.tensor_scalar(
+            xm_bf[0].rearrange("p (t m j) -> p t m j", t=2, j=LANES),
+            xm_raw[:].rearrange("p j (m t) -> p t m j", t=LANES)[:, 0:2, :, :],
+            1.0, -0.0, MULT, ADD,
+        )
 
         nm, nw = {}, {}
         m_g_at = {first: 185 * KIB, second: 187 * KIB, third: 193 * KIB, last: 120 * KIB}
@@ -212,16 +218,23 @@ def tile_attend_gsig_pl_mom_kernel(tc, xT, wT, y, wt, xm, mT, offs, out_0, out_1
 
         def columns(t):
             cols = slice(t * P, (t + 1) * P)
-            dw = bank("sum", 4)
-            nc.tensor.matmul_mx(dw[:], xm_q[:, cols].bitcast(E4M3), xm_s[:, cols], g_q[:].bitcast(E5M2), g_s[:], start=True, stop=True)
+            dw = [bank("sum", 4) for cut in (parts if t == first else parts[:1])]
+            for k, cut in enumerate(parts if t == first else [slice(0, N)]):
+                nc.tensor.matmul_mx(dw[k][:, cut], xm_q[t // 2][:, t % 2 * P:(t % 2 + 1) * P].bitcast(E4M3), xm_s[:, cols], g_q[:, cut].bitcast(E5M2), g_s[:, cut], start=True, stop=True)
             m_g = m_first if t == first else at(m_g_at[t], [P, N], F32, "m_g%d" % t)
             nm[t] = at((129 + 2 * t) * KIB, [P, N], F32, "nm%d" % t)
             nw[t] = at(nw_at[t], [P, N], F32, "nw%d" % t)
             old = parked[t][:] if t in parked else w_g[t // 2][:, t % 2, :]
-            for h in range(1 if t == first else 2):
-                nc.vector.tensor_copy(m_g[:, parts[h]], m_src[t][:].indirect(halves[h]))
-            for h in range(2):
-                nc.vector.scalar_tensor_tensor(nm[t][:, parts[h]], m_g[:, parts[h]], BETA, dw[:, parts[h]], MULT, ADD)
+            if t == second:
+                nc.vector.tensor_copy(m_g[:], m_src[t][:].indirect(offsets[:]))
+                nc.vector.tensor_copy(m_new[t][:, :SPLIT], m_src[t][:, :SPLIT])
+                nc.vector.scalar_tensor_tensor(nm[t][:], m_g[:], BETA, dw[0][:], MULT, ADD)
+                quantise_xm(0)
+            else:
+                for h in range(0 if t == first else 2):
+                    nc.vector.tensor_copy(m_g[:, parts[h]], m_src[t][:].indirect(halves[h]))
+                for h in range(2):
+                    nc.vector.scalar_tensor_tensor(nm[t][:, parts[h]], m_g[:, parts[h]], BETA, dw[h % len(dw)][:, parts[h]], MULT, ADD)
             if t in (second, third):
                 step = at(143 * KIB, [P, N], F32, "step%d" % t)
                 nc.gpsimd.tensor_scalar(step[:], nm[t][:], -LR, -0.0, MULT, ADD)
@@ -246,10 +259,8 @@ def tile_attend_gsig_pl_mom_kernel(tc, xT, wT, y, wt, xm, mT, offs, out_0, out_1
         columns(first)
         scalar_scatter(w_new[first], nw[first], one[:])
         store_w(first)
-        nc.vector.tensor_copy(m_new[first][:, SPLIT:], m_src[first][:, SPLIT:])
-        scalar_scatter(m_new[first], nm[first], one[:])
-        nc.vector.tensor_copy(m_new[second][:, T // 2:], m_src[second][:, T // 2:])
         columns(second)
+        scalar_scatter(m_new[first], nm[first], one[:])
         one_first = at(181 * KIB, [P, 1], F32, "one_first")
         nc.gpsimd.memset(one_first[:], 1.0)
         round_plane(first, one_first[:], slice(0, SPLIT))

@@ -27,6 +27,7 @@ HALF = N // 2
 KIB = 1024
 ORDER = (2, 3, 0, 1)
 SPLIT = 3 * T // 4
+BAND = T // 4
 
 
 def tile_attend_gsig_pl_mom_kernel(tc, xT, wT, y, wt, xm, mT, offs, out_0, out_1, out_2, out_3):
@@ -293,10 +294,10 @@ def tile_attend_gsig_pl_mom_kernel(tc, xT, wT, y, wt, xm, mT, offs, out_0, out_1
         nc.vector.tensor_scalar(place(second)[:, SPLIT:], w_new[second][:, SPLIT:], one_late[:], -0.0, MULT, ADD)
 
         words = pairs[:].bitcast(U32).rearrange("p (u c) -> p u c", u=2)
-        o_s = at(212 * KIB, [P, T], U8, "o_s")
+        o_s = at(212 * KIB, [P, BAND], U8, "o_s")
         o_q = at(145 * KIB, [P, T], U32, "o_q")
         words_hbm = out_2[0].rearrange("p c l -> p (c l)").bitcast(I32)
-        pieces = [(512, nc.scalar.copy), (512, nc.scalar.copy), (256, nc.vector.tensor_copy), (512, nc.scalar.copy), (256, nc.scalar.copy)]
+        pieces = [(512, nc.scalar.copy), (512, nc.scalar.copy), (256, nc.vector.tensor_copy), (256, nc.scalar.copy), (256, nc.scalar.copy), (256, nc.scalar.copy)]
         woven = []
         start = 0
         for k, (width, copy) in enumerate(pieces):
@@ -307,10 +308,11 @@ def tile_attend_gsig_pl_mom_kernel(tc, xT, wT, y, wt, xm, mT, offs, out_0, out_1
             start = cols.stop
         stored = 0
         for k, (cols, o_bf) in enumerate(woven):
-            nc.vector.quantize_mx(o_q[:, cols].bitcast(E4M3), o_s[:, cols], o_bf[:])
-            if k in (1, 3, 4):
+            band, inside = divmod(cols.start, BAND)
+            nc.vector.quantize_mx(o_q[:, cols].bitcast(E4M3), o_s[4 * band:, inside:inside + cols.stop - cols.start], o_bf[:])
+            if k in (1, 4, 5):
                 nc.sync.dma_start(words_hbm[:, stored:cols.stop], o_q[:, stored:cols.stop].bitcast(I32))
                 stored = cols.stop
         scales_hbm = out_3[0].bitcast(I32)
         for q in range(4):
-            nc.sync.dma_start(scales_hbm[4 * q:4 * q + 4, :], o_s[32 * q:32 * q + 4, :].bitcast(I32))
+            nc.sync.dma_start(scales_hbm[4 * q:4 * q + 4, :].rearrange("r (b c) -> b r c", b=4), o_s[32 * q:32 * q + 16, :].bitcast(I32))

from contextlib import ExitStack

import concourse.mybir as mybir
from concourse.masks import make_identity

F32 = mybir.dt.float32
BF16 = mybir.dt.bfloat16
I32 = mybir.dt.int32
U32 = mybir.dt.uint32
U16 = mybir.dt.uint16
U8 = mybir.dt.uint8
E4M3 = mybir.dt.float8_e4m3fn_x4
E5M2 = mybir.dt.float8_e5m2_x4
MULT = mybir.AluOpType.mult
ADD = mybir.AluOpType.add
COPY = mybir.ActivationFunctionType.Copy
SIGMOID = mybir.ActivationFunctionType.Sigmoid

P = 128
LANES = 4
N, T, D, R = 512, 2048, 512, 512
LR = 0.1
BETA = 0.9
FLOPS = 2 * 2 * D * R * N

HALF = N // 2
KIB = 1024
ORDER = (2, 3, 0, 1)
SPLIT = 3 * T // 4
BAND = T // 4


def tile_attend_gsig_pl_mom_kernel(tc, xT, wT, y, wt, xm, mT, offs, out_0, out_1, out_2, out_3):
    nc = tc.nc
    with ExitStack() as ctx:
        sb = ctx.enter_context(tc.tile_pool(name="sb", bufs=1))
        mem = ctx.enter_context(tc.tile_pool(name="mem", bufs=1))
        ps = ctx.enter_context(tc.psum_pool(name="ps", bufs=1))

        def at(offset, shape, dtype, name):
            return mem.tile(shape, dtype, name=name, offset=offset, align_bytes=64)

        def bank(tag, bufs):
            return ps.tile([P, 512], F32, name=tag, tag=tag, bufs=bufs)

        def planes(table):
            return table.rearrange("(p t) c -> p t c", t=LANES)

        w_hbm, m_hbm, o0_hbm, o1_hbm = planes(wT), planes(mT), planes(out_0), planes(out_1)
        parts = [slice(h * HALF, (h + 1) * HALF) for h in range(2)]
        first, second, third, last = ORDER

        offsets = sb.tile([P, N // 16], U16, name="offsets")
        halves = [offsets[:, h * (HALF // 16):(h + 1) * (HALF // 16)] for h in range(2)]
        wt_sb = sb.tile([P, LANES], F32, name="wt_sb")
        w_src = [at(8 * KIB * t, [P, T], F32, "w_src%d" % t) for t in range(LANES)]
        for t in range(LANES):
            nc.sync.dma_start(w_src[t][:], w_hbm[:, t, :])
            if t == 0:
                nc.sync.dma_start(offsets[:], offs)
            if t == 1:
                nc.sync.dma_start(wt_sb[:], wt[0].rearrange("(p t) o -> p (t o)", t=LANES))
        x_raw = at(129 * KIB, [P, LANES, R], F32, "x_raw")
        nc.sync.dma_start(x_raw[:], planes(xT[0]))
        y_sb = [at((137 + 4 * k) * KIB, [P, 2, N], F32, "y_sb%d" % k) for k in range(2)]
        for k in range(2):
            nc.sync.dma_start(y_sb[k][:], planes(y[0])[:, 2 * k:2 * k + 2, :])
        xm_raw = at(145 * KIB, [P, LANES, D], F32, "xm_raw")
        nc.sync.dma_start(xm_raw[:], planes(xm[0]))
        m_src = {t: at((64 + 8 * t) * KIB, [P, T], F32, "m_src%d" % t) for t in ORDER}
        m_new = {t: at((96 + 8 * k) * KIB, [P, T], F32, "m_new%d" % t) for k, t in enumerate((first, second, third))}
        for t in ORDER:
            if t == third:
                nc.sync.dma_start(m_new[t][:], m_hbm[:, t, :])
            nc.sync.dma_start(m_src[t][:], m_hbm[:, t, :])
            if t == second:
                nc.sync.dma_start(m_new[first][:, SPLIT:], m_hbm[:, first, SPLIT:])
                nc.sync.dma_start(m_new[t][:, SPLIT:], m_hbm[:, t, SPLIT:])

        warm = sb.tile([P, 1], F32, name="warm")
        nc.gpsimd.memset(warm[:], 0.0)
        nc.scalar.activation(warm[:], warm[:], SIGMOID)
        one = sb.tile([P, 1], F32, name="one")
        nc.gpsimd.memset(one[:], 1.0)
        ident = at(211 * KIB, [P, P], F32, "ident")
        make_identity(nc, ident[:])

        w_new = [at((32 + 8 * t) * KIB, [P, T], F32, "w_new%d" % t) for t in range(LANES)]
        w_g = [at((177 + 4 * k) * KIB, [P, 2, N], F32, "w_g%d" % k) for k in range(2)]
        w_bf = [at((185 + 2 * h) * KIB, [P, HALF * LANES], BF16, "w_bf%d" % h) for h in range(2)]
        w_view = [w_bf[h][:].rearrange("p (c t) -> p c t", t=LANES) for h in range(2)]
        once, parked = {}, {}

        def round_pair(k, h):
            nc.vector.tensor_copy(w_view[h][:, :, 2 * k:2 * k + 2], w_g[k][:, :, parts[h]].rearrange("p t c -> p c t"))

        def turn(dst, src):
            for b in range(N // P):
                nc.tensor.transpose(dst[:, b * P:(b + 1) * P], src[:, b * P:(b + 1) * P], ident[:])

        def park(t):
            turned = at((129 if t == last else 133) * KIB, [P, N], F32, "turned%d" % t)
            nc.scalar.copy(turned[:], once[t][:])
            parked[t] = bank("parked%d" % t, 1)
            turn(parked[t], turned)

        for t in range(LANES - 1):
            nc.vector.tensor_copy(w_g[t // 2][:, t % 2, :], w_src[t][:].indirect(offsets[:]))
            nc.scalar.activation(w_new[t][:], w_src[t][:], COPY)
            if t in (first, last):
                once[t] = bank("once", 2)
                turn(once[t], w_g[t // 2][:, t % 2, :])
            if t == 1:
                for h in range(2):
                    round_pair(0, h)
        for h in range(2):
            nc.vector.tensor_copy(w_g[1][:, 1, parts[h]], w_src[3][:].indirect(halves[h]))
        nc.scalar.activation(w_new[3][:], w_src[3][:], COPY)
        w_q = at(201 * KIB, [P, N], U32, "w_q")
        w_s = at(209 * KIB, [P, N], U8, "w_s")
        for h in range(2):
            round_pair(1, h)

        def quantise_w(h):
            nc.vector.quantize_mx(w_q[:, parts[h]].bitcast(E4M3), w_s[:, parts[h]], w_bf[h][:])

        def deal(dst, raw, k, copy, rows=slice(0, P)):
            copy(dst.rearrange("p (t m j) -> p m j t", t=2, j=LANES)[:, rows, :, :], raw[:].rearrange("p j (m t) -> p m j t", t=LANES)[:, rows, :, 2 * k:2 * k + 2])

        x_bf = [at((189 + 2 * k) * KIB, [P, R * 2], BF16, "x_bf%d" % k) for k in range(2)]
        x_q = at(203 * KIB, [P, R], U32, "x_q")
        x_s = at(209 * KIB + 512, [P, R], U8, "x_s")

        def quantise_x(k):
            cols = slice(2 * k * P, (2 * k + 2) * P)
            nc.vector.quantize_mx(x_q[:, cols].bitcast(E4M3), x_s[:, cols], x_bf[k][:])

        for h in range(2):
            quantise_w(h)
        deal(x_bf[0][:], x_raw, 0, nc.scalar.copy)
        deal(x_bf[1][:], x_raw, 1, nc.vector.tensor_copy, slice(P // 2, P))
        deal(x_bf[1][:], x_raw, 1, nc.scalar.copy, slice(0, P // 2))
        quantise_x(0)

        sig = [at((153 + 4 * h) * KIB, [P, LANES, HALF], F32, "sig%d" % h) for h in range(2)]
        yw = at(161 * KIB, [P, LANES, N], F32, "yw")
        wt_neg = at(191 * KIB, [P, LANES], F32, "wt_neg")
        nc.vector.tensor_scalar(yw[:, 0, :], y_sb[0][:, 0, :], wt_sb[:, 0:1], -1.0, MULT, MULT)
        quantise_x(1)
        nc.gpsimd.tensor_scalar(wt_neg[:], wt_sb[:], -1.0, 0.0, MULT, ADD)
        for t in range(1, LANES):
            nc.gpsimd.tensor_scalar(yw[:, t, :], y_sb[t // 2][:, t % 2, :], wt_neg[:, t:t + 1], 0.0, MULT, ADD)
        scores = {}

        def score(h, k):
            scores[h, k] = bank("sum", 4)
            for e in range(2):
                cols = slice((2 * k + e) * P, (2 * k + e + 1) * P)
                nc.tensor.matmul_mx(scores[h, k][:, e * HALF:(e + 1) * HALF], x_q[:, cols].bitcast(E4M3), x_s[:, cols], w_q[:, parts[h]].bitcast(E4M3), w_s[:, parts[h]], start=True, stop=True)

        def weigh(h, k):
            z = at(((169 * KIB, 171 * KIB), (173 * KIB, 220 * KIB - 64))[h][k], [P, 2, HALF], F32, "z%d%d" % (h, k))
            nc.vector.tensor_tensor(z[:], scores[h, k][:].rearrange("p (e n) -> p e n", e=2), y_sb[k][:, :, parts[h]], MULT)
            nc.scalar.activation(sig[h][:, 2 * k:2 * k + 2, :], z[:], SIGMOID, scale=-1.0)

        for h in range(2):
            for k in range(2):
                score(h, k)
        park(first)
        park(last)
        for h in range(2):
            for k in range(2):
                weigh(h, k)

        xm_bf = {1: at(218 * KIB, [P, D * 2], BF16, "xm_bf1")[:]}
        xm_q = {}
        xm_s = at(210 * KIB, [P, D], U8, "xm_s")
        g_bf = [at((197 + 2 * h) * KIB, [P, HALF * LANES], BF16, "g_bf%d" % h) for h in range(2)]
        g_q = at(207 * KIB, [P, N], U32, "g_q")
        g_s = at(210 * KIB + 512, [P, N], U8, "g_s")
        deal(xm_bf[1], xm_raw, 1, nc.scalar.copy)
        m_first = at(185 * KIB, [P, N], F32, "m_g_first")
        for h in range(2):
            nc.scalar.activation(m_first[:, parts[h]], m_src[first][:].indirect(halves[h]), COPY)
        nc.scalar.activation(m_new[first][:, :SPLIT], m_src[first][:, :SPLIT], COPY)
        for h in range(2):
            nc.vector.tensor_tensor(
                g_bf[h][:].rearrange("p (c i t) -> p c t i", i=4, t=LANES),
                sig[h][:].rearrange("p t (c i) -> p c t i", i=4),
                yw[:, :, parts[h]].rearrange("p t (c i) -> p c t i", i=4),
                MULT,
            )

        def quantise_xm(k):
            cols = slice(2 * k * P, (2 * k + 2) * P)
            xm_q[k] = at(205 * KIB if k == 1 else (64 + 8 * second) * KIB, [P, D // 2], U32, "xm_q%d" % k)
            nc.vector.quantize_mx(xm_q[k][:].bitcast(E4M3), xm_s[:, cols], xm_bf[k])

        nc.vector.quantize_mx(g_q[:, parts[0]].bitcast(E5M2), g_s[:, parts[0]], g_bf[0][:])
        quantise_xm(1)
        nc.vector.quantize_mx(g_q[:, parts[1]].bitcast(E5M2), g_s[:, parts[1]], g_bf[1][:])
        xm_bf[0] = at(199 * KIB, [P, D * 2], BF16, "xm_bf0")[:]
        nc.gpsimd.tensor_scalar(
            xm_bf[0].rearrange("p (t m j) -> p t m j", t=2, j=LANES),
            xm_raw[:].rearrange("p j (m t) -> p t m j", t=LANES)[:, 0:2, :, :],
            1.0, -0.0, MULT, ADD,
        )

        nm, nw = {}, {}
        m_g_at = {first: 185 * KIB, second: 187 * KIB, third: 193 * KIB, last: 120 * KIB}
        nw_at = {first: 137 * KIB, second: 139 * KIB, third: 141 * KIB, last: 189 * KIB}
        pairs = at(0, [P, 4 * T], BF16, "pairs")

        def place(t):
            return pairs[:, t // 2 * 2 * T:(t // 2 + 1) * 2 * T].rearrange("p (c e) -> p c e", e=2)[:, :, t % 2]

        def round_plane(t, unit, cols=slice(0, T)):
            nc.gpsimd.tensor_scalar(place(t)[:, cols], w_new[t][:, cols], unit, -0.0, MULT, ADD)

        def columns(t):
            cols = slice(t * P, (t + 1) * P)
            dw = [bank("sum", 4) for cut in (parts if t == first else parts[:1])]
            for k, cut in enumerate(parts if t == first else [slice(0, N)]):
                nc.tensor.matmul_mx(dw[k][:, cut], xm_q[t // 2][:, t % 2 * P:(t % 2 + 1) * P].bitcast(E4M3), xm_s[:, cols], g_q[:, cut].bitcast(E5M2), g_s[:, cut], start=True, stop=True)
            m_g = m_first if t == first else at(m_g_at[t], [P, N], F32, "m_g%d" % t)
            nm[t] = at((129 + 2 * t) * KIB, [P, N], F32, "nm%d" % t)
            nw[t] = at(nw_at[t], [P, N], F32, "nw%d" % t)
            old = parked[t][:] if t in parked else w_g[t // 2][:, t % 2, :]
            if t == second:
                nc.vector.tensor_copy(m_g[:], m_src[t][:].indirect(offsets[:]))
                nc.vector.tensor_copy(m_new[t][:, :SPLIT], m_src[t][:, :SPLIT])
                nc.vector.scalar_tensor_tensor(nm[t][:], m_g[:], BETA, dw[0][:], MULT, ADD)
                quantise_xm(0)
            else:
                for h in range(0 if t == first else 2):
                    nc.vector.tensor_copy(m_g[:, parts[h]], m_src[t][:].indirect(halves[h]))
                for h in range(2):
                    nc.vector.scalar_tensor_tensor(nm[t][:, parts[h]], m_g[:, parts[h]], BETA, dw[h % len(dw)][:, parts[h]], MULT, ADD)
            if t in (second, third):
                step = at(143 * KIB, [P, N], F32, "step%d" % t)
                nc.gpsimd.tensor_scalar(step[:], nm[t][:], -LR, -0.0, MULT, ADD)
                nc.gpsimd.tensor_tensor(nw[t][:], step[:], old, ADD)
            else:
                for h in range(2):
                    nc.vector.scalar_tensor_tensor(nw[t][:, parts[h]], nm[t][:, parts[h]], -LR, old[:, parts[h]], MULT, ADD)

        def scalar_scatter(window, values, unit):
            nc.scalar.activation(window[:].indirect(offsets[:]), values[:], COPY, scale=unit)

        def vector_scatter(t):
            nc.vector.tensor_copy(m_new[t][:].indirect(offsets[:]), nm[t][:])
            nc.sync.dma_start(o1_hbm[:, t, :], m_new[t][:])

        def store_w(t):
            nc.sync.dma_start(o0_hbm[:, t, :], w_new[t][:])

        def store_m(t):
            nc.sync.dma_start(o1_hbm[:, t, :], m_new[t][:])

        columns(first)
        scalar_scatter(w_new[first], nw[first], one[:])
        store_w(first)
        columns(second)
        scalar_scatter(m_new[first], nm[first], one[:])
        one_first = at(181 * KIB, [P, 1], F32, "one_first")
        nc.gpsimd.memset(one_first[:], 1.0)
        round_plane(first, one_first[:], slice(0, SPLIT))
        scalar_scatter(w_new[second], nw[second], one[:])
        vector_scatter(second)
        store_m(first)
        store_w(second)
        columns(third)
        nc.vector.tensor_copy(m_new[third][:].indirect(halves[0]), nm[third][:, parts[0]])
        nc.scalar.activation(m_new[third][:].indirect(halves[1]), nm[third][:, parts[1]], COPY)
        store_m(third)
        scalar_scatter(w_new[third], nw[third], one[:])
        store_w(third)
        one_second = at(177 * KIB, [P, 1], F32, "one_second")
        nc.gpsimd.memset(one_second[:], 1.0)
        round_plane(first, one_second[:], slice(SPLIT, T))
        columns(last)
        m_new[last] = at(120 * KIB, [P, T], F32, "m_new_last")
        nc.vector.tensor_copy(m_new[last][:], m_src[last][:])
        nc.vector.tensor_copy(w_new[last][:].indirect(offsets[:]), nw[last][:])
        store_w(last)
        one_late = at((64 + 8 * last) * KIB, [P, 1], F32, "one_late")
        nc.gpsimd.memset(one_late[:], 1.0)
        round_plane(second, one_late[:], slice(0, SPLIT))
        scalar_scatter(m_new[last], nm[last], one[:])
        store_m(last)
        for cols in (slice(0, T // 2), slice(T // 2, T)):
            nc.vector.tensor_scalar(place(third)[:, cols], w_new[third][:, cols], one_late[:], -0.0, MULT, ADD)
            nc.vector.tensor_copy(place(last)[:, cols], w_new[last][:, cols])
        nc.vector.tensor_scalar(place(second)[:, SPLIT:], w_new[second][:, SPLIT:], one_late[:], -0.0, MULT, ADD)

        words = pairs[:].bitcast(U32).rearrange("p (u c) -> p u c", u=2)
        o_s = at(212 * KIB, [P, BAND], U8, "o_s")
        o_q = at(145 * KIB, [P, T], U32, "o_q")
        words_hbm = out_2[0].rearrange("p c l -> p (c l)").bitcast(I32)
        pieces = [(512, nc.scalar.copy), (512, nc.scalar.copy), (256, nc.vector.tensor_copy), (256, nc.scalar.copy), (256, nc.scalar.copy), (256, nc.scalar.copy)]
        woven = []
        start = 0
        for k, (width, copy) in enumerate(pieces):
            cols = slice(start, start + width)
            o_bf = at(16 * KIB + 8 * start, [P, width * LANES], BF16, "o_bf%d" % k)
            copy(o_bf[:].bitcast(U32).rearrange("p (c u) -> p c u", u=2), words[:, :, cols].rearrange("p u c -> p c u"))
            woven.append((cols, o_bf))
            start = cols.stop
        stored = 0
        for k, (cols, o_bf) in enumerate(woven):
            band, inside = divmod(cols.start, BAND)
            nc.vector.quantize_mx(o_q[:, cols].bitcast(E4M3), o_s[4 * band:, inside:inside + cols.stop - cols.start], o_bf[:])
            if k in (1, 4, 5):
                nc.sync.dma_start(words_hbm[:, stored:cols.stop], o_q[:, stored:cols.stop].bitcast(I32))
                stored = cols.stop
        scales_hbm = out_3[0].bitcast(I32)
        for q in range(4):
            nc.sync.dma_start(scales_hbm[4 * q:4 * q + 4, :].rearrange("r (b c) -> b r c", b=4), o_s[32 * q:32 * q + 16, :].bitcast(I32))
